import numpy as np, ml_dtypes
CORES = [83,85,87,115,117,119]
N = 6
BF = ml_dtypes.bfloat16
def gentries(a):
    return np.ascontiguousarray(a.reshape(8, 16, -1).transpose(0, 2, 1)).reshape(8, -1)
def gtable(e):
    e = np.asarray(e); return np.ascontiguousarray(e.reshape(8, -1, 16).transpose(0, 2, 1)).reshape(128, -1).astype(np.int32)
W, L, S, ST = 4096, 128, 32, 4
def parts(rng):
    x = rng.integers(0, 64, (N, 8, 16, W)); v = rng.integers(0, W, (N, 8, L, S)); c = rng.integers(0, W, (N, 8, L, S))
    n = np.where(rng.random((N, 8, L)) < 0.4, rng.integers(0, 4, (N, 8, L)), rng.integers(4, S + 1, (N, 8, L)))
    return x, v, c, n, rng.integers(220, 460, (N, 8)), rng.integers(0, 256, (N, 8, 16))
def pack(x, v, c, n, th, w):
    return {"xc": np.ascontiguousarray(x.reshape(N, 128, W)).astype(np.float32).astype(BF), "vl": np.stack([gtable(a.reshape(8, -1)) for a in v]), "cl": np.stack([gtable(a.reshape(8, -1)) for a in c]),
            "ln": np.ascontiguousarray(n).astype(np.int32), "th": np.ascontiguousarray(th.reshape(N, 8, 1)).astype(np.int32), "wt": np.ascontiguousarray(w.reshape(N, 128, 1)).astype(np.int32)}
def setup_inputs(rng):
    return pack(*parts(rng))
def setup_inputs_ties(rng):
    x, v, c, n, th, w = parts(rng)
    x = np.repeat(8 * rng.integers(0, 8, (N, 8, 1, W)), 16, axis=2); up = rng.integers(0, 3, (N, 8, W)) * (rng.random((N, 8, W)) < 0.4)
    x = x + up[:, :, None, :] * (np.arange(16)[:, None] == rng.integers(0, 16, (N, 8, 1, W)))
    o = np.argsort(rng.random((N, 8)), axis=1); j = o >> 1; less = np.where(rng.random((N, 8)) < 0.6, rng.integers(0, 2, (N, 8)), rng.integers(0, 32, (N, 8)))
    th = np.maximum(128 * j - less, 0); s = np.arange(S)
    for r in range(N):
        z = 128 * int(rng.integers(4, 7))
        for g, e in ((int(np.argmin(o[r])), 0), (int(np.argmax(o[r])), 1)):
            th[r, g] = z + e
            x[r, g, :, 0] = 0; x[r, g, :, 1] = 56; x[r, g, :, 2] = z >> 4; x[r, g, int(rng.integers(0, 16)), 2] += 1
            v[r, g, 1::2] = np.where(s < 2, 0, 2); c[r, g, 1::2] = np.where(s < 1, 1, 2); n[r, g, 1::2] = rng.integers(4, S + 1, L // 2)
    q = int(rng.integers(0, N)); a = (q - 1) % N; b = (q - 2) % N
    n[a] = np.where(n[a] >= 4, rng.integers(4, 6, (8, L)), n[a])
    n[q] = rng.integers(0, 4, (8, L)); p = rng.permutation(8 * L)[:31]; one = rng.integers(0, W, (31, 1))
    n[q, p // L, p % L] = 4; v[q, p // L, p % L] = one; c[q, p // L, p % L] = one; th[q] = 128 * rng.integers(1, 4, 8) - 16
    x[b, :, :, 16:40:3] = 0; x[b, :, :, 17:40:3] = 56; x[b, :, :, 18:40:3] = 63; x[b, :, :, 64:128] = 8 * rng.integers(0, 2, (8, 1, 64))
    f0 = 16 + 3 * (np.arange(L // 4)[:, None] & 7); far = rng.integers(64, 128, (8, L // 4, S)); e = rng.integers(128, W, (8, L // 4, S))
    v[b, :, ::4] = np.where(s == 0, e, np.where((s == 1) | (s >= S - 3), f0 + 2, np.where(s == 2, f0 + 1, far)))
    c[b, :, ::4] = np.where(s == 0, f0 + 2, np.where((s == 1) | (s == S - 3), f0, rng.integers(128, W, far.shape)))
    n[b, :, ::4] = S
    return pack(x, v, c, n, th, w)
def setup_inputs_alike(rng):
    x, v, c, n, th, w = parts(rng)
    few = np.array([0, W - 1, W // 2, 3, W - 2, 17])
    v[:, ::2] = few[rng.integers(0, 6, (N, 4, L, S))]; v[:, 1::2, :, 0] = few[rng.integers(0, 6, (N, 4, L))]
    w[:, ::2] = 0; th[:, ::2] = rng.integers(0, 260, (N, 4)); th[:, 1::2] = rng.integers(150, 500, (N, 4))
    o = rng.permutation(4); shutting = 2 * int(o[0]); taking = 2 * int(o[1]); growing = 1 + 2 * int(rng.integers(0, 4))
    n[:, growing] = rng.integers(4, S + 1, (N, L)); v[:, growing, :, 0] = few[int(rng.integers(0, 6))]; th[:, growing] = 0
    n[:, shutting] = rng.integers(ST + 3, S + 1, (N, L)); th[:, shutting] = 1008
    rest = np.where(rng.random((N, L)) < 0.8, 0, rng.integers(1, 4, (N, L)))
    n[:, taking] = np.where(np.arange(N)[:, None] % 2 == 0, rng.integers(ST + 3, S + 1, (N, L)), rest); th[:, taking] = 1008
    return pack(x, v, c, n, th, w)
def setup_inputs_corners(rng):
    x, v, c, n, th, w = parts(rng)
    lo = (W - 1) * rng.integers(0, 2, (N, 8, 1)); hi = W - 1 - lo
    x[..., 0] = np.where(lo == 0, 0, 63); x[..., W - 1] = np.where(lo == 0, 63, 0)
    n = rng.choice(np.array([0, 1, 2, 3, 4, 5, S - 1, S]), (N, 8, L)); kind = rng.integers(0, 5, (N, 8, L))
    for g, i in ((0, 0), (7, L - 1)):
        n[0, g, i] = S; kind[0, g, i] = 0; n[1, g, i] = 0
    n[N - 1, 7, L - 2] = S; kind[N - 1, 7, L - 2] = 1
    s = np.arange(S); q = np.maximum(n, 4)[..., None]; kd = kind[..., None]; A = lo[..., None]; H = hi[..., None]
    v0 = np.where((s < 2) | (s == q - 1), H, A); v1 = np.where((s == q - 3) | (s == q - 2), H, A); v2 = np.where(s >= q - 3, H, A)
    one = rng.integers(0, W, (N, 8, L, 1))
    v = np.where(kd == 0, v0, np.where(kd == 1, v1, np.where(kd == 2, v2, np.where(kd == 3, one, v))))
    c = np.where(kd < 3, A, np.where(kd == 3, one, c))
    v = np.where(s < n[..., None], v, (W - 1) * rng.integers(0, 2, v.shape)); c = np.where(s < n[..., None], c, (W - 1) * rng.integers(0, 2, c.shape))
    return pack(x, v, c, n, np.array([0, 5, 500, 900])[np.argsort(rng.random((N, 8)), axis=1) >> 1], w)
def setup_inputs_ends(rng):
    x, v, c, n, th, w = parts(rng)
    e = 63 * rng.integers(0, 2, (N, 8, 1)); e[N - 1, 7] = 0
    x = 63 * rng.integers(0, 2, (N, 8, 16, W)); x[..., 0] = e; x[..., W - 1] = 63 - e
    for j in range(1, 17):
        for col in (j, W - 1 - j):
            x[..., col] = 63 - e; x[:, :, j - 1, col] = np.abs(62 - e[..., 0])
    v = np.where(rng.random(v.shape) < 0.75, (W - 1) * rng.integers(0, 2, v.shape), v); c = np.where(rng.random(c.shape) < 0.75, (W - 1) * rng.integers(0, 2, c.shape), c)
    kind = rng.integers(0, 3, (N, 8, L)); kind[..., 0] = 1; kind[..., L - 1] = 1; kind[..., 1] = 2; kind[..., L - 2] = 2
    k1 = kind == 1; k2 = kind == 2; v[k1 | k2] = W - 1; c[k1] = W - 1
    c = np.where(k2[..., None], (W - 1) * rng.integers(0, 2, c.shape), c)
    near = rng.integers(1, 17, (N, 8, L)); near = np.where(rng.random((N, 8, L)) < 0.5, near, W - 1 - near)
    v[..., 0] = np.where(k1, near, v[..., 0]); c[..., 0] = np.where(k1, 0, c[..., 0]); c[..., S - 3] = np.where(k1 | k2, 0, c[..., S - 3])
    v[..., S - 1] = np.where(k1, (W - 1) * rng.integers(0, 2, (N, 8, L)), v[..., S - 1]); v[N - 1, 7, L - 1, S - 1] = 0
    n = np.where(rng.random((N, 8, L)) < 0.7, S, 0); n[..., 0] = S; n[..., 1] = S; n[..., 2] = 0; n[..., L - 2] = S; n[..., L - 1] = S; n[0, :, L - 1] = 0
    th = 1008 * (np.argsort(rng.random((N, 8)), axis=1) & 1)
    if th[N - 1, 7] > 0: th[N - 1] = 1008 - th[N - 1]
    w = 255 * rng.integers(0, 2, (N, 8, 16)); w[:, 7] = 255; w[:, 0] = 0
    return pack(x, v, c, n, th, w)
def setup_inputs_spread(rng):
    x, v, c, n, th, w = parts(rng)
    x = np.minimum((np.exp2(6.1 * rng.random((N, 8, 1, W))) * rng.random((N, 8, 16, W))).astype(np.int64), 63)
    po = rng.choice(np.array([1.0, 2.0, 4.0]), (N, 8, 1, 1)); v = np.minimum((W * rng.random(v.shape) ** po).astype(np.int64), W - 1); c = np.minimum((W * rng.random(c.shape) ** po[:, ::-1]).astype(np.int64), W - 1)
    n = np.minimum(((S + 1) * rng.random((N, 8, L)) ** rng.choice(np.array([0.5, 1.0, 2.0]), (N, 8, 1))).astype(np.int64), S)
    th = np.minimum(np.exp2(10 * rng.random((N, 8))).astype(np.int64) - 1, 1008); w = np.minimum(np.exp2(8.05 * rng.random((N, 8, 16))).astype(np.int64) - 1, 255)
    return pack(x, v, c, n, th, w)
def check_inputs(d):
    bad = []
    for k, lo, hi in (("xc", 0, 63), ("vl", 0, W - 1), ("cl", 0, W - 1), ("ln", 0, S), ("th", 0, 1008), ("wt", 0, 255)):
        a = np.asarray(d[k]).astype(np.float64)
        if not (np.min(a) >= lo and np.max(a) <= hi): bad.append("range of " + k)
    a = np.asarray(d["xc"]).astype(np.float64)
    if not np.all(np.floor(a) == a): bad.append("xc is not whole")
    return bad
def reference(xc, vl, cl, ln, th, wt):
    X = np.ascontiguousarray(xc.astype(np.float32).astype(np.int32).reshape(N, 8, 16, W).transpose(0, 1, 3, 2))
    V = np.stack([gentries(q) for q in vl]).astype(np.int32).reshape(N, 8, L, S); C = np.stack([gentries(q) for q in cl]).astype(np.int32).reshape(N, 8, L, S)
    n = ln.astype(np.int64).reshape(N, 8, L); lim = th.astype(np.int64).reshape(N, 8, 1, 1); w = wt.astype(np.int64).reshape(N, 8, 1, 16)
    a = np.arange(N)[:, None, None, None]; b = np.arange(8)[None, :, None, None]; s = np.arange(S); shut = np.zeros(N, np.int64)
    for t in range(ST):
        XV = X[a, b, V]; XC = X[a, b, C]; live = n >= 4
        bend = np.add.reduce(np.abs(XV[:, :, :, :-1] + XV[:, :, :, 1:] - 2 * XC[:, :, :, :-1]), axis=-1, dtype=np.int32)
        k = np.argmax(np.where(s[:-1] <= n[..., None] - 3, bend, -1), axis=3)[..., None]
        Vk = np.take_along_axis(V, k, 3); Vn = np.take_along_axis(V, k + 1, 3); Ck = np.take_along_axis(C, k, 3)
        y = np.clip(X[a, b, Vk] + X[a, b, Vn] - X[a, b, Ck], 0, 63)
        dist = np.add.reduce(np.abs(XV - y), axis=-1, dtype=np.int32)
        fit = (s >= k + 2) & (s <= n[..., None] - 1) & (dist <= lim + shut[:, None, None, None]) & live[..., None]
        close = np.any(fit, axis=3); m = np.argmax(fit, axis=3)[..., None]; grow = live & ~close
        size = np.where(close[..., None], m - k - 1, 0)
        ix = np.minimum(k + 1 + s, S - 1); keep = s < size
        PV = np.where(keep, np.take_along_axis(V, ix, 3), 0); PC = np.where(keep, np.take_along_axis(C, ix, 3), 0)
        y = y[:, :, :, 0]; u = np.add.reduce(w * y, axis=-1) & (W - 1)
        h = (((u * u) >> 5) + 37 * Vk[..., 0].astype(np.int64)) & (W - 1)
        src = np.minimum(np.where(s <= k, s, s + size - grow[..., None].astype(np.int64)), S - 1)
        V2 = np.take_along_axis(V, src, 3); C2 = np.take_along_axis(C, src, 3); new = grow[..., None] & (s == k + 1)
        V2 = np.where(new, h[..., None], V2); C2 = np.where(new, Vk, np.where(live[..., None] & (s == k), Vn, C2))
        n2 = np.minimum(n + grow.astype(np.int64), S) - size[..., 0]
        for i in range(L - 1, -1, -1):
            p, q = np.nonzero(grow[:, :, i]); X[p, q, h[p, q, i]] = y[p, q, i]
        d = 1 + t % (N - 1)
        came = np.roll(size, d, axis=0)[..., 0]; yin = np.roll(y, d, axis=0); lin = np.roll(live, d, axis=0)
        take = ~live & (came > n)
        V = np.where(take[..., None], np.roll(PV, d, axis=0), V2); C = np.where(take[..., None], np.roll(PC, d, axis=0), C2); n = np.where(take, came, n2)
        V = np.where(s < n[..., None], V, 0).astype(np.int32); C = np.where(s < n[..., None], C, 0).astype(np.int32)
        has = lin & (n >= 1); old = X.copy()
        for i in range(L - 1, -1, -1):
            p, q = np.nonzero(has[:, :, i]); z = V[p, q, i, 0]; X[p, q, z] = (old[p, q, z] + yin[p, q, i]) >> 1
        shut = np.add.reduce(close.astype(np.int64).reshape(N, -1), axis=1) & 31
    return {"yx": np.ascontiguousarray(X.transpose(0, 1, 3, 2)).reshape(N, 128, W).astype(np.float32).astype(BF), "yv": np.stack([gtable(q.reshape(8, -1)) for q in V]).astype(np.float32),
            "yc": np.stack([gtable(q.reshape(8, -1)) for q in C]).astype(np.float32), "yn": n.astype(np.float32)}

@@ -1,0 +1,781 @@
+import numpy as np
+import comms_topo
+from concourse.mybir import dt, AluOpType, AxisListType, ActivationFunctionType
+
+A = AluOpType
+AF = ActivationFunctionType
+N = 6
+ST = 4
+BIG = 16777216
+NX = 4224
+NV = 5
+SLACK = 0.03
+HA = 21
+GCS = (8, 17, 26)
+
+SCRATCH = {}
+
+
+def _add(where, dtype, names, cols, rows=128):
+    for nm in names.split():
+        SCRATCH[nm] = (where, [rows, cols], dtype)
+
+
+_add("sbuf", "bfloat16", "X", NX)
+_add("sbuf", "bfloat16", "XV H D AB", 4480)
+_add("sbuf", "int32", "W0 W1 W2 W3 W4 LW0 LW1 LW2 LW3 VI CI DLT BIT", 288)
+_add("sbuf", "bfloat16", "R0 R1 R2 R3 R4 QT ZERO ONES INV MK PP XB A1 A2 RX TDR", 288)
+_add("sbuf", "float32", "POS Z Z0 RQ LX OA SP GG PZ WA E T1 TM U", 288)
+_add("sbuf", "uint16", "VL CL", 288)
+_add("sbuf", "uint16", "JL OL OB", 8)
+_add("sbuf", "bfloat16", "YR0 YR1 YR2 YR3 LY0 LY1 LY2 LY3", 416)
+_add("sbuf", "float32", "M0 M1 M2 M3 LM0 LM1 LM2 LM3", 24)
+_add("sbuf", "float32", "SM", 720)
+_add("sbuf", "int32", "SI", 240)
+_add("sbuf", "float32", "ROWI", 143)
+_add("sbuf", "bfloat16", "WB1 WBK WB4 WBM WBW", 143)
+_add("sbuf", "bfloat16", "ID IDM IDH IDN DK TK BI YX", 128)
+_add("sbuf", "float32", "BLK GB EX EXC", 128)
+_add("sbuf", "int32", "CIO BO", 128)
+_add("sbuf", "float32", "BS", 128)
+_add("sbuf", "float32", "DG", 16)
+_add("sbuf", "float32", "AA", 1024)
+_add("sbuf", "int32", "VR CR", 256)
+_add("sbuf", "float32", "RT RU TA TB TC TE OUT", 256)
+_add("sbuf", "float32", "OV OC", 256)
+_add("sbuf", "int32", "OI", 256)
+_add("sbuf", "int32", "NR", 8)
+_add("sbuf", "int32", "THR8", 1, 8)
+_add("sbuf", "int32", "WT", 1)
+_add("psum", "float32", "pA pB pK pD pY pS pI pJ", 512)
+
+SEMAPHORES = ["qv", "qa", "qt", "qp", "ls"] + ["d%d" % i for i in range(12)] + [
+    m + str(t) for m in ("aw", "ay", "am") for t in range(ST)]
+
+
+def rank_program(g, core, T, topo):
+    rank = T.rank_of(core)
+    if rank is None:
+        return
+    Q = {"v": g.vector, "a": g.scalar, "t": g.tensor, "p": g, "s": g.sync}
+    SEM = {"v": "qv", "a": "qa", "t": "qt", "p": "qp", "s": None}
+    cnt = {"qv": 0, "qa": 0, "qt": 0, "qp": 0, "ls": 0}
+    clk = {e: {} for e in Q}
+    acc = {n: [] for n in SCRATCH}
+    nd = [0]
+
+    def v(name, lo=0, hi=None, step=1, p0=0, p1=None):
+        sh = SCRATCH[name][1]
+        return (name, lo, sh[1] if hi is None else hi, step, p0, sh[0] if p1 is None else p1)
+
+    def ap(w):
+        if w[0] == "ind":
+            return ap(w[1]).indirect(ap(w[2]))
+        n, lo, hi, st, p0, p1 = w
+        if st == 1:
+            return T[n][p0:p1, lo:hi]
+        return T[n][p0:p1, lo:hi:st]
+
+    def ind(win, off):
+        return ("ind", win, off)
+
+    def meets(x, y):
+        if x[1] >= y[2] or y[1] >= x[2] or x[4] >= y[5] or y[4] >= x[5]:
+            return False
+        if x[3] == y[3] and x[3] > 1 and (x[1] - y[1]) % x[3]:
+            return False
+        return True
+
+    def covers(x, y):
+        return x[3] == 1 and x[1] <= y[1] and x[2] >= y[2] and x[4] <= y[4] and x[5] >= y[5]
+
+    ops, dacc, phase = [], {n: [] for n in SCRATCH}, {n: [] for n in SCRATCH}
+    LAT = 0.06
+
+    def emit(eng, call, writes, reads, tok=None, inc=1, note=True, cost=0.1, tail=0.0):
+        ws = [w[1] if w[0] == "ind" else w for w in writes]
+        rs = [w[2] for w in writes if w[0] == "ind"]
+        for w in reads:
+            if w[0] == "ind":
+                rs.append(w[1]); rs.append(w[2])
+            elif isinstance(w, tuple):
+                rs.append(w)
+        me, deps = len(ops), {}
+        for lst, wr in ((rs, False), (ws, True)):
+            for w in lst:
+                psum = w[0][0] == "p"
+                for (i, w2, wr2) in dacc[w[0]]:
+                    e2 = ops[i][0]
+                    if (wr or wr2) and (meets(w, w2) or (psum and eng == "t" and e2 == "t")):
+                        deps[i] = max(deps.get(i, 0.0), 0.0 if psum and e2 == eng == "t" else LAT)
+                if psum:
+                    ph = phase[w[0]]
+                    if ph and ph[-1][0] == eng:
+                        prev = ph[-2][1] if len(ph) > 1 else []
+                        ph[-1][1].append(me)
+                    else:
+                        prev = ph[-1][1] if ph else []
+                        ph.append([eng, [me]])
+                    for i in prev:
+                        deps[i] = LAT
+        deps.pop(me, None)
+        for w in rs:
+            dacc[w[0]].append((me, w, False))
+        for w in ws:
+            dacc[w[0]] = [x for x in dacc[w[0]] if not covers(w, x[1])] + [(me, w, True)]
+        ops.append((eng, call, writes, reads, tok, inc, note, cost, tail, deps))
+
+    def flush():
+        n = len(ops)
+        succ = [[] for _ in range(n)]
+        for i, o in enumerate(ops):
+            for d in o[9]:
+                succ[d].append((i, o[9][d]))
+        pri = [0.0] * n
+        for i in range(n - 1, -1, -1):
+            o = ops[i]
+            pri[i] = o[7] + max([o[8] + l + pri[s] for s, l in succ[i]] + [0.0])
+        left = [len(o[9]) for o in ops]
+        ready = {e: [] for e in list(Q) + ["x"]}
+        avail = [0.0] * n
+        for i in range(n):
+            if not left[i]:
+                ready[ops[i][0]].append(i)
+        free = {e: 0.0 for e in ready}
+        order, done = [], 0
+        while done < n:
+            best = None
+            for e in ready:
+                if ready[e]:
+                    t0 = max(free[e], min(avail[i] for i in ready[e]))
+                    if best is None or t0 < best[0]:
+                        best = (t0, e)
+            t0, e = best
+            i = max((i for i in ready[e] if avail[i] <= t0 + SLACK), key=lambda i: (pri[i], -i))
+            ready[e].remove(i)
+            st = max(t0, avail[i])
+            fin = st + ops[i][7]
+            if e != "x":
+                free[e] = fin
+            order.append((st, i))
+            done += 1
+            for s, l in succ[i]:
+                avail[s] = max(avail[s], fin + ops[i][8] + l)
+                left[s] -= 1
+                if not left[s]:
+                    ready[ops[s][0]].append(s)
+        for st, i in order:
+            if ops[i][0] != "x":
+                issue(*ops[i][:7])
+
+    def issue(eng, call, writes, reads, tok=None, inc=1, note=True):
+        ws, rs = [], []
+        for w in writes:
+            if w[0] == "ind":
+                ws.append(w[1]); rs.append(w[2])
+            else:
+                ws.append(w)
+        for w in reads:
+            if w[0] == "ind":
+                rs.append(w[1]); rs.append(w[2])
+            elif isinstance(w, tuple):
+                rs.append(w)
+        mysem = tok[0] if tok else SEM[eng]
+        need = {}
+        for lst, wr in ((rs, False), (ws, True)):
+            for w in lst:
+                psum = w[0][0] == "p"
+                for (tk, w2, wr2, ck2) in acc[w[0]]:
+                    same = tk[0] == mysem
+                    if psum and not same:
+                        hit = True
+                    elif same:
+                        hit = (wr or wr2) and meets(w, w2) and not (psum and eng == "t")
+                    else:
+                        hit = (wr or wr2) and meets(w, w2)
+                    if hit and clk[eng].get(tk[0], 0) < tk[1] and need.get(tk[0], (0,))[0] < tk[1]:
+                        need[tk[0]] = (tk[1], ck2)
+        ck = clk[eng]
+        for s in list(need):
+            val, c2 = need[s]
+            if any(s2 != s and need[s2][1].get(s, 0) >= val for s2 in need):
+                continue
+            Q[eng].wait_ge(T.sem[s], val)
+            for k2 in c2:
+                ck[k2] = max(ck.get(k2, 0), c2[k2])
+            ck[s] = max(ck.get(s, 0), val)
+        ins = call()
+        if not note:
+            return None
+        if tok is None:
+            cnt[mysem] += 1
+            tok = (mysem, cnt[mysem])
+        ins.then_inc(T.sem[tok[0]], inc)
+        snap = dict(ck)
+        snap[tok[0]] = tok[1]
+        record(tok, ws, rs, snap)
+        return tok
+
+    def record(tok, ws, rs, snap):
+        for w in rs:
+            old = acc[w[0]]
+            if w[0][0] == "p":
+                old = [x for x in old if x[0][0] == tok[0]]
+            acc[w[0]] = [x for x in old if not (x[0][0] == tok[0] and not x[2] and covers(w, x[1]))] + [(tok, w, False, snap)]
+        for w in ws:
+            old = acc[w[0]]
+            if w[0][0] == "p":
+                old = [x for x in old if x[0][0] == tok[0]]
+            acc[w[0]] = [x for x in old if not covers(w, x[1])] + [(tok, w, True, snap)]
+
+    def sc(x):
+        return ap(x) if isinstance(x, tuple) else x
+
+    def width(w):
+        if w[0] == "ind":
+            return 16 * (w[2][2] - w[2][1])
+        return (w[2] - w[1] + w[3] - 1) // w[3]
+
+    def us(o, ins, rate, fix=0.0, gather=1.56):
+        if o[0] == "ind":
+            return 0.05 + 3.5 * width(o) * 0.00083
+        if any(x[0] == "ind" for x in ins):
+            return 0.05 + gather * width(o) * 0.00083
+        return max(64, max(width(x) for x in ins) * rate) * 0.00083 + fix
+
+    def small(*vs):
+        return 0.5 if all(x[0] != "ind" and x[0][0] != "p" and SCRATCH[x[0]][2] in ("bfloat16", "uint16") for x in vs) else 1
+
+    def tc(o, i):
+        emit("v", lambda: g.vector.tensor_copy(ap(o), ap(i)), [o], [i], cost=us(o, [i], small(o, i)))
+
+    def tt(o, x, y, op):
+        emit("v", lambda: g.vector.tensor_tensor(ap(o), ap(x), ap(y), op), [o], [x, y],
+             cost=us(o, [x, y], 1 if "p" in (x[0][0], y[0][0]) else 2))
+
+    def ts(o, x, s1, op0, s2=None, op1=None):
+        r = [x] + [s for s in (s1, s2) if isinstance(s, tuple)]
+        c = us(o, [x], small(o, x))
+        if op1 is None:
+            emit("v", lambda: g.vector.tensor_scalar(ap(o), ap(x), sc(s1), None, op0), [o], r, cost=c)
+        else:
+            emit("v", lambda: g.vector.tensor_scalar(ap(o), ap(x), sc(s1), sc(s2), op0, op1), [o], r, cost=c)
+
+    def tr(o, x, op, ab=False):
+        emit("v", lambda: g.vector.tensor_reduce(ap(o), ap(x), AxisListType.X, op, apply_absolute_value=ab), [o], [x],
+             cost=us(o, [x], 1))
+
+    def ms(o, c):
+        emit("v", lambda: g.vector.memset(ap(o), c), [o], [], cost=us(o, [o], 1))
+
+    def tp(o, x):
+        emit("v", lambda: g.vector.transpose(ap(o), ap(x)), [o], [x], cost=us(o, [x], 1))
+
+    def act(o, x, f, bias=None, scale=1.0):
+        r = [x] + [s for s in (bias, scale) if isinstance(s, tuple)]
+        c = us(o, [x], 1)
+        if bias is None:
+            emit("a", lambda: g.scalar.activation(ap(o), ap(x), f, scale=sc(scale)), [o], r, cost=c)
+        else:
+            emit("a", lambda: g.scalar.activation(ap(o), ap(x), f, bias=sc(bias), scale=sc(scale)), [o], r, cost=c)
+
+    def mm(o, l, r, start, stop):
+        c = max(64, width(r)) * 0.00083 * (4 if SCRATCH[r[0]][2] == "float32" else 1)
+        emit("t", lambda: g.tensor.matmul(ap(o), ap(l), ap(r), start, stop), [o], [l, r], cost=c)
+
+    def iota(o, pat, base, cm):
+        c = 0.13 + 2 * width(o) * 0.00083
+        if SCRATCH[o[0]][2] == "int32":
+            emit("p", lambda: g.iota(ap(o), pat, base, cm), [o], [], cost=c)
+        else:
+            emit("p", lambda: g.iota(ap(o), pat, base, cm, allow_small_or_imprecise_dtypes=True), [o], [], cost=c)
+
+    def dma(eng, out, in_, writes, reads):
+        s = "d%d" % nd[0]
+        nd[0] += 1
+        emit(eng, lambda: Q[eng].dma_start(out, in_), writes, reads, tok=(s, 16), inc=16,
+             tail=2.0 + sum(width(w) for w in writes) * 128 * 2 / 200e3)
+        return s
+
+    scol = {}
+    jcol = {}
+
+    def S(nm, b=None):
+        if nm not in scol:
+            scol[nm] = 8 * len(scol)
+        c = scol[nm]
+        return v("SM", c, c + 8) if b is None else v("SM", c + b, c + b + 1)
+
+    def J(nm):
+        if nm not in jcol:
+            jcol[nm] = 8 * len(jcol)
+        c = jcol[nm]
+        return v("SI", c, c + 8)
+
+    def send(src, dst, width, sem, to):
+        rid, pid, _e = topo.addr(to)
+        m = topo.mask(core, to)
+        o, i = v(dst, 0, width), v(src, 0, width)
+        emit("p", lambda: g.remote_dma(ap(o), ap(i), T.sem[sem], T.sem.ls, pid, rid, m), [], [i], note=False, cost=0.6)
+        ops.append(("x", None, [], [], None, 0, False, 0.0, 0.0, {len(ops) - 1: 3.0}))
+        dacc[dst].append((len(ops) - 1, v(dst, 0, width), True))
+        cnt["ls"] += len(topo.engines(core, to))
+
+    dma("s", ap(v("VR")), T.vl[:], [v("VR")], [])
+    dma("a", ap(v("CR")), T.cl[:], [v("CR")], [])
+    dma("a", ap(v("X", 2048, 4096)), T.xc[:, 2048:4096], [v("X", 2048, 4096)], [])
+    dma("s", ap(v("X", 0, 2048)), T.xc[:, 0:2048], [v("X", 0, 2048)], [])
+    dma("s", ap(v("NR")), T.ln[:], [v("NR")], [])
+    dma("a", ap(v("THR8")), T.th[:], [v("THR8")], [])
+    dma("a", ap(v("WT")), T.wt[:], [v("WT")], [])
+
+    pi = v("SI", 232, 233)
+    pg = v("SI", 233, 234)
+    pa = v("SI", 234, 235)
+    pp = v("SI", 235, 236)
+    iota(pi, [[1, 1]], 0, 1)
+    iota(v("ROWI"), [[1, 143]], -15, 0)
+    iota(v("CIO"), [[1, 128]], 0, 0)
+    iota(S("BA"), [[16, 8]], 8064, 0)
+    iota(S("B8"), [[1, 8]], 0, 0)
+    iota(v("R0", 0, 256), [[1, 32], [0, 8]], 0, 0)
+    iota(v("R0", 256, 288), [[0, 4], [0, 8]], 64, 0)
+    iota(v("QT"), [[-128, 36], [0, 8]], 8064, 0)
+    iota(v("POS"), [[128, 36], [16, 8]], 0, 0)
+    iota(v("PP"), [[1, 36], [0, 8]], 0, 0)
+    ts(pg, pi, 4, A.arith_shift_right)
+    ts(pa, pi, 15, A.bitwise_and)
+    ts(pp, pi, 4, A.arith_shift_right, 1, A.bitwise_and)
+    pf, pgf, pg16, paf, od, ev, pa8 = [S("cols", b) for b in range(7)]
+    tc(od, pp)
+    ts(ev, pp, -1.0, A.mult, 1.0, A.add)
+    ts(pg16, pg, 16.0, A.mult)
+    tc(pf, pi)
+    tc(pgf, pg)
+    tc(paf, pa)
+    ts(pa8, pa, 8.0, A.mult)
+    ts(v("ID"), v("ROWI", 15, 143), pf, A.is_equal)
+    ts(v("IDM"), v("ROWI", 15, 143), pf, A.is_equal, float(-BIG), A.mult)
+    ts(v("IDH"), v("ID"), float(-BIG // 2), A.mult)
+    ts(v("IDN"), v("ID"), -1.0, A.mult)
+    for nm, wv in (("WB1", 1.0), ("WBK", 16384.0), ("WB4", 4.0), ("WBM", -2.0)):
+        ts(v(nm), v("ROWI"), pg16, A.is_equal, wv, A.mult)
+    for t in range(ST):
+        ms(v("W%d" % t, 256 + 8 * t, 264 + 8 * t), -BIG)
+        if t:
+            ms(v("R%d" % t, 256 + 8 * t, 264 + 8 * t), 64.0)
+    ms(v("X", 4096, NX), 0.0)
+    ms(v("ZERO"), 0.0)
+    ms(v("XB", 0, 8), 0.0)
+    ms(v("ONES"), 1.0)
+
+    def turn(raw, w0, w1):
+        for b in range(8):
+            tp(v("TA", b, 256, 8), v(raw, b, 256, 8))
+            tp(v("TB", b, 256, 8), v("RU", b, 256, 8))
+        ts(v("TC", 0, 128), v("TA", 0, 128), ev, A.mult)
+        ts(v("TC", 128, 256), v("TB", 0, 128), ev, A.mult)
+        ts(v("TE", 0, 128), v("TB", 128, 256), od, A.mult)
+        ts(v("TE", 128, 256), v("TA", 128, 256), od, A.mult)
+        tt(w0, v("TC", 0, 128), v("TE", 0, 128), A.add)
+        tt(w1, v("TC", 128, 256), v("TE", 128, 256), A.add)
+
+    ts(v("OUT"), v("VR"), 4096.0, A.mult, float(-BIG), A.add)
+    tt(v("RT", 0, 128), v("OUT", 0, 256, 2), v("CR", 0, 256, 2), A.add)
+    tt(v("RT", 128, 256), v("OUT", 1, 256, 2), v("CR", 1, 256, 2), A.add)
+    tc(v("RU", 0, 128), v("RT", 128, 256))
+    tc(v("RU", 128, 256), v("RT", 0, 128))
+    turn("RT", v("W0", 0, 128), v("W0", 128, 256))
+
+    def lists(t):
+        P = 32 + t
+        W = "W%d" % t
+        for r0, r1 in ((0, 9), (9, P)):
+            ts(v("VI", r0 * 8, r1 * 8), v(W, r0 * 8, r1 * 8), 12, A.arith_shift_right, 4095, A.bitwise_and)
+            tc(v("VL", r0 * 8, r1 * 8), v("VI", r0 * 8, r1 * 8))
+        ts(v("CI", 0, P * 8 - 16), v(W, 0, P * 8 - 16), 4095, A.bitwise_and)
+        tc(v("CL", 0, P * 8 - 16), v("CI", 0, P * 8 - 16))
+
+    def late_constants():
+        ts(S("wt", 0), v("WT"), 1.0, A.mult)
+        ts(v("WBW"), v("WB1"), S("wt", 0), A.mult)
+        ts(v("CIO"), v("CIO"), 4, A.arith_shift_right)
+        ts(v("BLK"), v("CIO"), pgf, A.is_equal)
+        ts(v("DG"), v("ROWI", 15, 31), paf, A.is_equal, 128.0, A.mult)
+        ts(v("POS"), v("POS"), paf, A.add)
+        ts(S("BA"), S("BA"), paf, A.add)
+        ts(S("II"), S("B8"), pa8, A.add)
+        ts(S("DUMP"), S("II"), 4096.0, A.add)
+        ts(S("KF0"), S("II"), 1.0 / 128, A.mult)
+        tt(S("KF"), S("KF0"), S("DUMP"), A.add)
+        tt(S("V00"), v("VI", 0, 8), S("DUMP"), A.subtract)
+        ts(v("GB", 0, 128, 1, 0, 8), v("CIO", 0, 128, 1, 0, 8), v("SM", pf[1], pf[2], 1, 0, 8), A.is_equal)
+        thf = v("SM", scol["wt"] + 1, scol["wt"] + 2, 1, 0, 8)
+        tc(thf, v("THR8"))
+        mm(v("pS", 0, 1), v("GB", 0, 128, 1, 0, 8), thf, True, True)
+        tc(S("th", 0), v("pS", 0, 1))
+        tc(S("lim", 0), S("th", 0))
+
+    def scalar_constants():
+        act(S("THR"), S("II"), AF.Copy, bias=-0.5, scale=0.5)
+        act(S("HC"), S("II"), AF.Copy, bias=0.5, scale=0.5)
+        act(S("HI"), S("II"), AF.Copy, scale=0.5)
+        act(S("KD"), S("KF"), AF.Copy, scale=128.0)
+        for b in range(8):
+            act(v("EXC", b * 16, b * 16 + 16), v("DG"), AF.Copy, scale=S("KF", b))
+        tt(S("HK"), S("HC"), S("KD"), A.subtract)
+
+    def masks(t):
+        R, G8 = "R%d" % t, (30 + t) * 8
+        mm(v("pI", 0, G8), v("ID"), v(R, 8, G8 + 8), True, False)
+        mm(v("pI", 0, G8), v("IDN"), v(R, 0, G8), False, True)
+        act(S("b25"), S("n%d" % t), AF.Copy, bias=2.5, scale=-1.0)
+        for b in range(8):
+            act(v("INV", b, G8, 8), v(R, b, G8, 8), AF.Sign, bias=S("b25", b))
+        act(v("MK", 0, G8), v("pI", 0, G8), AF.Relu, bias=1.0, scale=-1.0)
+
+    def dedupe(t2):
+        mm(v("pI", 0, 128), v("BLK"), v("EXC"), True, False)
+        for b in range(8):
+            act(v("EX", b * 16, b * 16 + 16), v("DG"), AF.Copy, scale=v("SM", t2[1] + b, t2[1] + b + 1))
+        mm(v("pI", 0, 128), v("BLK"), v("EX"), False, True)
+        ts(S("nc0"), t2, -128.0, A.mult)
+        tt(S("nc"), S("nc0"), S("HK"), A.add)
+
+    def far(b):
+        act(v("AA", b * 128, b * 128 + 128), v("pI", 0, 128), AF.Abs, bias=S("nc", b))
+
+    def hit(b):
+        x, o = v("AA", b * 128, b * 128 + 128), v("AB", b * 128, b * 128 + 128)
+        emit("a", lambda: g.scalar.activation(ap(o), ap(x), AF.Relu, bias=ap(S("HI", b)), scale=-1.0, accum_out=ap(S("hit", b))),
+             [o, S("hit", b)], [x, S("HI", b)], cost=0.126)
+
+    def half(nm, k):
+        c = S(nm)[1]
+        return v("SM", c + NV * k, c + (8 if k else NV))
+
+    def dedupe2(t2, off):
+        for b in range(NV):
+            tr(S("mn", b), v("AA", b * 128, b * 128 + 128), A.min)
+        tt(half("nd", 0), half("mn", 0), half("THR", 0), A.is_gt)
+        ts(half("nd", 1), half("hit", 1), 0.0, A.is_equal)
+        tt(S("t3"), t2, S("nd"), A.mult)
+        tt(S("t4"), S("t3"), S("DUMP"), A.add)
+        tc(v(off), S("t4"))
+
+    xwin = v("X")
+
+    def step(t):
+        P = 32 + t
+        P1, G = P + 1, P - 2
+        n8, m8, G8 = P * 8, P1 * 8, G * 8
+        W, R, Wn, Rn = "W%d" % t, "R%d" % t, "W%d" % (t + 1), "R%d" % (t + 1)
+        YR, M, LW, LY, LM = ["%s%d" % (k, t) for k in ("YR", "M", "LW", "LY", "LM")]
+        n, nn, V0, V0n, TH = S("n%d" % t), S("n%d" % (t + 1)), S("V0%d" % t), S("V0%d" % (t + 1)), S("lim", t)
+        d = 1 + t % 5
+        to, fr = T.cores[(rank + d) % N], T.cores[(rank - d) % N]
+        ne = len(topo.engines(fr, core))
+        for buf, sem, wd in ((LW, "aw", m8), (LY, "ay", 128 + m8), (LM, "am", 24)):
+            record((sem + str(t), ne), [v(buf, 0, wd)], [], {})
+
+        c1, c2, c3 = GCS
+        gc = [(0, c1), (c1, c2), (c2, c3), (c3, G)]
+        vc = [(0, c1 + 1), (c1 + 1, c2 + 1), (c2 + 1, c3 + 1), (c3 + 1, P)]
+
+        def gv(c):
+            r0, r1 = vc[c]
+            for r0, r1 in ([(0, 5), (5, r1)] if c == 0 else [(r0, r1)]):
+                act(v("XV", r0 * 128, r1 * 128), ind(v("X", 0, 4096), v("VL", r0 * 8, r1 * 8)), AF.Copy, scale=0.5)
+
+        def hs(c):
+            r0, r1 = gc[c]
+            return [(r, min(r + 4, r1)) for r in range(r0, r1, 4)]
+
+        hb = ("pA", "pB", "pJ")
+
+        def idp(c):
+            for k, (r0, r1) in enumerate(hs(c)):
+                mm(v(hb[k], 0, (r1 - r0) * 128), v("ID"), v("XV", r0 * 128, r1 * 128), True, r0 < HA)
+                if r0 >= HA:
+                    mm(v(hb[k], 0, (r1 - r0) * 128), v("ID"), v("XV", r0 * 128 + 128, r1 * 128 + 128), False, True)
+
+        def hh(c):
+            for k, (r0, r1) in enumerate(hs(c)):
+                if r0 >= HA:
+                    act(v("H", r0 * 128, r1 * 128), v(hb[k], 0, (r1 - r0) * 128), AF.Copy)
+                    continue
+                tt(v("H", r0 * 128, r1 * 128), v("XV", r0 * 128 + 128, r1 * 128 + 128), v(hb[k], 0, (r1 - r0) * 128), A.add)
+
+        def dd(c):
+            r0, r1 = gc[c]
+            tt(v("D", r0 * 128, r1 * 128), ind(v("X", 0, 4096), v("CL", r0 * 8, r1 * 8)), v("H", r0 * 128, r1 * 128), A.subtract)
+
+        def aba(c):
+            r0, r1 = gc[c]
+            act(v("AB", r0 * 128, r1 * 128), v("D", r0 * 128, r1 * 128), AF.Abs)
+
+        def sums(bank, wb, buf, r0, r1, last):
+            for a in range(16):
+                mm(v(bank, r0 * 8, r1 * 8), v(wb, 15 - a, 143 - a), v(buf, r0 * 128 + a, r1 * 128, 16), False, last and a == 15)
+
+        gv(0)
+        if t == 0:
+            masks(0)
+            late_constants()
+        ts(S("L"), n, 4.0, A.is_ge)
+        tt(S("nL"), n, S("L"), A.mult)
+        idp(0)
+        mm(v("pK", 0, G8), v("ID"), v("QT", 0, G8), True, False)
+        mm(v("pK", 0, G8), v("ID"), v(R, 0, G8), False, False)
+        mm(v("pK", 0, G8), v("IDH"), v("ONES", 0, G8), False, False)
+        mm(v("pK", 0, G8), v("IDH"), v("INV", 0, G8), False, False)
+        mm(v("pK", 0, G8), v("IDM"), v("MK", 0, G8), False, False)
+        mm(v("pD", 0, n8), v("ID"), v("ZERO", 0, n8), True, False)
+        gv(1)
+        gv(2)
+        hh(0)
+        dd(0)
+        idp(1)
+        sums("pD", "WBM", "XV", 0, c1 + 1, False)
+        hh(1)
+        idp(2)
+        sums("pD", "WBM", "XV", c1 + 1, c2 + 1, False)
+        aba(0)
+        sums("pK", "WBK", "AB", 0, c1, False)
+        gv(3)
+        dd(1)
+        hh(2)
+        idp(3)
+        sums("pD", "WBM", "XV", c2 + 1, c3 + 1, False)
+        aba(1)
+        sums("pK", "WBK", "AB", c1, c2, False)
+        dd(2)
+        hh(3)
+        aba(2)
+        sums("pK", "WBK", "AB", c2, c3, False)
+        dd(3)
+        aba(3)
+        sums("pK", "WBK", "AB", gc[3][0], G, True)
+        sums("pD", "WBM", "XV", c3 + 1, P, False)
+        tt(v("pJ", 8, m8), v(W, 0, n8), v(W, 8, m8), A.subtract)
+        if t:
+            cj = v("SI", 236, 237)
+            tc(cj, v("pS", 400, 401))
+            ts(cj, cj, 31, A.bitwise_and)
+            tt(TH, S("th", 0), cj, A.add)
+        ts(v("Z0", 0, G8), v("VI", 0, G8), 4096.0, A.mult, float(-BIG), A.add)
+        tt(v("Z", 0, G8), v("Z0", 0, G8), v("VI", 8, G8 + 8), A.add)
+        if t == 0:
+            scalar_constants()
+
+        for b in range(8):
+            tr(v("SI", J("mx")[1] + b, J("mx")[1] + b + 1), v("pK", b, G8, 8), A.max)
+        ts(J("q"), J("mx"), 8064, A.bitwise_and)
+        tt(S("jk"), S("BA"), J("q"), A.subtract)
+        tc(v("JL"), S("jk"))
+        tc(v("DK"), ind(v("D", 0, G * 128), v("JL")))
+        tt(v("TK"), ind(v("H", 0, G * 128), v("JL")), v("DK"), A.subtract)
+        Y = v(YR, 0, 128)
+        ts(Y, v("TK"), 0.0, A.max, 63.0, A.min)
+        for k in range(2):
+            ts(v("pY", k * 128, k * 128 + 128), Y, 0.5, A.mult)
+        ts(J("k"), J("mx"), 127, A.bitwise_and)
+        tc(S("k"), J("k"))
+        ts(S("bO"), J("mx"), -1.0 / 128, A.mult, 0.5, A.add)
+        act(S("nk"), S("k"), AF.Copy, bias=-1.0, scale=-1.0)
+        act(S("k15"), S("k"), AF.Copy, bias=1.5)
+        act(S("kn"), S("k"), AF.Copy, scale=-1.0)
+        act(v(M, 16, 24), S("L"), AF.Copy)
+        act(S("jb"), S("jk"), AF.Copy, bias=-0.5, scale=-1.0)
+        act(S("jb1"), S("jk"), AF.Copy, bias=-128.0, scale=-1.0)
+        for b in range(8):
+            act(v(YR, 128 + b, 128 + m8, 8), v(R, b, m8, 8), AF.Relu, bias=S("nk", b))
+        send(W, LW, m8, "aw%d" % t, to)
+        send(YR, LY, 128 + m8, "ay%d" % t, to)
+        for b in range(8):
+            act(v("pA", b, n8, 8), v(R, b, n8, 8), AF.Relu, bias=S("k15", b), scale=-1.0)
+        for b in range(8):
+            act(v("RQ", b, n8, 8), v(R, b, n8, 8), AF.Relu, bias=S("nL", b), scale=-1.0)
+        for b in range(8):
+            act(v("pB", b, G8, 8), v("pK", b, G8, 8), AF.Sign, bias=S("bO", b), scale=1.0 / 128)
+
+        for a in range(16):
+            mm(v("pS", 304, 312), v("WB1", 15 - a, 143 - a), v(YR, a, 128, 16), a == 0, a == 15)
+        dc = [(2, 8), (8, 16), (16, 24), (24, P)]
+        for c, (r0, r1) in enumerate(dc):
+            for r in range(r0, r1, 2):
+                e = min(r + 2, r1)
+                tt(v("AB", r * 128, e * 128), v("XV", r * 128, e * 128), v("pY", 0, (e - r) * 128), A.max)
+            sums("pD", "WB4", "AB", r0, r1, c == 3)
+            if c == 1:
+                ts(S("lm"), v("pS", 304, 312), TH, A.add)
+                for b in range(8):
+                    act(v("LX", b, n8, 8), v("pA", b, n8, 8), AF.Identity, bias=S("lm", b), scale=-8192.0)
+                for b in range(8):
+                    act(v("SP", b, m8, 8), v("POS", b, m8, 8), AF.Sign, bias=S("jb", b))
+                for b in range(8):
+                    act(v("OA", b, m8, 8), v("POS", b, m8, 8), AF.Abs, bias=S("jb1", b))
+                act(v("OA", 0, m8), v("OA", 0, m8), AF.Relu, bias=1.0, scale=-1.0)
+                for b in range(8):
+                    act(v("A2", b, m8, 8), v(R, b, m8, 8), AF.Relu, bias=S("k", b), scale=-1.0)
+        for a in range(16):
+            mm(v("pI", 0, 8), v("WBW", 15 - a, 143 - a), v(YR, a, 128, 16), a == 0, a == 15)
+        mm(v("pY", 8, m8), v("ID"), v("ONES", 8, m8), True, False)
+        mm(v("pY", 8, m8), v("ID"), v(R, 0, n8), False, False)
+        mm(v("pY", 8, m8), v("IDN"), v(R, 8, m8), False, True)
+        tt(S("nk1"), n, S("nk"), A.add)
+        tt(v("PZ", 0, G8), v("pB", 0, G8), v("Z", 0, G8), A.mult)
+        for b in range(8):
+            tr(v("SI", J("z")[1] + b, J("z")[1] + b + 1), v("PZ", b, G8, 8), A.min)
+        ts(J("vk"), J("z"), 12, A.arith_shift_right, 4095, A.bitwise_and)
+        ts(J("vk1"), J("z"), 4095, A.bitwise_and)
+        tt(v(M, 8, 16), J("vk1"), S("DUMP"), A.subtract)
+        tt(v("pA", 0, n8), v("pD", 0, n8), v("LX", 0, n8), A.is_le)
+        tt(v("PZ", 0, n8), v("pA", 0, n8), v("RQ", 0, n8), A.mult)
+        for b in range(8):
+            tr(S("vm", b), v("PZ", b, n8, 8), A.max)
+        ts(S("cl"), S("vm"), 0.0, A.is_gt)
+        tt(S("sz0"), S("cl"), S("nk1"), A.mult)
+        tt(v(M, 0, 8), S("sz0"), S("vm"), A.subtract)
+        sz = v(M, 0, 8)
+        send(M, LM, 24, "am%d" % t, to)
+        tt(S("gr"), S("L"), S("cl"), A.subtract)
+        for b in range(8):
+            act(v("GG", b, m8, 8), v("SP", b, m8, 8), AF.Relu, scale=S("gr", b))
+
+        tc(J("u"), v("pI", 0, 8))
+        ts(J("u2"), J("u"), 4095, A.bitwise_and)
+        tt(J("uu"), J("u2"), J("u2"), A.mult)
+        ts(J("v37"), J("vk"), 37.0, A.mult)
+        ts(J("us"), J("uu"), 5, A.arith_shift_right)
+        tt(J("h0"), J("us"), J("v37"), A.add)
+        ts(J("h"), J("h0"), 4095, A.bitwise_and)
+        tt(S("hd"), J("h"), S("DUMP"), A.subtract)
+        tt(S("t2g"), S("hd"), S("gr"), A.mult)
+        dedupe(S("t2g"))
+        ts(S("wn0"), J("h"), 4096.0, A.mult, float(-BIG), A.add)
+        tt(S("wn1"), S("wn0"), J("vk"), A.add)
+        tt(S("wn"), S("wn1"), S("gr"), A.mult)
+        for b in range(8):
+            act(v("pD", b, m8, 8), v("OA", b, m8, 8), AF.Copy, scale=S("wn", b))
+        tt(v("XB", 8, m8), v("GG", 8, m8), v("pY", 8, m8), A.mult)
+        mm(v("pA", 0, m8), v("ID"), v(R, 0, m8), True, False)
+        mm(v("pA", 0, m8), v("ID"), v("XB", 0, m8), False, True)
+        tt(v("pB", 8, m8), v("GG", 8, m8), v("pJ", 8, m8), A.mult)
+        tt(v("WA", 8, m8), v(W, 8, m8), v("pB", 8, m8), A.add)
+        tc(v("WA", 0, 8), v(W, 0, 8))
+        tt(S("kns"), S("kn"), sz, A.subtract)
+        tt(S("zl"), J("z"), S("L"), A.mult)
+        act(v("YX", 0, 8), S("cl"), AF.Copy)
+        act(S("rest"), S("L"), AF.Copy, bias=1.0, scale=-1.0)
+        for b in range(8):
+            far(b)
+        for b in range(NV, 8):
+            hit(b)
+        for b in range(8):
+            act(v("A1", b, m8, 8), v("pA", b, m8, 8), AF.Relu, bias=S("kns", b))
+        tt(S("ng"), n, S("gr"), A.add)
+        ts(S("ng"), S("ng"), 32.0, A.min)
+        tt(S("n2"), S("ng"), sz, A.subtract)
+        dedupe2(S("t2g"), "OL")
+        tc(ind(xwin, v("OL")), Y)
+        mm(v("pA", 0, m8), v("ID"), v("A1", 0, m8), True, False)
+        mm(v("pA", 0, m8), v("IDN"), v("A2", 0, m8), False, True)
+        act(v("RQ", 0, m8), v("pA", 0, m8), AF.Abs)
+        act(v("RQ", 0, m8), v("RQ", 0, m8), AF.Relu, bias=1.0, scale=-1.0)
+        mm(v("pS", 0, m8), v("ID"), v(LY, 128, 128 + m8), True, False)
+        mm(v("pS", 0, m8), v("IDN"), v(R, 0, m8), False, True)
+        if t < ST - 1:
+            for b in range(8):
+                mm(v("pS", 400, 401), v("ONES", 0, 128), v("YX", b, b + 1), b == 0, b == 7)
+
+        tt(S("rc"), v(LM, 0, 8), S("rest"), A.mult)
+        tt(S("dv"), v(LM, 8, 16), V0, A.subtract)
+        tt(S("tk"), S("rc"), S("n2"), A.is_gt)
+        tt(nn, S("rc"), S("n2"), A.max)
+        tt(S("dvt"), S("dv"), S("tk"), A.mult)
+        tt(S("has"), nn, v(LM, 16, 24), A.min)
+        tt(V0n, V0, S("dvt"), A.add)
+        tt(S("t2b"), V0n, S("has"), A.mult)
+        dedupe(S("t2b"))
+        for b in range(8):
+            act(v("T1", b, m8, 8), v("RQ", b, m8, 8), AF.Copy, scale=S("zl", b))
+        for b in range(8):
+            act(v("RX", b, m8, 8), v("pA", b, m8, 8), AF.Identity, bias=S("k", b))
+        for b in range(8):
+            ts(v("pK", b, m8, 8), v(LW, b, m8, 8), S("tk", b), A.mult)
+        tt(v("TM", 0, m8), v("T1", 0, m8), v("pD", 0, m8), A.add)
+        tt(v("TM", 0, m8), v("TM", 0, m8), v("pK", 0, m8), A.add)
+        ts(v("pY", 0, m8), v("TM", 0, m8), 0.0, A.is_equal)
+        tt(v("pB", 0, m8), v("WA", 0, m8), v("pY", 0, m8), A.mult)
+        tt(v(Wn, 0, m8), v("TM", 0, m8), v("pB", 0, m8), A.add)
+        for b in range(8):
+            far(b)
+        for b in range(NV, 8):
+            hit(b)
+        for b in range(8):
+            act(v("TDR", b, m8, 8), v("pS", b, m8, 8), AF.Copy, scale=S("tk", b))
+        mm(v("pJ", 0, m8), v("ID"), v("RX", 0, m8), True, False)
+        mm(v("pJ", 0, m8), v("ID"), v("TDR", 0, m8), False, True)
+        act(v(Rn, 0, m8), v("pJ", 0, m8), AF.Copy)
+        dedupe2(S("t2b"), "OB")
+        tt(v("BS"), ind(xwin, v("OB")), v(LY, 0, 128), A.add)
+        if t < ST - 1:
+            masks(t + 1)
+        else:
+            mm(v("pA", 0, 280), v("ID"), v(Rn, 8, 288), True, False)
+            mm(v("pA", 0, 280), v("IDN"), v(Rn, 0, 280), False, True)
+            mm(v("pY", 0, 288), v("ID"), v("PP"), True, False)
+            mm(v("pY", 0, 288), v("IDN"), v(Rn), False, True)
+            act(S("n5"), nn, AF.Copy, bias=-0.5)
+            for b in range(8):
+                act(v("SP", b, 288, 8), v(Rn, b, 288, 8), AF.Sign, bias=S("n5", b), scale=-1.0)
+            act(v("pB", 0, 288), v("SP"), AF.Relu)
+            act(v("T1", 0, 280), v("pA", 0, 280), AF.Sign)
+        ts(v("BO"), v("BS"), 0.5, A.mult, -0.25, A.add)
+        tc(ind(xwin, v("OB")), v("BO"))
+        if t < ST - 1:
+            lists(t + 1)
+
+    lists(0)
+    tc(S("n0"), v("NR"))
+    for t in range(ST):
+        step(t)
+
+    so = [dma("s", T.yx[:, 0:2048], ap(v("X", 0, 2048)), [], [v("X", 0, 2048)]),
+          dma("a", T.yx[:, 2048:4096], ap(v("X", 2048, 4096)), [], [v("X", 2048, 4096)]),
+          dma("s", T.yn[:], ap(S("n4")), [], [S("n4")])]
+    ms(v("T1", 280, 288), 1.0)
+    ts(v("U"), v("W4"), float(BIG), A.add)
+    tt(v("E"), v("T1"), v("pB", 0, 288), A.mult)
+    tt(v("DLT"), v("E"), v("pY", 0, 288), A.mult)
+    tt(v("U"), v("U"), v("E"), A.mult)
+    for i in range(6):
+        lo = 8 << i
+        w = 288 - lo
+        ts(v("BIT", lo, 288), v("DLT", lo, 288), i, A.arith_shift_right, 1, A.bitwise_and)
+        tc(v("pA", lo, 288), v("BIT", lo, 288))
+        tt(v("pB", lo, 288), v("U", lo, 288), v("pA", lo, 288), A.mult)
+        if i < 5:
+            tt(v("pK", lo, 288), v("DLT", lo, 288), v("pA", lo, 288), A.mult)
+        tt(v("U", lo, 288), v("U", lo, 288), v("pB", lo, 288), A.subtract)
+        if i < 5:
+            tt(v("DLT", lo, 288), v("DLT", lo, 288), v("pK", lo, 288), A.subtract)
+        tt(v("U", 0, w), v("U", 0, w), v("pB", lo, 288), A.add)
+        if i < 5:
+            tt(v("DLT", 0, w), v("DLT", 0, w), v("pK", lo, 288), A.add)
+    tc(v("RU", 0, 128), v("U", 128, 256))
+    tc(v("RU", 128, 256), v("U", 0, 128))
+    turn("U", v("OI", 0, 256, 2), v("OI", 1, 256, 2))
+    ts(v("VI", 0, 256), v("OI"), 12, A.arith_shift_right)
+    tc(v("OV"), v("VI", 0, 256))
+    so.append(dma("s", T.yv[:], ap(v("OV")), [], [v("OV")]))
+    ts(v("CI", 0, 256), v("OI"), 4095, A.bitwise_and)
+    tc(v("OC"), v("CI", 0, 256))
+    so.append(dma("a", T.yc[:], ap(v("OC")), [], [v("OC")]))
+    flush()
+    for s in so:
+        g.sync.wait_ge(T.sem[s], 16)
+    for s in ("qv", "qa", "qt", "qp"):
+        g.sync.wait_ge(T.sem[s], cnt[s])
+    g.wait_ge(T.sem.ls, cnt["ls"])

@@ -7,50 +7,75 @@ AF = ActivationFunctionType
 N = 6
 ST = 4
 BIG = 16777216
-NX = 4224
-NV = 5
+NX = 4112
+SG = 37
+NL = 8 * SG
 SLACK = 0.03
-HA = 21
-GCS = (8, 17, 26)
+LAT = 0.06
+FLY = 2.5
+EARLY = 8.0
+WAYS = "XZXZXYYYY"
+VCUT = (5, 9, 17, 25)
+TCUT = (4, 8, 16, 24, 28)
 
 SCRATCH = {}
+TILES = {}
 
 
 def _add(where, dtype, names, cols, rows=128):
     for nm in names.split():
-        SCRATCH[nm] = (where, [rows, cols], dtype)
+        if where == "psum" or cols > 1024:
+            SCRATCH[nm] = (where, [rows, cols], dtype)
+            TILES[nm] = (where, [rows, cols], dtype, nm, 0)
+        else:
+            buf = "all_" + dtype
+            at = SCRATCH[buf][1][1] if buf in SCRATCH else 0
+            SCRATCH[buf] = (where, [128, at + (cols + 15) // 16 * 16], dtype)
+            TILES[nm] = (where, [rows, cols], dtype, buf, at)
 
 
 _add("sbuf", "bfloat16", "X", NX)
-_add("sbuf", "bfloat16", "XV H D AB", 4480)
-_add("sbuf", "int32", "W0 W1 W2 W3 W4 LW0 LW1 LW2 LW3 VI CI DLT BIT", 288)
-_add("sbuf", "bfloat16", "R0 R1 R2 R3 R4 QT ZERO ONES INV MK PP XB A1 A2 RX TDR", 288)
-_add("sbuf", "float32", "POS Z Z0 RQ LX OA SP GG PZ WA E T1 TM U", 288)
+_add("sbuf", "bfloat16", "XV T1 D AB", 4480)
+_add("sbuf", "int32", "W0 W1 W2 W3 W4 LW0 LW1 LW2 LW3 KS FS", 296)
+_add("sbuf", "int32", "VI CI DLT BIT", 288)
 _add("sbuf", "uint16", "VL CL", 288)
-_add("sbuf", "uint16", "JL OL OB", 8)
-_add("sbuf", "bfloat16", "YR0 YR1 YR2 YR3 LY0 LY1 LY2 LY3", 416)
-_add("sbuf", "float32", "M0 M1 M2 M3 LM0 LM1 LM2 LM3", 24)
-_add("sbuf", "float32", "SM", 720)
-_add("sbuf", "int32", "SI", 240)
-_add("sbuf", "float32", "ROWI", 143)
-_add("sbuf", "bfloat16", "WB1 WBK WB4 WBM WBW", 143)
-_add("sbuf", "bfloat16", "ID IDM IDH IDN DK TK BI YX", 128)
-_add("sbuf", "float32", "BLK GB EX EXC", 128)
-_add("sbuf", "int32", "CIO BO", 128)
-_add("sbuf", "float32", "BS", 128)
-_add("sbuf", "float32", "DG", 16)
-_add("sbuf", "float32", "AA", 1024)
-_add("sbuf", "int32", "VR CR", 256)
-_add("sbuf", "float32", "RT RU TA TB TC TE OUT", 256)
-_add("sbuf", "float32", "OV OC", 256)
-_add("sbuf", "int32", "OI", 256)
-_add("sbuf", "int32", "NR", 8)
-_add("sbuf", "int32", "THR8", 1, 8)
+_add("sbuf", "bfloat16", "R0 R1 R2 R3 R4", 298)
+_add("sbuf", "bfloat16", "Q NF QT DM CM S1 A1 B1 TDR RS P32 BR ONES", 296)
+_add("sbuf", "bfloat16", "SEG THX", 296, 64)
+_add("sbuf", "float32", "PL SEGI", 296)
+_add("sbuf", "bfloat16", "PP SP G1 ZS SK SO RT4", 288)
+_add("sbuf", "float32", "POS OA ZM WA DW U RT", 288)
+_add("sbuf", "float32", "UF", 384)
+_add("sbuf", "float32", "TAB", 512)
+_add("sbuf", "uint16", "JL OF", 16)
+_add("sbuf", "uint16", "XL XF OG", 8)
+_add("sbuf", "uint16", "LI LO", 16)
+_add("sbuf", "uint16", "LS LU", 18)
+_add("sbuf", "bfloat16", "YR0 YR1 YR2 YR3 LY0 LY1 LY2 LY3", 424)
+_add("sbuf", "int32", "M0 M1 M2 M3 LM0 LM1 LM2 LM3", 16)
+_add("sbuf", "float32", "MV0 MV1 MV2 MV3 LV0 LV1 LV2 LV3", 8)
+_add("sbuf", "float32", "SM", 1600)
+_add("sbuf", "int32", "SI", 480)
+_add("sbuf", "float32", "ROWI", 256)
+_add("sbuf", "bfloat16", "WBW", 143)
+_add("sbuf", "bfloat16", "C2 RZ", 256)
+_add("sbuf", "bfloat16", "ID IDN I22 N22 I21 IDH DG TRI EXB GA GB GC EQ EC GX NB", 128)
+_add("sbuf", "float16", "BLK EXH", 128)
+_add("sbuf", "float16", "CVH", 8)
+_add("sbuf", "bfloat16", "BW CV", 24)
+_add("sbuf", "float32", "IDF EXR ONF", 128)
+_add("sbuf", "float32", "GV", 256)
+_add("sbuf", "int32", "SC VR CR OI", 256)
+_add("sbuf", "int32", "BO CIO", 128)
+_add("sbuf", "float32", "OV OC NM", 256)
+_add("sbuf", "int32", "NR", 128, 8)
+_add("sbuf", "float32", "NO", 128, 8)
+_add("sbuf", "int32", "TH8", 4, 64)
 _add("sbuf", "int32", "WT", 1)
-_add("psum", "float32", "pA pB pK pD pY pS pI pJ", 512)
+_add("psum", "float32", "pA pB pC pK pD pY pT pR", 512)
 
-SEMAPHORES = ["qv", "qa", "qt", "qp", "ls"] + ["d%d" % i for i in range(12)] + [
-    m + str(t) for m in ("aw", "ay", "am") for t in range(ST)]
+SEMAPHORES = ["qv", "qa", "qt", "qp", "ls"] + ["d%d" % i for i in range(14)] + [
+    m + str(t) for m in ("aw", "ay", "av", "am") for t in range(ST)]
 
 
 def rank_program(g, core, T, topo):
@@ -61,20 +86,22 @@ def rank_program(g, core, T, topo):
     SEM = {"v": "qv", "a": "qa", "t": "qt", "p": "qp", "s": None}
     cnt = {"qv": 0, "qa": 0, "qt": 0, "qp": 0, "ls": 0}
     clk = {e: {} for e in Q}
-    acc = {n: [] for n in SCRATCH}
+    acc = {n: [] for n in TILES}
     nd = [0]
+    boost = [0.0]
 
     def v(name, lo=0, hi=None, step=1, p0=0, p1=None):
-        sh = SCRATCH[name][1]
+        sh = TILES[name][1]
         return (name, lo, sh[1] if hi is None else hi, step, p0, sh[0] if p1 is None else p1)
 
     def ap(w):
         if w[0] == "ind":
             return ap(w[1]).indirect(ap(w[2]))
         n, lo, hi, st, p0, p1 = w
+        buf, at = TILES[n][3:]
         if st == 1:
-            return T[n][p0:p1, lo:hi]
-        return T[n][p0:p1, lo:hi:st]
+            return T[buf][p0:p1, at + lo:at + hi]
+        return T[buf][p0:p1, at + lo:at + hi:st]
 
     def ind(win, off):
         return ("ind", win, off)
@@ -87,12 +114,19 @@ def rank_program(g, core, T, topo):
         return True
 
     def covers(x, y):
-        return x[3] == 1 and x[1] <= y[1] and x[2] >= y[2] and x[4] <= y[4] and x[5] >= y[5]
+        if x[3] > 1 and (x[3] != y[3] or (x[1] - y[1]) % x[3]):
+            return False
+        return x[1] <= y[1] and x[2] >= y[2] and x[4] <= y[4] and x[5] >= y[5]
 
-    ops, dacc, phase = [], {n: [] for n in SCRATCH}, {n: [] for n in SCRATCH}
-    LAT = 0.06
+    ops, dacc, phase, extra, chains = [], {n: [] for n in TILES}, {n: [] for n in TILES}, {}, {}
+
+    def after(name):
+        if name in chains:
+            ops[-1][9].setdefault(chains[name], 0.0)
+        chains[name] = len(ops) - 1
 
     def emit(eng, call, writes, reads, tok=None, inc=1, note=True, cost=0.1, tail=0.0):
+        extra[len(ops)] = boost[0]
         ws = [w[1] if w[0] == "ind" else w for w in writes]
         rs = [w[2] for w in writes if w[0] == "ind"]
         for w in reads:
@@ -104,14 +138,16 @@ def rank_program(g, core, T, topo):
         for lst, wr in ((rs, False), (ws, True)):
             for w in lst:
                 psum = w[0][0] == "p"
-                for (i, w2, wr2) in dacc[w[0]]:
-                    e2 = ops[i][0]
-                    if (wr or wr2) and (meets(w, w2) or (psum and eng == "t" and e2 == "t")):
-                        deps[i] = max(deps.get(i, 0.0), 0.0 if psum and e2 == eng == "t" else LAT)
+                if not (psum and eng == "t"):
+                    for (i, w2, wr2) in dacc[w[0]]:
+                        if (wr or wr2) and meets(w, w2):
+                            deps[i] = LAT
                 if psum:
                     ph = phase[w[0]]
                     if ph and ph[-1][0] == eng:
                         prev = ph[-2][1] if len(ph) > 1 else []
+                        if eng == "t" and ph[-1][1][-1] != me:
+                            deps[ph[-1][1][-1]] = 0.0
                         ph[-1][1].append(me)
                     else:
                         prev = ph[-1][1] if ph else []
@@ -122,7 +158,10 @@ def rank_program(g, core, T, topo):
         for w in rs:
             dacc[w[0]].append((me, w, False))
         for w in ws:
-            dacc[w[0]] = [x for x in dacc[w[0]] if not covers(w, x[1])] + [(me, w, True)]
+            if w[0][0] == "p" and eng == "t":
+                dacc[w[0]] = []
+            else:
+                dacc[w[0]] = [x for x in dacc[w[0]] if not covers(w, x[1])] + [(me, w, True)]
         ops.append((eng, call, writes, reads, tok, inc, note, cost, tail, deps))
 
     def flush():
@@ -134,7 +173,7 @@ def rank_program(g, core, T, topo):
         pri = [0.0] * n
         for i in range(n - 1, -1, -1):
             o = ops[i]
-            pri[i] = o[7] + max([o[8] + l + pri[s] for s, l in succ[i]] + [0.0])
+            pri[i] = o[7] + o[8] + max([l + pri[s] for s, l in succ[i]] + [0.0]) + extra.get(i, 0.0)
         left = [len(o[9]) for o in ops]
         ready = {e: [] for e in list(Q) + ["x"]}
         avail = [0.0] * n
@@ -225,7 +264,7 @@ def rank_program(g, core, T, topo):
         for w in ws:
             old = acc[w[0]]
             if w[0][0] == "p":
-                old = [x for x in old if x[0][0] == tok[0]]
+                old = [x for x in old if x[0][0] == tok[0] and tok[0] != "qt"]
             acc[w[0]] = [x for x in old if not covers(w, x[1])] + [(tok, w, True, snap)]
 
     def sc(x):
@@ -244,7 +283,7 @@ def rank_program(g, core, T, topo):
         return max(64, max(width(x) for x in ins) * rate) * 0.00083 + fix
 
     def small(*vs):
-        return 0.5 if all(x[0] != "ind" and x[0][0] != "p" and SCRATCH[x[0]][2] in ("bfloat16", "uint16") for x in vs) else 1
+        return 0.5 if all(x[0] != "ind" and x[0][0] != "p" and TILES[x[0]][2] in ("bfloat16", "uint16") for x in vs) else 1
 
     def tc(o, i):
         emit("v", lambda: g.vector.tensor_copy(ap(o), ap(i)), [o], [i], cost=us(o, [i], small(o, i)))
@@ -261,31 +300,36 @@ def rank_program(g, core, T, topo):
         else:
             emit("v", lambda: g.vector.tensor_scalar(ap(o), ap(x), sc(s1), sc(s2), op0, op1), [o], r, cost=c)
 
-    def tr(o, x, op, ab=False):
-        emit("v", lambda: g.vector.tensor_reduce(ap(o), ap(x), AxisListType.X, op, apply_absolute_value=ab), [o], [x],
-             cost=us(o, [x], 1))
+    def scan(o, x, y, op0, op1):
+        emit("v", lambda: g.vector.tensor_tensor_scan(ap(o), ap(x), ap(y), 0.0, op0, op1), [o], [x, y], cost=us(o, [x, y], 1))
 
     def ms(o, c):
-        emit("v", lambda: g.vector.memset(ap(o), c), [o], [], cost=us(o, [o], 1))
+        emit("v", lambda: g.vector.memset(ap(o), c), [o], [], cost=us(o, [o], small(o)))
 
     def tp(o, x):
         emit("v", lambda: g.vector.transpose(ap(o), ap(x)), [o], [x], cost=us(o, [x], 1))
 
-    def act(o, x, f, bias=None, scale=1.0):
+    def act(o, x, f, bias=None, scale=1.0, acc_out=None):
         r = [x] + [s for s in (bias, scale) if isinstance(s, tuple)]
         c = us(o, [x], 1)
-        if bias is None:
+        if acc_out is not None:
+            emit("a", lambda: g.scalar.activation(ap(o), ap(x), f, accum_out=ap(acc_out)), [o, acc_out], r, cost=c + 0.02)
+        elif bias is None:
             emit("a", lambda: g.scalar.activation(ap(o), ap(x), f, scale=sc(scale)), [o], r, cost=c)
         else:
             emit("a", lambda: g.scalar.activation(ap(o), ap(x), f, bias=sc(bias), scale=sc(scale)), [o], r, cost=c)
 
-    def mm(o, l, r, start, stop):
-        c = max(64, width(r)) * 0.00083 * (4 if SCRATCH[r[0]][2] == "float32" else 1)
+    def mm(o, l, r, start=False, stop=False):
+        c = max(min(64, width(l)), width(r)) * 0.00083 * (4 if TILES[r[0]][2] == "float32" else 1)
         emit("t", lambda: g.tensor.matmul(ap(o), ap(l), ap(r), start, stop), [o], [l, r], cost=c)
+
+    def lin(o, *terms):
+        for k, (l, r) in enumerate(terms):
+            mm(o, l, r, k == 0, k == len(terms) - 1)
 
     def iota(o, pat, base, cm):
         c = 0.13 + 2 * width(o) * 0.00083
-        if SCRATCH[o[0]][2] == "int32":
+        if TILES[o[0]][2] == "int32":
             emit("p", lambda: g.iota(ap(o), pat, base, cm), [o], [], cost=c)
         else:
             emit("p", lambda: g.iota(ap(o), pat, base, cm, allow_small_or_imprecise_dtypes=True), [o], [], cost=c)
@@ -293,480 +337,483 @@ def rank_program(g, core, T, topo):
     def dma(eng, out, in_, writes, reads):
         s = "d%d" % nd[0]
         nd[0] += 1
-        emit(eng, lambda: Q[eng].dma_start(out, in_), writes, reads, tok=(s, 16), inc=16,
-             tail=2.0 + sum(width(w) for w in writes) * 128 * 2 / 200e3)
+        emit(eng, lambda: Q[eng].dma_start(out, in_), writes, reads, tok=(s, 16), inc=16, cost=0.05,
+             tail=2.0 + sum(width(w) for w in writes + reads) * 128 * 2 / 100e3)
         return s
 
-    scol = {}
-    jcol = {}
+    scol, jcol = {}, {}
 
-    def S(nm, b=None):
+    def S(nm, lo=0, hi=8, step=1, p0=0, p1=128):
         if nm not in scol:
-            scol[nm] = 8 * len(scol)
-        c = scol[nm]
-        return v("SM", c, c + 8) if b is None else v("SM", c + b, c + b + 1)
+            scol[nm] = 16 * len(scol)
+        return v("SM", scol[nm] + lo, scol[nm] + hi, step, p0, p1)
 
-    def J(nm):
+    def J(nm, lo=0, hi=8, p0=0, p1=128):
         if nm not in jcol:
-            jcol[nm] = 8 * len(jcol)
-        c = jcol[nm]
-        return v("SI", c, c + 8)
+            jcol[nm] = 16 * len(jcol)
+        return v("SI", jcol[nm] + lo, jcol[nm] + hi, 1, p0, p1)
+
+    def S2(nm):
+        return S(nm, 0, 16)
+
+    def col(w, b):
+        return (w[0], w[1] + b, w[1] + b + 1, 1, w[4], w[5])
+
+    def seg(nm, k, off=0):
+        return v(nm, off + k * SG + 1, off + k * SG + SG)
+
+    def row(nm, p):
+        return v(nm, SG - 1 - p, NL, SG)
 
     def send(src, dst, width, sem, to):
         rid, pid, _e = topo.addr(to)
         m = topo.mask(core, to)
         o, i = v(dst, 0, width), v(src, 0, width)
         emit("p", lambda: g.remote_dma(ap(o), ap(i), T.sem[sem], T.sem.ls, pid, rid, m), [], [i], note=False, cost=0.6)
-        ops.append(("x", None, [], [], None, 0, False, 0.0, 0.0, {len(ops) - 1: 3.0}))
+        ops.append(("x", None, [], [], None, 0, False, 0.0, 0.0, {len(ops) - 1: FLY + width / 80.0}))
         dacc[dst].append((len(ops) - 1, v(dst, 0, width), True))
         cnt["ls"] += len(topo.engines(core, to))
 
+    ID, IDN, DG = v("ID"), v("IDN"), v("DG")
+
+    ms(v("TH8"), 0)
     dma("s", ap(v("VR")), T.vl[:], [v("VR")], [])
     dma("a", ap(v("CR")), T.cl[:], [v("CR")], [])
     dma("a", ap(v("X", 2048, 4096)), T.xc[:, 2048:4096], [v("X", 2048, 4096)], [])
     dma("s", ap(v("X", 0, 2048)), T.xc[:, 0:2048], [v("X", 0, 2048)], [])
     dma("s", ap(v("NR")), T.ln[:], [v("NR")], [])
-    dma("a", ap(v("THR8")), T.th[:], [v("THR8")], [])
     dma("a", ap(v("WT")), T.wt[:], [v("WT")], [])
+    for p0, e in ((0, "s"), (32, "a")):
+        dma(e, ap(v("TH8", 0, 1, 1, p0, p0 + 8)), T.th[:], [v("TH8", 0, 4, 1, p0, p0 + 8)], [])
 
-    pi = v("SI", 232, 233)
-    pg = v("SI", 233, 234)
-    pa = v("SI", 234, 235)
-    pp = v("SI", 235, 236)
+    pi, pg, pa = J("pi", 0, 1), J("pi", 1, 2), J("pi", 2, 3)
     iota(pi, [[1, 1]], 0, 1)
-    iota(v("ROWI"), [[1, 143]], -15, 0)
-    iota(v("CIO"), [[1, 128]], 0, 0)
-    iota(S("BA"), [[16, 8]], 8064, 0)
-    iota(S("B8"), [[1, 8]], 0, 0)
-    iota(v("R0", 0, 256), [[1, 32], [0, 8]], 0, 0)
-    iota(v("R0", 256, 288), [[0, 4], [0, 8]], 64, 0)
-    iota(v("QT"), [[-128, 36], [0, 8]], 8064, 0)
-    iota(v("POS"), [[128, 36], [16, 8]], 0, 0)
+    iota(v("ROWI"), [[1, 256]], 0, 0)
+    iota(J("li", 0, 16), [[256, 2], [2, 8]], 0, 0)
+    iota(v("CIO"), [[0, 8], [1, 16]], 0, 0)
+    iota(v("R0", 0, NL), [[0, 8], [-1, SG]], SG - 1, 0)
+    iota(v("QT"), [[0, 8], [32, SG]], 27 * 32, 0)
+    iota(v("SEGI"), [[1, 8], [0, SG]], 0, 0)
+    iota(v("POS"), [[1, 288]], 0, 0)
+    iota(v("P32"), [[0, 8], [-32, SG]], 32 * (SG - 1), 0)
+    iota(S("cj", 0, 8), [[16, 8]], 63 * 128, 0)
+    iota(S("cj", 8, 16), [[1, 8]], 63 * 8, 0)
+    iota(J("lo", 0, 16), [[32, 8], [8, 2]], 0, 0)
     iota(v("PP"), [[1, 36], [0, 8]], 0, 0)
+    B8 = v("ROWI", 0, 8)
     ts(pg, pi, 4, A.arith_shift_right)
     ts(pa, pi, 15, A.bitwise_and)
-    ts(pp, pi, 4, A.arith_shift_right, 1, A.bitwise_and)
-    pf, pgf, pg16, paf, od, ev, pa8 = [S("cols", b) for b in range(7)]
-    tc(od, pp)
-    ts(ev, pp, -1.0, A.mult, 1.0, A.add)
-    ts(pg16, pg, 16.0, A.mult)
-    tc(pf, pi)
-    tc(pgf, pg)
-    tc(paf, pa)
-    ts(pa8, pa, 8.0, A.mult)
-    ts(v("ID"), v("ROWI", 15, 143), pf, A.is_equal)
-    ts(v("IDM"), v("ROWI", 15, 143), pf, A.is_equal, float(-BIG), A.mult)
-    ts(v("IDH"), v("ID"), float(-BIG // 2), A.mult)
-    ts(v("IDN"), v("ID"), -1.0, A.mult)
-    for nm, wv in (("WB1", 1.0), ("WBK", 16384.0), ("WB4", 4.0), ("WBM", -2.0)):
-        ts(v(nm), v("ROWI"), pg16, A.is_equal, wv, A.mult)
-    for t in range(ST):
-        ms(v("W%d" % t, 256 + 8 * t, 264 + 8 * t), -BIG)
-        if t:
-            ms(v("R%d" % t, 256 + 8 * t, 264 + 8 * t), 64.0)
+    pf, pgf, paf, dump, dumpk, dk4, q31, is8 = [S("cols", b, b + 1) for b in range(8)]
+    tc(S("cols", 0, 3), J("pi", 0, 3))
+
+    def bits(o, x, sh, mask):
+        ts(o, x, sh, A.arith_shift_right, mask, A.bitwise_and)
+
+    k = [J("k", b, b + 1) for b in range(16)]
+    f = [S("kf", b, b + 1) for b in range(16)]
+    bits(k[0], pi, 4, 1)
+    bits(k[1], pi, 3, 1)
+    bits(k[2], pi, 0, 7)
+    tt(k[3], k[2], k[0], A.subtract)
+    bits(k[4], k[3], 0, 1)
+    bits(k[5], k[3], 1, 3)
+    ts(f[0], k[0], 16.0, A.mult)
+    ts(f[1], k[4], 128.0, A.mult, f[0], A.add)
+    ts(f[2], k[5], 32.0, A.mult, f[1], A.add)
+    tt(f[3], f[2], k[1], A.add)
+    ts(v("LI"), J("li", 0, 16), f[3], A.add)
+    ts(ID, v("ROWI", 0, 128), pf, A.is_equal)
+    ts(DG, v("CIO"), paf, A.is_equal)
+    ts(v("XL"), B8, 1.0, A.mult)
+    for t in range(ST + 1):
+        ms(v("W%d" % t, 256, 296), -BIG)
+        ms(v("R%d" % t, 0 if t == 0 else NL, 298, SG), -1.0)
     ms(v("X", 4096, NX), 0.0)
-    ms(v("ZERO"), 0.0)
-    ms(v("XB", 0, 8), 0.0)
-    ms(v("ONES"), 1.0)
 
-    def turn(raw, w0, w1):
-        for b in range(8):
-            tp(v("TA", b, 256, 8), v(raw, b, 256, 8))
-            tp(v("TB", b, 256, 8), v("RU", b, 256, 8))
-        ts(v("TC", 0, 128), v("TA", 0, 128), ev, A.mult)
-        ts(v("TC", 128, 256), v("TB", 0, 128), ev, A.mult)
-        ts(v("TE", 0, 128), v("TB", 128, 256), od, A.mult)
-        ts(v("TE", 128, 256), v("TA", 128, 256), od, A.mult)
-        tt(w0, v("TC", 0, 128), v("TE", 0, 128), A.add)
-        tt(w1, v("TC", 128, 256), v("TE", 128, 256), A.add)
+    def late_constants():
+        for nm, w in (("IDN", -1.0), ("I22", 2.0 ** 22), ("N22", -2.0 ** 22), ("I21", 2.0 ** 21), ("IDH", 0.5),
+                      ("IDF", 1.0)):
+            act(v(nm), ID, AF.Copy, scale=w)
+        for i, w in enumerate((8192.0, -4096.0, 4096.0)):
+            ts(v("BW", 8 * i, 8 * i + 8), B8, pgf, A.is_equal, w, A.mult)
+        for i, w in enumerate((-128.0, -8.0, 1.0)):
+            ts(v("CV", 8 * i, 8 * i + 8), B8, pgf, A.is_equal, w, A.mult)
+        ts(v("CVH"), B8, pgf, A.is_equal)
+        ms(v("ONES"), 1.0)
+        ms(v("ONF"), 1.0)
+        ms(v("RS", 0, NL, SG), -2.0 ** 25)
+        ms(v("RZ"), 1.0)
+        ms(v("RZ", 0, 256, 16), 0.0)
+        ms(v("P32", 0, NL, SG), 2048.0)
+        for nm in ("Q", "A1", "B1", "TDR", "DM"):
+            ms(v(nm, 0, NL, SG), 0.0)
+        ts(S("cj", 0, 8), S("cj", 0, 8), paf, A.add)
+        ts(v("XF"), B8, float(SG), A.mult, float(SG - 1), A.add)
+        ts(v("BR"), v("SEGI"), pgf, A.is_equal, -2048.0, A.mult)
+        ts(v("TRI"), v("CIO"), paf, A.is_ge, 8192.0, A.mult)
+        ts(v("BO"), v("ROWI", 0, 128), 1.0 / 16, A.mult, -0.46875, A.add)
+        ts(v("BLK"), v("BO"), pgf, A.is_equal)
+        ts(dump, pa, 4096.0, A.add)
+        ts(dumpk, pa, 2048.0, A.add)
+        ts(dk4, pa, 6144.0, A.add)
+        ts(S("wt", 0, 1), v("WT"), 1.0, A.mult)
+        ts(S("wt", 1, 2), pg, 16.0, A.mult, 15.0, A.add)
+        ts(v("WBW"), v("ROWI", 0, 143), S("wt", 1, 2), A.is_equal, S("wt", 0, 1), A.mult)
+        ts(S("V00"), v("VI", 0, 8), dump, A.subtract)
+        ts(S("b8"), B8, -8.0, A.add)
+        bits(k[6], pi, 0, 31)
+        tc(q31, k[6])
+        ts(is8, pi, 8.0, A.is_equal)
+        ts(v("SEG"), v("SEGI", 0, NL, 1, 0, 64), S("cols", 6, 7, 1, 0, 64), A.is_equal, S("cols", 7, 8, 1, 0, 64), A.max)
+        ts(v("TH8", 1, 2, 1, 0, 32), v("TH8", 0, 1, 1, 0, 32), 992, A.bitwise_and)
+        ts(v("TH8", 1, 2, 1, 32, 64), v("TH8", 0, 1, 1, 32, 64), 31, A.bitwise_and)
+        ts(f[4], is8, 2.0 ** 21, A.mult)
+        ts(S("th", 0, 1, 1, 0, 64), v("TH8", 1, 2), -2048.0, A.mult, S("kf", 4, 5, 1, 0, 64), A.add)
+        ts(S("th", 1, 2), pi, 32.0, A.is_ge, -2048.0, A.mult)
+        ts(v("THX"), v("SEG"), S("th", 0, 1, 1, 0, 64), A.mult)
 
-    ts(v("OUT"), v("VR"), 4096.0, A.mult, float(-BIG), A.add)
-    tt(v("RT", 0, 128), v("OUT", 0, 256, 2), v("CR", 0, 256, 2), A.add)
-    tt(v("RT", 128, 256), v("OUT", 1, 256, 2), v("CR", 1, 256, 2), A.add)
-    tc(v("RU", 0, 128), v("RT", 128, 256))
-    tc(v("RU", 128, 256), v("RT", 0, 128))
-    turn("RT", v("W0", 0, 128), v("W0", 128, 256))
+    def last_constants():
+        bits(k[7], pi, 0, 1)
+        tt(k[8], k[7], k[0], A.not_equal)
+        bits(k[9], pi, 1, 7)
+        ts(f[5], k[8], 256.0, A.mult, f[0], A.add)
+        tt(f[6], f[5], k[9], A.add)
+        ts(v("LO"), J("lo", 0, 16), f[6], A.add)
+        tt(k[10], pg, k[2], A.add)
+        bits(k[11], k[10], 0, 7)
+        ts(f[7], k[11], float(SG), A.mult, float(SG - 1), A.add)
+        tt(f[8], f[7], k[1], A.subtract)
+        ts(v("LS"), v("ROWI", 0, 18), -2.0, A.mult, f[8], A.add)
+        tt(k[12], pg, k[2], A.subtract)
+        bits(k[13], k[12], 0, 7)
+        ts(f[9], k[1], 8.0, A.mult)
+        tt(f[10], f[9], k[13], A.add)
+        ts(v("LU"), v("ROWI", 0, 18), 16.0, A.mult, f[10], A.add)
+        act(v("C2", 0, 128), ID, AF.Copy)
+        act(v("C2", 128, 256), ID, AF.Copy)
+
+    ts(v("pA", 0, 256), v("VR"), 4096.0, A.mult, float(-BIG), A.add)
+    tt(v("RT", 0, 256), v("CR"), v("pA", 0, 256), A.add)
+    tc(v("RT", 256, 288), v("RT", 0, 32))
+    for s in range(2):
+        for w in range(2):
+            tp(v("TAB", s * 256 + w * 128, s * 256 + w * 128 + 128), v("RT", 32 * w + s, 32 * w + 256, 2))
+    tc(v("W0", 0, 256), ind(v("TAB"), v("LI")))
 
     def lists(t):
         P = 32 + t
         W = "W%d" % t
-        for r0, r1 in ((0, 9), (9, P)):
-            ts(v("VI", r0 * 8, r1 * 8), v(W, r0 * 8, r1 * 8), 12, A.arith_shift_right, 4095, A.bitwise_and)
+        for r0, r1 in ((0, VCUT[1]), (VCUT[1], P)):
+            bits(v("VI", r0 * 8, r1 * 8), v(W, r0 * 8, r1 * 8), 12, 4095)
             tc(v("VL", r0 * 8, r1 * 8), v("VI", r0 * 8, r1 * 8))
-        ts(v("CI", 0, P * 8 - 16), v(W, 0, P * 8 - 16), 4095, A.bitwise_and)
-        tc(v("CL", 0, P * 8 - 16), v("CI", 0, P * 8 - 16))
-
-    def late_constants():
-        ts(S("wt", 0), v("WT"), 1.0, A.mult)
-        ts(v("WBW"), v("WB1"), S("wt", 0), A.mult)
-        ts(v("CIO"), v("CIO"), 4, A.arith_shift_right)
-        ts(v("BLK"), v("CIO"), pgf, A.is_equal)
-        ts(v("DG"), v("ROWI", 15, 31), paf, A.is_equal, 128.0, A.mult)
-        ts(v("POS"), v("POS"), paf, A.add)
-        ts(S("BA"), S("BA"), paf, A.add)
-        ts(S("II"), S("B8"), pa8, A.add)
-        ts(S("DUMP"), S("II"), 4096.0, A.add)
-        ts(S("KF0"), S("II"), 1.0 / 128, A.mult)
-        tt(S("KF"), S("KF0"), S("DUMP"), A.add)
-        tt(S("V00"), v("VI", 0, 8), S("DUMP"), A.subtract)
-        ts(v("GB", 0, 128, 1, 0, 8), v("CIO", 0, 128, 1, 0, 8), v("SM", pf[1], pf[2], 1, 0, 8), A.is_equal)
-        thf = v("SM", scol["wt"] + 1, scol["wt"] + 2, 1, 0, 8)
-        tc(thf, v("THR8"))
-        mm(v("pS", 0, 1), v("GB", 0, 128, 1, 0, 8), thf, True, True)
-        tc(S("th", 0), v("pS", 0, 1))
-        tc(S("lim", 0), S("th", 0))
-
-    def scalar_constants():
-        act(S("THR"), S("II"), AF.Copy, bias=-0.5, scale=0.5)
-        act(S("HC"), S("II"), AF.Copy, bias=0.5, scale=0.5)
-        act(S("HI"), S("II"), AF.Copy, scale=0.5)
-        act(S("KD"), S("KF"), AF.Copy, scale=128.0)
-        for b in range(8):
-            act(v("EXC", b * 16, b * 16 + 16), v("DG"), AF.Copy, scale=S("KF", b))
-        tt(S("HK"), S("HC"), S("KD"), A.subtract)
+        for r0, r1 in ((0, 8), (8, P - 2)):
+            ts(v("CI", r0 * 8, r1 * 8), v(W, r0 * 8, r1 * 8), 4095, A.bitwise_and)
+            tc(v("CL", r0 * 8, r1 * 8), v("CI", r0 * 8, r1 * 8))
 
     def masks(t):
-        R, G8 = "R%d" % t, (30 + t) * 8
-        mm(v("pI", 0, G8), v("ID"), v(R, 8, G8 + 8), True, False)
-        mm(v("pI", 0, G8), v("IDN"), v(R, 0, G8), False, True)
-        act(S("b25"), S("n%d" % t), AF.Copy, bias=2.5, scale=-1.0)
+        R = "R%d" % t
+        lin(v("pR", 0, NL), (ID, v(R, 0, NL)), (IDN, v(R, 1, NL + 1)))
+        act(S("b25"), S("n%d" % t, 8, 16), AF.Copy, bias=-2.5 * 2 ** 25, scale=2.0 ** 25)
+        boost[0] = EARLY
+        act(v("NF"), v("pR", 0, NL), AF.Relu, bias=1.0, scale=-1.0)
         for b in range(8):
-            act(v("INV", b, G8, 8), v(R, b, G8, 8), AF.Sign, bias=S("b25", b))
-        act(v("MK", 0, G8), v("pI", 0, G8), AF.Relu, bias=1.0, scale=-1.0)
-
-    def dedupe(t2):
-        mm(v("pI", 0, 128), v("BLK"), v("EXC"), True, False)
-        for b in range(8):
-            act(v("EX", b * 16, b * 16 + 16), v("DG"), AF.Copy, scale=v("SM", t2[1] + b, t2[1] + b + 1))
-        mm(v("pI", 0, 128), v("BLK"), v("EX"), False, True)
-        ts(S("nc0"), t2, -128.0, A.mult)
-        tt(S("nc"), S("nc0"), S("HK"), A.add)
-
-    def far(b):
-        act(v("AA", b * 128, b * 128 + 128), v("pI", 0, 128), AF.Abs, bias=S("nc", b))
-
-    def hit(b):
-        x, o = v("AA", b * 128, b * 128 + 128), v("AB", b * 128, b * 128 + 128)
-        emit("a", lambda: g.scalar.activation(ap(o), ap(x), AF.Relu, bias=ap(S("HI", b)), scale=-1.0, accum_out=ap(S("hit", b))),
-             [o, S("hit", b)], [x, S("HI", b)], cost=0.126)
-
-    def half(nm, k):
-        c = S(nm)[1]
-        return v("SM", c + NV * k, c + (8 if k else NV))
-
-    def dedupe2(t2, off):
-        for b in range(NV):
-            tr(S("mn", b), v("AA", b * 128, b * 128 + 128), A.min)
-        tt(half("nd", 0), half("mn", 0), half("THR", 0), A.is_gt)
-        ts(half("nd", 1), half("hit", 1), 0.0, A.is_equal)
-        tt(S("t3"), t2, S("nd"), A.mult)
-        tt(S("t4"), S("t3"), S("DUMP"), A.add)
-        tc(v(off), S("t4"))
+            act(seg("RS", b), seg(R, b, -1), AF.Identity, bias=col(S("b25"), b), scale=-2.0 ** 25)
+        boost[0] = 0.0
 
     xwin = v("X")
 
+    def winners(key):
+        mm(v("pT", 128, 256), ID, v("TRI"), True, False)
+        tt(v("EXH"), ind(key, v("XL")), DG, A.mult)
+        act(v("EXR"), ind(key, v("XL")), AF.Copy)
+        mm(v("pT", 128, 256), v("BLK"), v("EXH"), False, True)
+        tt(v("EQ"), v("EXR"), v("pT", 128, 256), A.is_equal)
+        scan(v("EC"), v("RZ", 0, 128), v("EQ"), A.mult, A.max)
+        ts(S("bd"), v("EC", 15, 128, 16), dk4, A.mult, -4096.0, A.add)
+        tt(S("of"), S("bd"), key, A.max)
+        ts(v("OF", 0, 16, 2), S("of"), 2048.0, A.add)
+
+    def put(src):
+        for b in range(7, -1, -1):
+            tc(ind(xwin, v("OF", 2 * b, 2 * b + 1)), v(src, 16 * b, 16 * b + 16))
+
     def step(t):
         P = 32 + t
-        P1, G = P + 1, P - 2
-        n8, m8, G8 = P * 8, P1 * 8, G * 8
+        G = P - 2
+        n8, m8 = P * 8, P * 8 + 8
         W, R, Wn, Rn = "W%d" % t, "R%d" % t, "W%d" % (t + 1), "R%d" % (t + 1)
-        YR, M, LW, LY, LM = ["%s%d" % (k, t) for k in ("YR", "M", "LW", "LY", "LM")]
-        n, nn, V0, V0n, TH = S("n%d" % t), S("n%d" % (t + 1)), S("V0%d" % t), S("V0%d" % (t + 1)), S("lim", t)
+        YR, M, MV, LW, LY, LM, LV = ["%s%d" % (q, t) for q in ("YR", "M", "MV", "LW", "LY", "LM", "LV")]
+        n, nn, V0, V0n = S2("n%d" % t), S2("n%d" % (t + 1)), S("V0%d" % t), S("V0%d" % (t + 1))
         d = 1 + t % 5
         to, fr = T.cores[(rank + d) % N], T.cores[(rank - d) % N]
         ne = len(topo.engines(fr, core))
-        for buf, sem, wd in ((LW, "aw", m8), (LY, "ay", 128 + m8), (LM, "am", 24)):
+        for buf, sem, wd in ((LW, "aw", m8 + 8), (LY, "ay", 128 + NL), (LV, "av", 8), (LM, "am", 16)):
             record((sem + str(t), ne), [v(buf, 0, wd)], [], {})
 
-        c1, c2, c3 = GCS
-        gc = [(0, c1), (c1, c2), (c2, c3), (c3, G)]
-        vc = [(0, c1 + 1), (c1 + 1, c2 + 1), (c2 + 1, c3 + 1), (c3 + 1, P)]
+        def rows(nm, r0, r1):
+            return v(nm, r0 * 128, r1 * 128)
 
-        def gv(c):
-            r0, r1 = vc[c]
-            for r0, r1 in ([(0, 5), (5, r1)] if c == 0 else [(r0, r1)]):
-                act(v("XV", r0 * 128, r1 * 128), ind(v("X", 0, 4096), v("VL", r0 * 8, r1 * 8)), AF.Copy, scale=0.5)
-
-        def hs(c):
-            r0, r1 = gc[c]
-            return [(r, min(r + 4, r1)) for r in range(r0, r1, 4)]
-
-        hb = ("pA", "pB", "pJ")
-
-        def idp(c):
-            for k, (r0, r1) in enumerate(hs(c)):
-                mm(v(hb[k], 0, (r1 - r0) * 128), v("ID"), v("XV", r0 * 128, r1 * 128), True, r0 < HA)
-                if r0 >= HA:
-                    mm(v(hb[k], 0, (r1 - r0) * 128), v("ID"), v("XV", r0 * 128 + 128, r1 * 128 + 128), False, True)
-
-        def hh(c):
-            for k, (r0, r1) in enumerate(hs(c)):
-                if r0 >= HA:
-                    act(v("H", r0 * 128, r1 * 128), v(hb[k], 0, (r1 - r0) * 128), AF.Copy)
-                    continue
-                tt(v("H", r0 * 128, r1 * 128), v("XV", r0 * 128 + 128, r1 * 128 + 128), v(hb[k], 0, (r1 - r0) * 128), A.add)
-
-        def dd(c):
-            r0, r1 = gc[c]
-            tt(v("D", r0 * 128, r1 * 128), ind(v("X", 0, 4096), v("CL", r0 * 8, r1 * 8)), v("H", r0 * 128, r1 * 128), A.subtract)
-
-        def aba(c):
-            r0, r1 = gc[c]
-            act(v("AB", r0 * 128, r1 * 128), v("D", r0 * 128, r1 * 128), AF.Abs)
-
-        def sums(bank, wb, buf, r0, r1, last):
-            for a in range(16):
-                mm(v(bank, r0 * 8, r1 * 8), v(wb, 15 - a, 143 - a), v(buf, r0 * 128 + a, r1 * 128, 16), False, last and a == 15)
-
-        gv(0)
-        if t == 0:
-            masks(0)
-            late_constants()
-        ts(S("L"), n, 4.0, A.is_ge)
-        tt(S("nL"), n, S("L"), A.mult)
-        idp(0)
-        mm(v("pK", 0, G8), v("ID"), v("QT", 0, G8), True, False)
-        mm(v("pK", 0, G8), v("ID"), v(R, 0, G8), False, False)
-        mm(v("pK", 0, G8), v("IDH"), v("ONES", 0, G8), False, False)
-        mm(v("pK", 0, G8), v("IDH"), v("INV", 0, G8), False, False)
-        mm(v("pK", 0, G8), v("IDM"), v("MK", 0, G8), False, False)
-        mm(v("pD", 0, n8), v("ID"), v("ZERO", 0, n8), True, False)
-        gv(1)
-        gv(2)
-        hh(0)
-        dd(0)
-        idp(1)
-        sums("pD", "WBM", "XV", 0, c1 + 1, False)
-        hh(1)
-        idp(2)
-        sums("pD", "WBM", "XV", c1 + 1, c2 + 1, False)
-        aba(0)
-        sums("pK", "WBK", "AB", 0, c1, False)
-        gv(3)
-        dd(1)
-        hh(2)
-        idp(3)
-        sums("pD", "WBM", "XV", c2 + 1, c3 + 1, False)
-        aba(1)
-        sums("pK", "WBK", "AB", c1, c2, False)
-        dd(2)
-        hh(3)
-        aba(2)
-        sums("pK", "WBK", "AB", c2, c3, False)
-        dd(3)
-        aba(3)
-        sums("pK", "WBK", "AB", gc[3][0], G, True)
-        sums("pD", "WBM", "XV", c3 + 1, P, False)
-        tt(v("pJ", 8, m8), v(W, 0, n8), v(W, 8, m8), A.subtract)
-        if t:
-            cj = v("SI", 236, 237)
-            tc(cj, v("pS", 400, 401))
-            ts(cj, cj, 31, A.bitwise_and)
-            tt(TH, S("th", 0), cj, A.add)
-        ts(v("Z0", 0, G8), v("VI", 0, G8), 4096.0, A.mult, float(-BIG), A.add)
-        tt(v("Z", 0, G8), v("Z0", 0, G8), v("VI", 8, G8 + 8), A.add)
-        if t == 0:
-            scalar_constants()
-
+        vcut = [0] + list(VCUT) + [P]
+        tcut = [0] + list(TCUT) + [G]
+        banks = ("pA", "pB", "pC")
+        ts(S2("L64"), n, 4.0, A.is_ge, 64.0, A.mult)
+        act(S2("L"), S2("L64"), AF.Copy, scale=1.0 / 64)
+        tt(S2("thr"), n, S2("L64"), A.max)
+        tc(v(W, m8, m8 + 8), S("L"))
+        boost[0] = EARLY
+        send(W, LW, m8 + 8, "aw%d" % t, to)
+        boost[0] = 0.0
+        mm(v("pK", 0, NL), ID, v("QT"), True, False)
+        mm(v("pD", 0, NL), v("ONES", 0, 128, 1, 0, 64), v("THX"), True, False)
+        gv = gt = 0
+        for c, r0 in enumerate(range(0, G, 4)):
+            r1 = min(r0 + 4, G)
+            while vcut[gv] < r1 + 1:
+                act(rows("XV", vcut[gv], vcut[gv + 1]), ind(v("X", 0, 4096), v("VL", vcut[gv] * 8, vcut[gv + 1] * 8)), AF.Copy, scale=0.5)
+                after("gv")
+                gv += 1
+            while tcut[gt] < r1:
+                a0, a1 = tcut[gt], tcut[gt + 1]
+                tt(rows("T1", a0, a1), ind(v("X", 0, 4096), v("CL", a0 * 8, a1 * 8)), rows("XV", a0, a1), A.subtract)
+                after("gt")
+                gt += 1
+            way, bank = WAYS[c], v(banks[c % 3], 0, (r1 - r0) * 128)
+            nxt, own, ab = rows("XV", r0 + 1, r1 + 1), rows("T1", r0, r1), rows("AB", r0, r1)
+            if way == "Y":
+                lin(bank, (IDN, nxt), (ID, own))
+                act(ab, bank, AF.Abs)
+            elif way == "Z":
+                lin(bank, (ID, nxt))
+                tt(rows("D", r0, r1), own, bank, A.subtract)
+                act(ab, rows("D", r0, r1), AF.Abs)
+            else:
+                lin(bank, (ID, nxt))
+                tt(ab, own, bank, A.max)
+            for r in range(r0, r1):
+                if way == "X":
+                    mm(row("pK", r), rows("XV", r + 1, r + 2), v("BW", 8, 16))
+                    mm(row("pK", r), rows("T1", r, r + 1), v("BW", 8, 16))
+            for r in range(r0, r1):
+                mm(row("pK", r), rows("AB", r, r + 1), v("BW", 0, 8) if way == "X" else v("BW", 16, 24), False, r == G - 1)
+            if c == 2:
+                mm(v("pK", 0, NL), ID, v(R, 0, NL))
+                mm(v("pK", 1, NL), v("N22"), v("NF", 0, NL - 1))
+        while gv < len(vcut) - 1:
+            act(rows("XV", vcut[gv], vcut[gv + 1]), ind(v("X", 0, 4096), v("VL", vcut[gv] * 8, vcut[gv + 1] * 8)), AF.Copy, scale=0.5)
+            gv += 1
+        for r in range(2, P):
+            mm(row("pD", r), rows("XV", r, r + 1), v("BW", 8, 16))
+        tt(S("nL"), S("n%d" % t, 8, 16), S("L", 8, 16), A.mult)
+        act(S("bn"), S("nL"), AF.Copy, bias=0.5, scale=-1.0)
         for b in range(8):
-            tr(v("SI", J("mx")[1] + b, J("mx")[1] + b + 1), v("pK", b, G8, 8), A.max)
-        ts(J("q"), J("mx"), 8064, A.bitwise_and)
-        tt(S("jk"), S("BA"), J("q"), A.subtract)
-        tc(v("JL"), S("jk"))
-        tc(v("DK"), ind(v("D", 0, G * 128), v("JL")))
-        tt(v("TK"), ind(v("H", 0, G * 128), v("JL")), v("DK"), A.subtract)
+            act(seg("DM", b), seg(R, b), AF.Sign, bias=col(S("bn"), b))
+        mm(v("pD", 0, NL), v("I22"), v("NF"))
+        mm(v("pD", 0, NL), v("I21"), v("DM"))
+
+        mm(v("pT", 0, 16), v("IDF"), S2("cj"), True, False)
+        scan(v("KS"), v("RS"), v("pK", 0, NL), A.min, A.max)
+        bits(J("q"), row("KS", 0), 5, 63)
+        tt(v("EXB"), ind(J("q"), v("XL")), DG, A.mult)
+        mm(v("pT", 0, 16), v("EXB"), v("CV", 0, 16), False, True)
+        tc(v("JL"), v("pT", 0, 16))
+        jk, jw = v("JL", 0, 8), v("JL", 8, 16)
+        act(v("GA"), ind(v("XV", 128, G * 128 + 128), jk), AF.Copy, scale=2.0)
+        tt(v("GB"), ind(v("T1", 0, G * 128), jk), v("GA"), A.subtract)
+        tt(v("GC"), ind(v("XV", 0, G * 128), jk), v("GB"), A.subtract)
         Y = v(YR, 0, 128)
-        ts(Y, v("TK"), 0.0, A.max, 63.0, A.min)
-        for k in range(2):
-            ts(v("pY", k * 128, k * 128 + 128), Y, 0.5, A.mult)
-        ts(J("k"), J("mx"), 127, A.bitwise_and)
-        tc(S("k"), J("k"))
-        ts(S("bO"), J("mx"), -1.0 / 128, A.mult, 0.5, A.add)
-        act(S("nk"), S("k"), AF.Copy, bias=-1.0, scale=-1.0)
-        act(S("k15"), S("k"), AF.Copy, bias=1.5)
-        act(S("kn"), S("k"), AF.Copy, scale=-1.0)
-        act(v(M, 16, 24), S("L"), AF.Copy)
-        act(S("jb"), S("jk"), AF.Copy, bias=-0.5, scale=-1.0)
-        act(S("jb1"), S("jk"), AF.Copy, bias=-128.0, scale=-1.0)
+        ts(Y, v("GC"), 0.0, A.max, 63.0, A.min)
+        for q in range(2):
+            mm(v("pY", q * 128, q * 128 + 128), v("IDH"), Y, True, True)
+        ts(J("kk"), row("KS", 0), 31, A.bitwise_and)
+        ts(S("nk"), J("kk"), -1.0, A.mult)
+        act(S("jw"), v("pT", 8, 16), AF.Copy)
+        act(S("jb"), v("pT", 8, 16), AF.Copy, bias=-0.5, scale=-1.0)
+        act(S("jb1"), v("pT", 8, 16), AF.Copy, bias=-8.0, scale=-1.0)
         for b in range(8):
-            act(v(YR, 128 + b, 128 + m8, 8), v(R, b, m8, 8), AF.Relu, bias=S("nk", b))
-        send(W, LW, m8, "aw%d" % t, to)
-        send(YR, LY, 128 + m8, "ay%d" % t, to)
-        for b in range(8):
-            act(v("pA", b, n8, 8), v(R, b, n8, 8), AF.Relu, bias=S("k15", b), scale=-1.0)
-        for b in range(8):
-            act(v("RQ", b, n8, 8), v(R, b, n8, 8), AF.Relu, bias=S("nL", b), scale=-1.0)
-        for b in range(8):
-            act(v("pB", b, G8, 8), v("pK", b, G8, 8), AF.Sign, bias=S("bO", b), scale=1.0 / 128)
+            act(seg("Q", b), seg(R, b), AF.Relu, bias=col(S("nk"), b))
+        act(v("CM"), v("Q"), AF.Relu, bias=2.0, scale=-1.0)
+        RK = v(YR, 128, 128 + NL)
+        act(RK, v("Q"), AF.Relu, bias=-1.0)
+        send(YR, LY, 128 + NL, "ay%d" % t, to)
+        lin(v("pR", 0, NL), (ID, v("P32")), (ID, RK))
+        act(v("PL"), v("pR", 0, NL), AF.Copy)
+        act(v("S1"), v("Q"), AF.Sign)
 
+        mm(v("pD", 0, NL), Y, v("BR"))
+        for r in range(2, P, 2):
+            e = min(r + 2, P)
+            tt(rows("AB", r, e), rows("XV", r, e), v("pY", 0, (e - r) * 128), A.max)
+            for q in range(r, e):
+                mm(row("pD", q), rows("AB", q, q + 1), v("BW", 0, 8), False, q == P - 1)
+            if r == 16:
+                mm(v("pD", 0, NL), v("I22"), v("CM"))
         for a in range(16):
-            mm(v("pS", 304, 312), v("WB1", 15 - a, 143 - a), v(YR, a, 128, 16), a == 0, a == 15)
-        dc = [(2, 8), (8, 16), (16, 24), (24, P)]
-        for c, (r0, r1) in enumerate(dc):
-            for r in range(r0, r1, 2):
-                e = min(r + 2, r1)
-                tt(v("AB", r * 128, e * 128), v("XV", r * 128, e * 128), v("pY", 0, (e - r) * 128), A.max)
-            sums("pD", "WB4", "AB", r0, r1, c == 3)
-            if c == 1:
-                ts(S("lm"), v("pS", 304, 312), TH, A.add)
-                for b in range(8):
-                    act(v("LX", b, n8, 8), v("pA", b, n8, 8), AF.Identity, bias=S("lm", b), scale=-8192.0)
-                for b in range(8):
-                    act(v("SP", b, m8, 8), v("POS", b, m8, 8), AF.Sign, bias=S("jb", b))
-                for b in range(8):
-                    act(v("OA", b, m8, 8), v("POS", b, m8, 8), AF.Abs, bias=S("jb1", b))
-                act(v("OA", 0, m8), v("OA", 0, m8), AF.Relu, bias=1.0, scale=-1.0)
-                for b in range(8):
-                    act(v("A2", b, m8, 8), v(R, b, m8, 8), AF.Relu, bias=S("k", b), scale=-1.0)
-        for a in range(16):
-            mm(v("pI", 0, 8), v("WBW", 15 - a, 143 - a), v(YR, a, 128, 16), a == 0, a == 15)
-        mm(v("pY", 8, m8), v("ID"), v("ONES", 8, m8), True, False)
-        mm(v("pY", 8, m8), v("ID"), v(R, 0, n8), False, False)
-        mm(v("pY", 8, m8), v("IDN"), v(R, 8, m8), False, True)
-        tt(S("nk1"), n, S("nk"), A.add)
-        tt(v("PZ", 0, G8), v("pB", 0, G8), v("Z", 0, G8), A.mult)
+            mm(v("pK", 0, 8), v("WBW", 15 - a, 143 - a), v(YR, a, 128, 16), a == 0, a == 15)
+        for q in range(2):
+            tt(v("GV", 128 * q, 128 * q + 128), ind(v(W, 8 * q, n8), jw), DG, A.mult)
+        scan(v("SC"), v("RZ"), v("GV"), A.mult, A.add)
+        bits(J("vk", 0, 16), v("SC", 15, 256, 16), 12, 4095)
+        vk, vk1, wk = J("vk"), J("vk", 8, 16), v("SC", 15, 128, 16)
+        ts(v(MV), vk1, dump, A.subtract)
+        send(MV, LV, 8, "av%d" % t, to)
         for b in range(8):
-            tr(v("SI", J("z")[1] + b, J("z")[1] + b + 1), v("PZ", b, G8, 8), A.min)
-        ts(J("vk"), J("z"), 12, A.arith_shift_right, 4095, A.bitwise_and)
-        ts(J("vk1"), J("z"), 4095, A.bitwise_and)
-        tt(v(M, 8, 16), J("vk1"), S("DUMP"), A.subtract)
-        tt(v("pA", 0, n8), v("pD", 0, n8), v("LX", 0, n8), A.is_le)
-        tt(v("PZ", 0, n8), v("pA", 0, n8), v("RQ", 0, n8), A.mult)
+            act(v("SP", b, m8, 8), v("POS", b, m8, 8), AF.Sign, bias=col(S("jb"), b))
         for b in range(8):
-            tr(S("vm", b), v("PZ", b, n8, 8), A.max)
-        ts(S("cl"), S("vm"), 0.0, A.is_gt)
-        tt(S("sz0"), S("cl"), S("nk1"), A.mult)
-        tt(v(M, 0, 8), S("sz0"), S("vm"), A.subtract)
-        sz = v(M, 0, 8)
-        send(M, LM, 24, "am%d" % t, to)
-        tt(S("gr"), S("L"), S("cl"), A.subtract)
-        for b in range(8):
-            act(v("GG", b, m8, 8), v("SP", b, m8, 8), AF.Relu, scale=S("gr", b))
+            act(v("OA", b, m8, 8), v("POS", b, m8, 8), AF.Abs, bias=col(S("jb1"), b))
+        act(v("OA", 0, m8), v("OA", 0, m8), AF.Relu, bias=1.0, scale=-1.0)
+        scan(v("FS"), v("pD", 0, NL), v("PL"), A.min, A.max)
+        tt(v("EXH"), ind(v("FS"), v("XF")), DG, A.mult)
+        mm(v("pT", 0, 8), v("EXH"), v("CVH"), True, True)
+        tc(J("vm"), v("pT", 0, 8))
+        ts(v(M, 0, 8), J("vm"), 31, A.bitwise_and)
+        ts(v(M, 8, 16), row("FS", 0), 31, A.bitwise_and)
+        send(M, LM, 16, "am%d" % t, to)
+        sz = v(M)
+        ts(S2("cl"), sz, 1.0, A.min)
+        tt(S2("gr"), S2("L"), S2("cl"), A.subtract)
 
-        tc(J("u"), v("pI", 0, 8))
+        tc(J("u"), v("pK", 0, 8))
         ts(J("u2"), J("u"), 4095, A.bitwise_and)
         tt(J("uu"), J("u2"), J("u2"), A.mult)
-        ts(J("v37"), J("vk"), 37.0, A.mult)
+        ts(J("v37"), vk, 37.0, A.mult)
         ts(J("us"), J("uu"), 5, A.arith_shift_right)
         tt(J("h0"), J("us"), J("v37"), A.add)
         ts(J("h"), J("h0"), 4095, A.bitwise_and)
-        tt(S("hd"), J("h"), S("DUMP"), A.subtract)
-        tt(S("t2g"), S("hd"), S("gr"), A.mult)
-        dedupe(S("t2g"))
-        ts(S("wn0"), J("h"), 4096.0, A.mult, float(-BIG), A.add)
-        tt(S("wn1"), S("wn0"), J("vk"), A.add)
-        tt(S("wn"), S("wn1"), S("gr"), A.mult)
-        for b in range(8):
-            act(v("pD", b, m8, 8), v("OA", b, m8, 8), AF.Copy, scale=S("wn", b))
-        tt(v("XB", 8, m8), v("GG", 8, m8), v("pY", 8, m8), A.mult)
-        mm(v("pA", 0, m8), v("ID"), v(R, 0, m8), True, False)
-        mm(v("pA", 0, m8), v("ID"), v("XB", 0, m8), False, True)
-        tt(v("pB", 8, m8), v("GG", 8, m8), v("pJ", 8, m8), A.mult)
-        tt(v("WA", 8, m8), v(W, 8, m8), v("pB", 8, m8), A.add)
-        tc(v("WA", 0, 8), v(W, 0, 8))
-        tt(S("kns"), S("kn"), sz, A.subtract)
-        tt(S("zl"), J("z"), S("L"), A.mult)
-        act(v("YX", 0, 8), S("cl"), AF.Copy)
-        act(S("rest"), S("L"), AF.Copy, bias=1.0, scale=-1.0)
-        for b in range(8):
-            far(b)
-        for b in range(NV, 8):
-            hit(b)
-        for b in range(8):
-            act(v("A1", b, m8, 8), v("pA", b, m8, 8), AF.Relu, bias=S("kns", b))
-        tt(S("ng"), n, S("gr"), A.add)
-        ts(S("ng"), S("ng"), 32.0, A.min)
-        tt(S("n2"), S("ng"), sz, A.subtract)
-        dedupe2(S("t2g"), "OL")
-        tc(ind(xwin, v("OL")), Y)
-        mm(v("pA", 0, m8), v("ID"), v("A1", 0, m8), True, False)
-        mm(v("pA", 0, m8), v("IDN"), v("A2", 0, m8), False, True)
-        act(v("RQ", 0, m8), v("pA", 0, m8), AF.Abs)
-        act(v("RQ", 0, m8), v("RQ", 0, m8), AF.Relu, bias=1.0, scale=-1.0)
-        mm(v("pS", 0, m8), v("ID"), v(LY, 128, 128 + m8), True, False)
-        mm(v("pS", 0, m8), v("IDN"), v(R, 0, m8), False, True)
-        if t < ST - 1:
-            for b in range(8):
-                mm(v("pS", 400, 401), v("ONES", 0, 128), v("YX", b, b + 1), b == 0, b == 7)
+        ts(S("hd"), J("h"), dump, A.subtract)
+        tt(S("hg"), S("hd"), S("gr"), A.mult)
+        ts(S("kg"), S("hg"), dumpk, A.add)
+        winners(S("kg"))
+        put(YR)
 
-        tt(S("rc"), v(LM, 0, 8), S("rest"), A.mult)
-        tt(S("dv"), v(LM, 8, 16), V0, A.subtract)
-        tt(S("tk"), S("rc"), S("n2"), A.is_gt)
-        tt(nn, S("rc"), S("n2"), A.max)
+        ts(S("z0"), vk, 4096.0, A.mult, float(-BIG), A.add)
+        tt(S("z"), S("z0"), vk1, A.add)
+        ts(S("wn0"), J("h"), 4096.0, A.mult, float(-BIG), A.add)
+        tt(S("wn1"), vk, wk, A.subtract)
+        tt(S("wn2"), S("wn0"), S("wn1"), A.add)
+        tt(S("wn"), S("wn2"), S("gr"), A.mult)
+        tt(S("c1"), S("b8"), S("jw"), A.subtract)
+        act(S("rs"), S("L"), AF.Copy, bias=-1000.0, scale=1000.0)
+        tt(S("c2"), S("jw"), S("rs"), A.add)
+        bits(J("pm"), J("vm"), 2, 504)
+        tt(S("c3"), J("pm"), S("c1"), A.add)
+        tt(S("c4"), S("c3"), S("cl"), A.mult)
+        tt(S("pz"), S("c4"), S("c2"), A.add)
+        for b in range(8):
+            ts(v("ZM", b, m8, 8), v("POS", b, m8, 8), col(S("pz"), b), A.is_equal, col(S("z"), b), A.mult)
+        act(v("ZS", 0, m8), v("ZM", 0, m8), AF.Sign)
+        for b in range(8):
+            act(v("G1", b, m8, 8), v("SP", b, m8, 8), AF.Relu, scale=col(S("gr"), b))
+        lin(v("pB", 0, m8), (ID, v("G1", 0, m8)))
+        lin(v("pA", 0, m8), (ID, v("ONES", 0, m8)), (IDN, v("G1", 0, m8)), (ID, v("ZS", 0, m8)))
+        for b in range(8):
+            act(v("pC", b, m8, 8), v("OA", b, m8, 8), AF.Copy, scale=col(S("wn"), b))
+        tt(v("pB", 8, m8), v(W, 0, n8), v("pB", 8, m8), A.mult)
+        tt(v("ZM", 0, m8), v("ZM", 0, m8), v("pC", 0, m8), A.add)
+        tt(v("ZM", 8, m8), v("ZM", 8, m8), v("pB", 8, m8), A.add)
+        tt(v("pA", 0, m8), v(W, 0, m8), v("pA", 0, m8), A.mult)
+        tt(v("WA", 0, m8), v("ZM", 0, m8), v("pA", 0, m8), A.add)
+        tt(v("DW", 0, m8), v(LW, 0, m8), v("pA", 0, m8), A.subtract)
+        ts(S("nsz"), v(M, 8, 16), -1.0, A.mult)
+        act(S("g2"), S("gr", 8, 16), AF.Copy, bias=-2.0)
+        lin(v("pY", 0, NL), (ID, v("S1")), (ID, v("NF")))
+        lin(v("pD", 0, NL), (ID, v(LY, 128, 128 + NL)), (IDN, v(R, 0, NL)))
+        for b in range(8):
+            act(seg("A1", b), seg("Q", b), AF.Relu, bias=col(S("nsz"), b))
+        for b in range(8):
+            act(seg("B1", b), seg("pY", b), AF.Relu, bias=col(S("g2"), b))
+        for l, r in ((ID, v(R, 0, NL)), (IDN, v("Q")), (ID, v("A1")), (ID, v("B1"))):
+            mm(v("pR", 0, NL), l, r, r[0] == R, False)
+        tt(S2("ng"), n, S2("gr"), A.add)
+        ts(S2("ng"), S2("ng"), 32.0, A.min)
+        tt(S2("n2"), S2("ng"), sz, A.subtract)
+        if t < ST - 1:
+            act(S("clc"), S("cl", 8, 16), AF.Copy, acc_out=S("cs", 0, 1))
+            mm(v("pC", 400, 401, 1, 0, 64), v("ONF", 0, 64), S("cs", 0, 1), True, True)
+            cj = J("c", 0, 1, 0, 64)
+            tc(cj, v("pC", 400, 401, 1, 0, 64))
+            ts(cj, cj, 31, A.bitwise_and)
+            ts(S("th", 2, 3, 1, 0, 64), cj, S("th", 1, 2, 1, 0, 64), A.mult, S("th", 0, 1, 1, 0, 64), A.add)
+            ts(v("THX"), v("SEG"), S("th", 2, 3, 1, 0, 64), A.mult)
+
+        act(v("pK", 320, 448), v(LY, 0, 128), AF.Copy, bias=-0.25, scale=0.5)
+        tt(S("has"), S("n%d" % t), v(LW, m8, m8 + 8), A.min)
+        tt(S("hv"), S("has"), V0, A.mult)
+        tt(S("dl"), v(LV), S("hv"), A.subtract)
+        ts(S("base"), S("hv"), dumpk, A.add)
+        tt(S("dv"), v(LV), V0, A.subtract)
+        tt(S2("tk"), v(LM), S2("thr"), A.is_gt)
+        tt(S("kd"), S("tk"), S("dl"), A.mult)
+        tt(S("kb"), S("kd"), S("base"), A.add)
+        ts(v("OG"), S("kb"), 2048.0, A.add)
+        winners(S("kb"))
+        act(v("GX"), ind(xwin, v("OG")), AF.Copy, scale=0.5)
+        for b in range(8):
+            act(v("pK", b, m8, 8), v("DW", b, m8, 8), AF.Copy, scale=col(S("tk"), b))
+        tt(v("BO"), v("GX"), v("pK", 320, 448), A.add)
+        tt(v(Wn, 0, m8), v("WA", 0, m8), v("pK", 0, m8), A.add)
+        put("BO")
+        tt(S2("rc"), v(LM), S2("tk"), A.mult)
+        tt(nn, S2("rc"), S2("n2"), A.max)
         tt(S("dvt"), S("dv"), S("tk"), A.mult)
-        tt(S("has"), nn, v(LM, 16, 24), A.min)
         tt(V0n, V0, S("dvt"), A.add)
-        tt(S("t2b"), V0n, S("has"), A.mult)
-        dedupe(S("t2b"))
         for b in range(8):
-            act(v("T1", b, m8, 8), v("RQ", b, m8, 8), AF.Copy, scale=S("zl", b))
-        for b in range(8):
-            act(v("RX", b, m8, 8), v("pA", b, m8, 8), AF.Identity, bias=S("k", b))
-        for b in range(8):
-            ts(v("pK", b, m8, 8), v(LW, b, m8, 8), S("tk", b), A.mult)
-        tt(v("TM", 0, m8), v("T1", 0, m8), v("pD", 0, m8), A.add)
-        tt(v("TM", 0, m8), v("TM", 0, m8), v("pK", 0, m8), A.add)
-        ts(v("pY", 0, m8), v("TM", 0, m8), 0.0, A.is_equal)
-        tt(v("pB", 0, m8), v("WA", 0, m8), v("pY", 0, m8), A.mult)
-        tt(v(Wn, 0, m8), v("TM", 0, m8), v("pB", 0, m8), A.add)
-        for b in range(8):
-            far(b)
-        for b in range(NV, 8):
-            hit(b)
-        for b in range(8):
-            act(v("TDR", b, m8, 8), v("pS", b, m8, 8), AF.Copy, scale=S("tk", b))
-        mm(v("pJ", 0, m8), v("ID"), v("RX", 0, m8), True, False)
-        mm(v("pJ", 0, m8), v("ID"), v("TDR", 0, m8), False, True)
-        act(v(Rn, 0, m8), v("pJ", 0, m8), AF.Copy)
-        dedupe2(S("t2b"), "OB")
-        tt(v("BS"), ind(xwin, v("OB")), v(LY, 0, 128), A.add)
+            act(seg("TDR", b), seg("pD", b), AF.Copy, scale=col(S("tk", 8, 16), b))
+        mm(v("pR", 0, NL), ID, v("TDR"), False, True)
+        act(v(Rn, 0, NL), v("pR", 0, NL), AF.Copy)
         if t < ST - 1:
             masks(t + 1)
-        else:
-            mm(v("pA", 0, 280), v("ID"), v(Rn, 8, 288), True, False)
-            mm(v("pA", 0, 280), v("IDN"), v(Rn, 0, 280), False, True)
-            mm(v("pY", 0, 288), v("ID"), v("PP"), True, False)
-            mm(v("pY", 0, 288), v("IDN"), v(Rn), False, True)
-            act(S("n5"), nn, AF.Copy, bias=-0.5)
-            for b in range(8):
-                act(v("SP", b, 288, 8), v(Rn, b, 288, 8), AF.Sign, bias=S("n5", b), scale=-1.0)
-            act(v("pB", 0, 288), v("SP"), AF.Relu)
-            act(v("T1", 0, 280), v("pA", 0, 280), AF.Sign)
-        ts(v("BO"), v("BS"), 0.5, A.mult, -0.25, A.add)
-        tc(ind(xwin, v("OB")), v("BO"))
-        if t < ST - 1:
             lists(t + 1)
 
     lists(0)
-    tc(S("n0"), v("NR"))
+    late_constants()
+    tc(v("NB", 0, 128, 1, 0, 8), v("NR"))
+    mm(v("pT", 8, 16), v("NB", 0, 128, 1, 0, 8), v("ID", 0, 8, 1, 0, 8), True, True)
+    tc(S("n0", 8, 16), v("pT", 8, 16))
+    tc(S("nl"), v("pT", 8, 16))
+    tt(v("EXB"), ind(S("nl"), v("XL")), DG, A.mult)
+    mm(v("pT", 0, 8), v("EXB"), v("CV", 16, 24), True, True)
+    tc(S("n0"), v("pT", 0, 8))
+    masks(0)
     for t in range(ST):
+        if t == ST - 1:
+            last_constants()
         step(t)
 
+    act(v("NB", 0, 8), S("n4", 8, 16), AF.Copy)
+    mm(v("pC", 0, 128, 1, 0, 8), v("NB", 0, 8), ID, True, True)
+    act(v("NO"), v("pC", 0, 128, 1, 0, 8), AF.Copy)
     so = [dma("s", T.yx[:, 0:2048], ap(v("X", 0, 2048)), [], [v("X", 0, 2048)]),
           dma("a", T.yx[:, 2048:4096], ap(v("X", 2048, 4096)), [], [v("X", 2048, 4096)]),
-          dma("s", T.yn[:], ap(S("n4")), [], [S("n4")])]
-    ms(v("T1", 280, 288), 1.0)
-    ts(v("U"), v("W4"), float(BIG), A.add)
-    tt(v("E"), v("T1"), v("pB", 0, 288), A.mult)
-    tt(v("DLT"), v("E"), v("pY", 0, 288), A.mult)
-    tt(v("U"), v("U"), v("E"), A.mult)
+          dma("s", T.yn[:], ap(v("NO")), [], [v("NO")])]
+    act(v("SK"), ind(v("R4", 0, NL), v("LS")), AF.Copy)
+    for e in range(8):
+        mm(v("pD", e, 288, 8), v("C2", 128 - 16 * e, 256 - 16 * e), v("SK", e, 288, 8), True, True)
+    act(v("SO"), v("pD", 0, 288), AF.Copy)
+    act(v("RT4"), ind(v("SO"), v("LU")), AF.Copy)
+    lin(v("pK", 0, 280), (ID, v("RT4", 8, 288)), (IDN, v("RT4", 0, 280)))
+    lin(v("pK", 280, 288), (ID, v("ONES", 0, 8)))
+    lin(v("pY", 0, 288), (ID, v("PP")), (IDN, v("RT4")))
+    act(S("n5"), S("n4"), AF.Copy, bias=-0.5)
+    for b in range(8):
+        act(v("NM", b, 256, 8), v("PP", b, 256, 8), AF.Sign, bias=col(S("n5"), b), scale=-1.0)
+    act(v("NM"), v("NM"), AF.Relu)
+    ts(v("U"), v("W4", 0, 288), float(BIG), A.add)
+    tc(v("DLT"), v("pY", 0, 288))
+    tt(v("pA", 0, 288), v("U"), v("pK", 0, 288), A.mult)
     for i in range(6):
         lo = 8 << i
         w = 288 - lo
-        ts(v("BIT", lo, 288), v("DLT", lo, 288), i, A.arith_shift_right, 1, A.bitwise_and)
-        tc(v("pA", lo, 288), v("BIT", lo, 288))
-        tt(v("pB", lo, 288), v("U", lo, 288), v("pA", lo, 288), A.mult)
-        if i < 5:
-            tt(v("pK", lo, 288), v("DLT", lo, 288), v("pA", lo, 288), A.mult)
-        tt(v("U", lo, 288), v("U", lo, 288), v("pB", lo, 288), A.subtract)
-        if i < 5:
-            tt(v("DLT", lo, 288), v("DLT", lo, 288), v("pK", lo, 288), A.subtract)
-        tt(v("U", 0, w), v("U", 0, w), v("pB", lo, 288), A.add)
-        if i < 5:
-            tt(v("DLT", 0, w), v("DLT", 0, w), v("pK", lo, 288), A.add)
-    tc(v("RU", 0, 128), v("U", 128, 256))
-    tc(v("RU", 128, 256), v("U", 0, 128))
-    turn("U", v("OI", 0, 256, 2), v("OI", 1, 256, 2))
+        bit = v("BIT" if i % 2 else "CI", lo, 288)
+        bits(bit, v("DLT", lo, 288), i, 1)
+        tt(v("U", lo, 288), bit, v("pA", lo, 288), A.mult)
+        tt(v("pA", lo, 288), v("pA", lo, 288), v("U", lo, 288), A.subtract)
+        tt(v("pA", 0, w), v("pA", 0, w), v("U", lo, 288), A.add)
+    tt(v("UF", 0, 256), v("NM"), v("pA", 0, 256), A.mult)
+    tt(v("UF", 256, 384), v("NM", 0, 128), v("pA", 0, 128), A.mult)
+    for w in range(2):
+        for b in range(8):
+            tp(v("TAB", w * 256 + b * 32, w * 256 + b * 32 + 32), v("UF", 128 * w + b, 128 * w + 256, 8))
+    tc(v("OI"), ind(v("TAB"), v("LO")))
     ts(v("VI", 0, 256), v("OI"), 12, A.arith_shift_right)
     tc(v("OV"), v("VI", 0, 256))
     so.append(dma("s", T.yv[:], ap(v("OV")), [], [v("OV")]))

@@ -11,12 +11,25 @@ NX = 4112
 SG = 37
 NL = 8 * SG
 SLACK = 0.03
+WAIT = 10.0
 LAT = 0.06
 FLY = 2.5
 EARLY = 8.0
-WAYS = "XZXZXYYYY"
-VCUT = (5, 9, 17, 25)
-TCUT = (4, 8, 16, 24, 28)
+PASSES = 6
+ORDER = []
+SH = 10
+GS = False
+UB = 1.0
+HB = 1.0
+YB = 0.0
+VOWN = ()
+WAYS = "XYZZYZYYZ"
+SIZES = (3, 4, 4, 4, 4, 4, 4, 4, 1)
+GROW = 0
+MASKAT = 0
+VCUT = (1, 2, 3, 5, 7)
+TCUT = (1, 2, 3, 5, 7, 8)
+LCUT = 12
 
 SCRATCH = {}
 TILES = {}
@@ -57,13 +70,12 @@ _add("sbuf", "float32", "MV0 MV1 MV2 MV3 LV0 LV1 LV2 LV3", 8)
 _add("sbuf", "float32", "SM", 1600)
 _add("sbuf", "int32", "SI", 480)
 _add("sbuf", "float32", "ROWI", 256)
-_add("sbuf", "bfloat16", "WBW", 143)
 _add("sbuf", "bfloat16", "C2 RZ", 256)
-_add("sbuf", "bfloat16", "ID IDN I22 N22 I21 IDH DG TRI EXB GA GB GC EQ EC GX NB", 128)
+_add("sbuf", "bfloat16", "ID IDN I22 N22 I21 IDH IDM DG TRI EXB GA GB GC EQ GX NB", 128)
 _add("sbuf", "float16", "BLK EXH", 128)
 _add("sbuf", "float16", "CVH", 8)
-_add("sbuf", "bfloat16", "BW CV", 24)
-_add("sbuf", "float32", "IDF EXR ONF", 128)
+_add("sbuf", "bfloat16", "BW CV", 32)
+_add("sbuf", "float32", "IDF EXR ONF EXF BLF EC RD", 128)
 _add("sbuf", "float32", "GV", 256)
 _add("sbuf", "int32", "SC VR CR OI", 256)
 _add("sbuf", "int32", "BO CIO", 128)
@@ -122,7 +134,7 @@ def rank_program(g, core, T, topo):
 
     def after(name):
         if name in chains:
-            ops[-1][9].setdefault(chains[name], 0.0)
+            ops[-1][9].setdefault(chains[name], -ops[chains[name]][8])
         chains[name] = len(ops) - 1
 
     def emit(eng, call, writes, reads, tok=None, inc=1, note=True, cost=0.1, tail=0.0):
@@ -165,47 +177,67 @@ def rank_program(g, core, T, topo):
         ops.append((eng, call, writes, reads, tok, inc, note, cost, tail, deps))
 
     def flush():
-        n = len(ops)
-        succ = [[] for _ in range(n)]
-        for i, o in enumerate(ops):
-            for d in o[9]:
-                succ[d].append((i, o[9][d]))
-        pri = [0.0] * n
-        for i in range(n - 1, -1, -1):
-            o = ops[i]
-            pri[i] = o[7] + o[8] + max([l + pri[s] for s, l in succ[i]] + [0.0]) + extra.get(i, 0.0)
-        left = [len(o[9]) for o in ops]
-        ready = {e: [] for e in list(Q) + ["x"]}
-        avail = [0.0] * n
-        for i in range(n):
-            if not left[i]:
-                ready[ops[i][0]].append(i)
-        free = {e: 0.0 for e in ready}
-        order, done = [], 0
-        while done < n:
-            best = None
-            for e in ready:
-                if ready[e]:
-                    t0 = max(free[e], min(avail[i] for i in ready[e]))
-                    if best is None or t0 < best[0]:
-                        best = (t0, e)
-            t0, e = best
-            i = max((i for i in ready[e] if avail[i] <= t0 + SLACK), key=lambda i: (pri[i], -i))
-            ready[e].remove(i)
-            st = max(t0, avail[i])
-            fin = st + ops[i][7]
-            if e != "x":
-                free[e] = fin
-            order.append((st, i))
-            done += 1
-            for s, l in succ[i]:
-                avail[s] = max(avail[s], fin + ops[i][8] + l)
-                left[s] -= 1
-                if not left[s]:
-                    ready[ops[s][0]].append(s)
-        for st, i in order:
+        if not ORDER:
+            ORDER.extend(arrange())
+        for i in ORDER:
             if ops[i][0] != "x":
                 issue(*ops[i][:7])
+
+    def arrange():
+        n = len(ops)
+        succ, pred = [[] for _ in range(n)], [[] for _ in range(n)]
+        for i, o in enumerate(ops):
+            for d in o[9]:
+                succ[d].append((i, o[9][d] + ops[d][8]))
+                pred[i].append((d, o[9][d] + ops[d][8]))
+
+        def run(nxt, prv, pri, avail):
+            left = [len(x) for x in prv]
+            ready = {e: [] for e in list(Q) + ["x"]}
+            for i in range(n):
+                if not left[i]:
+                    ready[ops[i][0]].append(i)
+            free = {e: 0.0 for e in ready}
+            order, end = [], [0.0] * n
+            while len(order) < n:
+                best = None
+                for e in ready:
+                    if ready[e]:
+                        t0 = max(free[e], min(avail[i] for i in ready[e]))
+                        if best is None or t0 < best[0]:
+                            best = (t0, e)
+                t0, e = best
+                now = [i for i in ready[e] if avail[i] <= t0 + SLACK]
+                i = max(now, key=lambda i: (pri[i], -i))
+                j = max((j for j in ready[e] if avail[j] <= t0 + ops[i][7]), key=lambda j: (pri[j] - avail[j], -j), default=i)
+                gap = avail[j] - t0
+                if gap > SLACK and max(gap + pri[j], gap + ops[j][7] + pri[i]) + WAIT < max(pri[i], ops[i][7] + pri[j]):
+                    fits = [k for k in now if ops[k][7] <= gap + SLACK]
+                    i = max(fits, key=lambda k: (pri[k], -k)) if fits else j
+                ready[e].remove(i)
+                end[i] = max(t0, avail[i]) + ops[i][7]
+                if e != "x":
+                    free[e] = end[i]
+                order.append(i)
+                for s, l in nxt[i]:
+                    avail[s] = max(avail[s], end[i] + l)
+                    left[s] -= 1
+                    if not left[s]:
+                        ready[ops[s][0]].append(s)
+            return order, end
+
+        pri = [0.0] * n
+        for i in range(n - 1, -1, -1):
+            pri[i] = ops[i][7] + max([l + pri[s] for s, l in succ[i]] + [ops[i][8]]) + extra.get(i, 0.0)
+        best = None
+        for _ in range(PASSES):
+            order, end = run(succ, pred, pri, [0.0] * n)
+            span = max(end[i] + ops[i][8] for i in range(n))
+            if best is None or span < best[0]:
+                best = (span, order)
+            pri = run(pred, succ, end, [o[8] for o in ops])[1]
+            pri = [pri[i] + extra.get(i, 0.0) for i in range(n)]
+        return best[1]
 
     def issue(eng, call, writes, reads, tok=None, inc=1, note=True):
         ws, rs = [], []
@@ -338,7 +370,8 @@ def rank_program(g, core, T, topo):
         s = "d%d" % nd[0]
         nd[0] += 1
         emit(eng, lambda: Q[eng].dma_start(out, in_), writes, reads, tok=(s, 16), inc=16, cost=0.05,
-             tail=2.0 + sum(width(w) for w in writes + reads) * 128 * 2 / 100e3)
+             tail=2.0 + sum(width(w) for w in writes + reads) * 128 * 2 / (200e3 if writes else 100e3))
+        after("dma" + eng)
         return s
 
     scol, jcol = {}, {}
@@ -376,6 +409,7 @@ def rank_program(g, core, T, topo):
 
     ID, IDN, DG = v("ID"), v("IDN"), v("DG")
 
+    boost[0] = 100.0
     ms(v("TH8"), 0)
     dma("s", ap(v("VR")), T.vl[:], [v("VR")], [])
     dma("a", ap(v("CR")), T.cl[:], [v("CR")], [])
@@ -385,6 +419,7 @@ def rank_program(g, core, T, topo):
     dma("a", ap(v("WT")), T.wt[:], [v("WT")], [])
     for p0, e in ((0, "s"), (32, "a")):
         dma(e, ap(v("TH8", 0, 1, 1, p0, p0 + 8)), T.th[:], [v("TH8", 0, 4, 1, p0, p0 + 8)], [])
+    boost[0] = 0.0
 
     pi, pg, pa = J("pi", 0, 1), J("pi", 1, 2), J("pi", 2, 3)
     iota(pi, [[1, 1]], 0, 1)
@@ -432,7 +467,7 @@ def rank_program(g, core, T, topo):
 
     def late_constants():
         for nm, w in (("IDN", -1.0), ("I22", 2.0 ** 22), ("N22", -2.0 ** 22), ("I21", 2.0 ** 21), ("IDH", 0.5),
-                      ("IDF", 1.0)):
+                      ("IDM", -0.5), ("IDF", 1.0)):
             act(v(nm), ID, AF.Copy, scale=w)
         for i, w in enumerate((8192.0, -4096.0, 4096.0)):
             ts(v("BW", 8 * i, 8 * i + 8), B8, pgf, A.is_equal, w, A.mult)
@@ -455,10 +490,14 @@ def rank_program(g, core, T, topo):
         ts(v("BLK"), v("BO"), pgf, A.is_equal)
         ts(dump, pa, 4096.0, A.add)
         ts(dumpk, pa, 2048.0, A.add)
-        ts(dk4, pa, 6144.0, A.add)
+        tc(v("RD"), v("RZ", 0, 128))
+        ts(v("RD", 15, 128, 16), v("RZ", 15, 128, 16), dump, A.mult)
         ts(S("wt", 0, 1), v("WT"), 1.0, A.mult)
-        ts(S("wt", 1, 2), pg, 16.0, A.mult, 15.0, A.add)
-        ts(v("WBW"), v("ROWI", 0, 143), S("wt", 1, 2), A.is_equal, S("wt", 0, 1), A.mult)
+        ts(v("BW", 24, 32), B8, pgf, A.is_equal, S("wt", 0, 1), A.mult)
+        ts(S("cvf"), B8, pgf, A.is_equal)
+        ts(v("BLF"), v("BO"), pgf, A.is_equal)
+        for p in range(2, SH):
+            ms(row("BR", p), 0.0)
         ts(S("V00"), v("VI", 0, 8), dump, A.subtract)
         ts(S("b8"), B8, -8.0, A.add)
         bits(k[6], pi, 0, 31)
@@ -503,10 +542,10 @@ def rank_program(g, core, T, topo):
     def lists(t):
         P = 32 + t
         W = "W%d" % t
-        for r0, r1 in ((0, VCUT[1]), (VCUT[1], P)):
+        for r0, r1 in ((0, LCUT), (LCUT, P)):
             bits(v("VI", r0 * 8, r1 * 8), v(W, r0 * 8, r1 * 8), 12, 4095)
             tc(v("VL", r0 * 8, r1 * 8), v("VI", r0 * 8, r1 * 8))
-        for r0, r1 in ((0, 8), (8, P - 2)):
+        for r0, r1 in ((0, LCUT), (LCUT, P - 2)):
             ts(v("CI", r0 * 8, r1 * 8), v(W, r0 * 8, r1 * 8), 4095, A.bitwise_and)
             tc(v("CL", r0 * 8, r1 * 8), v("CI", r0 * 8, r1 * 8))
 
@@ -522,16 +561,21 @@ def rank_program(g, core, T, topo):
 
     xwin = v("X")
 
-    def winners(key):
+    def winners(key, on_scalar):
         mm(v("pT", 128, 256), ID, v("TRI"), True, False)
-        tt(v("EXH"), ind(key, v("XL")), DG, A.mult)
+        if on_scalar:
+            for b in range(8):
+                act(v("EXF", 16 * b, 16 * b + 16), v("DG", 0, 16), AF.Copy, scale=col(key, b))
+            mm(v("pT", 128, 256), v("BLF"), v("EXF"), False, True)
+        else:
+            tt(v("EXH"), ind(key, v("XL")), DG, A.mult)
+            mm(v("pT", 128, 256), v("BLK"), v("EXH"), False, True)
         act(v("EXR"), ind(key, v("XL")), AF.Copy)
-        mm(v("pT", 128, 256), v("BLK"), v("EXH"), False, True)
         tt(v("EQ"), v("EXR"), v("pT", 128, 256), A.is_equal)
-        scan(v("EC"), v("RZ", 0, 128), v("EQ"), A.mult, A.max)
-        ts(S("bd"), v("EC", 15, 128, 16), dk4, A.mult, -4096.0, A.add)
-        tt(S("of"), S("bd"), key, A.max)
-        ts(v("OF", 0, 16, 2), S("of"), 2048.0, A.add)
+        act(S("bd"), key, AF.Copy, bias=2048.0)
+        scan(v("EC"), v("RD"), v("EQ"), A.mult, A.max)
+        tt(S("of"), v("EC", 15, 128, 16), S("bd"), A.max)
+        tc(v("OF", 0, 16, 2), S("of"))
 
     def put(src):
         for b in range(7, -1, -1):
@@ -553,31 +597,39 @@ def rank_program(g, core, T, topo):
         def rows(nm, r0, r1):
             return v(nm, r0 * 128, r1 * 128)
 
-        vcut = [0] + list(VCUT) + [P]
-        tcut = [0] + list(TCUT) + [G]
-        banks = ("pA", "pB", "pC")
+        size = list(SIZES)
+        size[-2] -= max(0, 32 - G)
+        size[GROW] += max(0, G - 32)
+        cut = [sum(size[:c]) for c in range(len(size) + 1)]
+        vcut = [0] + [cut[c] + 1 for c in VCUT] + [P]
+        tcut = [0] + [cut[c] for c in TCUT] + [G]
+        banks = ("pA", "pB", "pC", "pY")
+        boost[0] = EARLY
         ts(S2("L64"), n, 4.0, A.is_ge, 64.0, A.mult)
         act(S2("L"), S2("L64"), AF.Copy, scale=1.0 / 64)
-        tt(S2("thr"), n, S2("L64"), A.max)
         tc(v(W, m8, m8 + 8), S("L"))
-        boost[0] = EARLY
         send(W, LW, m8 + 8, "aw%d" % t, to)
         boost[0] = 0.0
+        tt(S2("thr"), n, S2("L64"), A.max)
         mm(v("pK", 0, NL), ID, v("QT"), True, False)
         mm(v("pD", 0, NL), v("ONES", 0, 128, 1, 0, 64), v("THX"), True, False)
         gv = gt = 0
-        for c, r0 in enumerate(range(0, G, 4)):
-            r1 = min(r0 + 4, G)
+        for c, (r0, r1) in enumerate(zip(cut, cut[1:])):
             while vcut[gv] < r1 + 1:
-                act(rows("XV", vcut[gv], vcut[gv + 1]), ind(v("X", 0, 4096), v("VL", vcut[gv] * 8, vcut[gv + 1] * 8)), AF.Copy, scale=0.5)
-                after("gv")
+                a0, a1 = vcut[gv], vcut[gv + 1]
+                if gv in VOWN:
+                    ts(rows("XV", a0, a1), ind(v("X", 0, 4096), v("VL", a0 * 8, a1 * 8)), 0.5, A.mult)
+                    after("gt")
+                else:
+                    act(rows("XV", a0, a1), ind(v("X", 0, 4096), v("VL", a0 * 8, a1 * 8)), AF.Copy, scale=0.5)
+                    after("gv")
                 gv += 1
             while tcut[gt] < r1:
                 a0, a1 = tcut[gt], tcut[gt + 1]
                 tt(rows("T1", a0, a1), ind(v("X", 0, 4096), v("CL", a0 * 8, a1 * 8)), rows("XV", a0, a1), A.subtract)
                 after("gt")
                 gt += 1
-            way, bank = WAYS[c], v(banks[c % 3], 0, (r1 - r0) * 128)
+            way, bank = WAYS[c], v(banks[c % 4], 0, (r1 - r0) * 128)
             nxt, own, ab = rows("XV", r0 + 1, r1 + 1), rows("T1", r0, r1), rows("AB", r0, r1)
             if way == "Y":
                 lin(bank, (IDN, nxt), (ID, own))
@@ -595,14 +647,16 @@ def rank_program(g, core, T, topo):
                     mm(row("pK", r), rows("T1", r, r + 1), v("BW", 8, 16))
             for r in range(r0, r1):
                 mm(row("pK", r), rows("AB", r, r + 1), v("BW", 0, 8) if way == "X" else v("BW", 16, 24), False, r == G - 1)
-            if c == 2:
+            if c == MASKAT:
                 mm(v("pK", 0, NL), ID, v(R, 0, NL))
                 mm(v("pK", 1, NL), v("N22"), v("NF", 0, NL - 1))
         while gv < len(vcut) - 1:
             act(rows("XV", vcut[gv], vcut[gv + 1]), ind(v("X", 0, 4096), v("VL", vcut[gv] * 8, vcut[gv + 1] * 8)), AF.Copy, scale=0.5)
             gv += 1
-        for r in range(2, P):
+        for r in range(SH, P):
             mm(row("pD", r), rows("XV", r, r + 1), v("BW", 8, 16))
+        for r in range(2, SH, 4):
+            mm(v(banks[(r - 2) // 4]), ID, rows("XV", r, r + 4), True, False)
         tt(S("nL"), S("n%d" % t, 8, 16), S("L", 8, 16), A.mult)
         act(S("bn"), S("nL"), AF.Copy, bias=0.5, scale=-1.0)
         for b in range(8):
@@ -622,13 +676,14 @@ def rank_program(g, core, T, topo):
         tt(v("GC"), ind(v("XV", 0, G * 128), jk), v("GB"), A.subtract)
         Y = v(YR, 0, 128)
         ts(Y, v("GC"), 0.0, A.max, 63.0, A.min)
+        boost[0] = YB
         for q in range(2):
             mm(v("pY", q * 128, q * 128 + 128), v("IDH"), Y, True, True)
+        boost[0] = 0.0
         ts(J("kk"), row("KS", 0), 31, A.bitwise_and)
         ts(S("nk"), J("kk"), -1.0, A.mult)
         act(S("jw"), v("pT", 8, 16), AF.Copy)
         act(S("jb"), v("pT", 8, 16), AF.Copy, bias=-0.5, scale=-1.0)
-        act(S("jb1"), v("pT", 8, 16), AF.Copy, bias=-8.0, scale=-1.0)
         for b in range(8):
             act(seg("Q", b), seg(R, b), AF.Relu, bias=col(S("nk"), b))
         act(v("CM"), v("Q"), AF.Relu, bias=2.0, scale=-1.0)
@@ -639,16 +694,30 @@ def rank_program(g, core, T, topo):
         act(v("PL"), v("pR", 0, NL), AF.Copy)
         act(v("S1"), v("Q"), AF.Sign)
 
+        boost[0] = UB
+        mm(v("pK", 0, 8), Y, v("BW", 24, 32), True, True)
+        act(S("ul"), v("pK", 0, 8), AF.Copy)
+        for b in range(8):
+            act(v("EXF", 16 * b, 16 * b + 16), v("DG", 0, 16), AF.Copy, scale=col(S("ul"), b))
+        mm(v("pK", 8, 16), v("EXF"), S("cvf"), True, True)
+        boost[0] = 0.0
         mm(v("pD", 0, NL), Y, v("BR"))
-        for r in range(2, P, 2):
+        mm(v("pD", 0, NL), v("I22"), v("CM"))
+        shared = list(range(2, SH, 4))
+        for c, r in enumerate(range(SH, P, 2)):
             e = min(r + 2, P)
             tt(rows("AB", r, e), rows("XV", r, e), v("pY", 0, (e - r) * 128), A.max)
+            if c % 3 == 0 and shared:
+                r0 = shared.pop(0)
+                bank = banks[(r0 - 2) // 4]
+                for q in range(4):
+                    mm(v(bank, 128 * q, 128 * q + 128), v("IDM"), Y, False, q == 3)
+                act(rows("AB", r0, r0 + 4), v(bank), AF.Abs)
+            if c % 3 == 2 and c // 3 < (SH - 2) // 4:
+                for q in range(2 + c // 3 * 4, 6 + c // 3 * 4):
+                    mm(row("pD", q), rows("AB", q, q + 1), v("BW", 16, 24))
             for q in range(r, e):
                 mm(row("pD", q), rows("AB", q, q + 1), v("BW", 0, 8), False, q == P - 1)
-            if r == 16:
-                mm(v("pD", 0, NL), v("I22"), v("CM"))
-        for a in range(16):
-            mm(v("pK", 0, 8), v("WBW", 15 - a, 143 - a), v(YR, a, 128, 16), a == 0, a == 15)
         for q in range(2):
             tt(v("GV", 128 * q, 128 * q + 128), ind(v(W, 8 * q, n8), jw), DG, A.mult)
         scan(v("SC"), v("RZ"), v("GV"), A.mult, A.add)
@@ -658,9 +727,6 @@ def rank_program(g, core, T, topo):
         send(MV, LV, 8, "av%d" % t, to)
         for b in range(8):
             act(v("SP", b, m8, 8), v("POS", b, m8, 8), AF.Sign, bias=col(S("jb"), b))
-        for b in range(8):
-            act(v("OA", b, m8, 8), v("POS", b, m8, 8), AF.Abs, bias=col(S("jb1"), b))
-        act(v("OA", 0, m8), v("OA", 0, m8), AF.Relu, bias=1.0, scale=-1.0)
         scan(v("FS"), v("pD", 0, NL), v("PL"), A.min, A.max)
         tt(v("EXH"), ind(v("FS"), v("XF")), DG, A.mult)
         mm(v("pT", 0, 8), v("EXH"), v("CVH"), True, True)
@@ -672,7 +738,8 @@ def rank_program(g, core, T, topo):
         ts(S2("cl"), sz, 1.0, A.min)
         tt(S2("gr"), S2("L"), S2("cl"), A.subtract)
 
-        tc(J("u"), v("pK", 0, 8))
+        boost[0] = HB
+        tc(J("u"), v("pK", 8, 16))
         ts(J("u2"), J("u"), 4095, A.bitwise_and)
         tt(J("uu"), J("u2"), J("u2"), A.mult)
         ts(J("v37"), vk, 37.0, A.mult)
@@ -680,17 +747,17 @@ def rank_program(g, core, T, topo):
         tt(J("h0"), J("us"), J("v37"), A.add)
         ts(J("h"), J("h0"), 4095, A.bitwise_and)
         ts(S("hd"), J("h"), dump, A.subtract)
+        boost[0] = 0.0
         tt(S("hg"), S("hd"), S("gr"), A.mult)
-        ts(S("kg"), S("hg"), dumpk, A.add)
-        winners(S("kg"))
+        act(S("kg"), S("hg"), AF.Identity, bias=dumpk)
+        winners(S("kg"), GS)
         put(YR)
 
         ts(S("z0"), vk, 4096.0, A.mult, float(-BIG), A.add)
         tt(S("z"), S("z0"), vk1, A.add)
         ts(S("wn0"), J("h"), 4096.0, A.mult, float(-BIG), A.add)
         tt(S("wn1"), vk, wk, A.subtract)
-        tt(S("wn2"), S("wn0"), S("wn1"), A.add)
-        tt(S("wn"), S("wn2"), S("gr"), A.mult)
+        tt(S("wn"), S("wn0"), S("wn1"), A.add)
         tt(S("c1"), S("b8"), S("jw"), A.subtract)
         act(S("rs"), S("L"), AF.Copy, bias=-1000.0, scale=1000.0)
         tt(S("c2"), S("jw"), S("rs"), A.add)
@@ -699,16 +766,19 @@ def rank_program(g, core, T, topo):
         tt(S("c4"), S("c3"), S("cl"), A.mult)
         tt(S("pz"), S("c4"), S("c2"), A.add)
         for b in range(8):
-            ts(v("ZM", b, m8, 8), v("POS", b, m8, 8), col(S("pz"), b), A.is_equal, col(S("z"), b), A.mult)
-        act(v("ZS", 0, m8), v("ZM", 0, m8), AF.Sign)
+            act(v("OA", b, m8, 8), v("POS", b, m8, 8), AF.Abs, bias=col(S("pz"), b), scale=-1.0)
+        act(v("ZS", 0, m8), v("OA", 0, m8), AF.Relu, bias=1.0, scale=-1.0)
+        for b in range(8):
+            act(v("ZM", b, m8, 8), v("ZS", b, m8, 8), AF.Copy, scale=col(S("z"), b))
         for b in range(8):
             act(v("G1", b, m8, 8), v("SP", b, m8, 8), AF.Relu, scale=col(S("gr"), b))
         lin(v("pB", 0, m8), (ID, v("G1", 0, m8)))
-        lin(v("pA", 0, m8), (ID, v("ONES", 0, m8)), (IDN, v("G1", 0, m8)), (ID, v("ZS", 0, m8)))
+        lin(v("pC", 8, m8), (ID, v("G1", 8, m8)), (IDN, v("G1", 0, n8)))
+        lin(v("pA", 0, m8), (ID, v("ONES", 0, m8)), (IDN, v("G1", 0, m8)), (IDN, v("ZS", 0, m8)))
         for b in range(8):
-            act(v("pC", b, m8, 8), v("OA", b, m8, 8), AF.Copy, scale=col(S("wn"), b))
+            act(v("pC", 8 + b, m8, 8), v("pC", 8 + b, m8, 8), AF.Copy, scale=col(S("wn"), b))
         tt(v("pB", 8, m8), v(W, 0, n8), v("pB", 8, m8), A.mult)
-        tt(v("ZM", 0, m8), v("ZM", 0, m8), v("pC", 0, m8), A.add)
+        tt(v("ZM", 8, m8), v("ZM", 8, m8), v("pC", 8, m8), A.add)
         tt(v("ZM", 8, m8), v("ZM", 8, m8), v("pB", 8, m8), A.add)
         tt(v("pA", 0, m8), v(W, 0, m8), v("pA", 0, m8), A.mult)
         tt(v("WA", 0, m8), v("ZM", 0, m8), v("pA", 0, m8), A.add)
@@ -728,24 +798,26 @@ def rank_program(g, core, T, topo):
         tt(S2("n2"), S2("ng"), sz, A.subtract)
         if t < ST - 1:
             act(S("clc"), S("cl", 8, 16), AF.Copy, acc_out=S("cs", 0, 1))
-            mm(v("pC", 400, 401, 1, 0, 64), v("ONF", 0, 64), S("cs", 0, 1), True, True)
+            mm(v("pK", 16, 17, 1, 0, 64), v("ONF", 0, 64), S("cs", 0, 1), True, True)
             cj = J("c", 0, 1, 0, 64)
-            tc(cj, v("pC", 400, 401, 1, 0, 64))
+            tc(cj, v("pK", 16, 17, 1, 0, 64))
             ts(cj, cj, 31, A.bitwise_and)
             ts(S("th", 2, 3, 1, 0, 64), cj, S("th", 1, 2, 1, 0, 64), A.mult, S("th", 0, 1, 1, 0, 64), A.add)
-            ts(v("THX"), v("SEG"), S("th", 2, 3, 1, 0, 64), A.mult)
+            boost[0] = EARLY
+            act(v("THX"), v("SEG"), AF.Copy, scale=S("th", 2, 3, 1, 0, 64))
+            boost[0] = 0.0
 
         act(v("pK", 320, 448), v(LY, 0, 128), AF.Copy, bias=-0.25, scale=0.5)
         tt(S("has"), S("n%d" % t), v(LW, m8, m8 + 8), A.min)
         tt(S("hv"), S("has"), V0, A.mult)
         tt(S("dl"), v(LV), S("hv"), A.subtract)
-        ts(S("base"), S("hv"), dumpk, A.add)
+        act(S("base"), S("hv"), AF.Identity, bias=dumpk)
         tt(S("dv"), v(LV), V0, A.subtract)
         tt(S2("tk"), v(LM), S2("thr"), A.is_gt)
         tt(S("kd"), S("tk"), S("dl"), A.mult)
         tt(S("kb"), S("kd"), S("base"), A.add)
         ts(v("OG"), S("kb"), 2048.0, A.add)
-        winners(S("kb"))
+        winners(S("kb"), False)
         act(v("GX"), ind(xwin, v("OG")), AF.Copy, scale=0.5)
         for b in range(8):
             act(v("pK", b, m8, 8), v("DW", b, m8, 8), AF.Copy, scale=col(S("tk"), b))

@@ -10,25 +10,34 @@ BIG = 16777216
 NX = 4112
 SG = 37
 NL = 8 * SG
-SLACK = 0.03
+SLACK = 0.05
 WAIT = 10.0
-LAT = 0.06
-FLY = 2.5
-EARLY = 8.0
-PASSES = 6
+TTG = 1.56
+LAT = 0.18
+FLY = 3.0
+KV = False
+GD = (3,)
+ZV = (0, 1, 2, 3)
+CLV = True
+EARLY = 4.0
+PASSES = 40
+SHAKE = 0.3
 ORDER = []
-SH = 10
+SH = 8
+SW = 2
+YC = 1
+PEADD = 0
 GS = False
-UB = 1.0
+UB = 3.0
 HB = 1.0
-YB = 0.0
-VOWN = ()
-WAYS = "XYZZYZYYZ"
-SIZES = (3, 4, 4, 4, 4, 4, 4, 4, 1)
+YB = 1.0
+VOWN = (0,)
+WAYS = "XYYZYZYYZ"
+SIZES = (2, 4, 4, 4, 4, 4, 4, 4, 2)
 GROW = 0
 MASKAT = 0
-VCUT = (1, 2, 3, 5, 7)
-TCUT = (1, 2, 3, 5, 7, 8)
+VCUT = (1, 3, 5, 7)
+TCUT = (1, 3, 5, 7, 8)
 LCUT = 12
 
 SCRATCH = {}
@@ -56,24 +65,25 @@ _add("sbuf", "bfloat16", "R0 R1 R2 R3 R4", 298)
 _add("sbuf", "bfloat16", "Q NF QT DM CM S1 A1 B1 TDR RS P32 BR ONES", 296)
 _add("sbuf", "bfloat16", "SEG THX", 296, 64)
 _add("sbuf", "float32", "PL SEGI", 296)
-_add("sbuf", "bfloat16", "PP SP G1 ZS SK SO RT4", 288)
-_add("sbuf", "float32", "POS OA ZM WA DW U RT", 288)
+_add("sbuf", "bfloat16", "PP SP G1 ZS SK SO RT4 RTI F0 F1 F2 F3 F4 F5", 288)
+_add("sbuf", "float32", "POS P8 OA ZM WA DW U RT", 288)
 _add("sbuf", "float32", "UF", 384)
 _add("sbuf", "float32", "TAB", 512)
-_add("sbuf", "uint16", "JL OF", 16)
+_add("sbuf", "uint16", "JL", 24)
+_add("sbuf", "uint16", "OF", 16)
+_add("sbuf", "float32", "CJ", 32)
 _add("sbuf", "uint16", "XL XF OG", 8)
 _add("sbuf", "uint16", "LI LO", 16)
 _add("sbuf", "uint16", "LS LU", 18)
 _add("sbuf", "bfloat16", "YR0 YR1 YR2 YR3 LY0 LY1 LY2 LY3", 424)
-_add("sbuf", "int32", "M0 M1 M2 M3 LM0 LM1 LM2 LM3", 16)
-_add("sbuf", "float32", "MV0 MV1 MV2 MV3 LV0 LV1 LV2 LV3", 8)
-_add("sbuf", "float32", "SM", 1600)
+_add("sbuf", "int32", "M0 M1 M2 M3 LM0 LM1 LM2 LM3", 40)
+_add("sbuf", "float32", "SM", 1920)
 _add("sbuf", "int32", "SI", 480)
 _add("sbuf", "float32", "ROWI", 256)
-_add("sbuf", "bfloat16", "C2 RZ", 256)
-_add("sbuf", "bfloat16", "ID IDN I22 N22 I21 IDH IDM DG TRI EXB GA GB GC EQ GX NB", 128)
+_add("sbuf", "bfloat16", "C2 RZ DG2", 256)
+_add("sbuf", "bfloat16", "ID IDN I128 N128 N2 I22 N22 I21 IDH IDM DG TRI EXB GA GB GC EQ GX NB", 128)
 _add("sbuf", "float16", "BLK EXH", 128)
-_add("sbuf", "float16", "CVH", 8)
+_add("sbuf", "float16", "CVH", 16)
 _add("sbuf", "bfloat16", "BW CV", 32)
 _add("sbuf", "float32", "IDF EXR ONF EXF BLF EC RD", 128)
 _add("sbuf", "float32", "GV", 256)
@@ -87,7 +97,7 @@ _add("sbuf", "int32", "WT", 1)
 _add("psum", "float32", "pA pB pC pK pD pY pT pR", 512)
 
 SEMAPHORES = ["qv", "qa", "qt", "qp", "ls"] + ["d%d" % i for i in range(14)] + [
-    m + str(t) for m in ("aw", "ay", "av", "am") for t in range(ST)]
+    m + str(t) for m in ("aw", "ay", "am") for t in range(ST)]
 
 
 def rank_program(g, core, T, topo):
@@ -229,12 +239,16 @@ def rank_program(g, core, T, topo):
         pri = [0.0] * n
         for i in range(n - 1, -1, -1):
             pri[i] = ops[i][7] + max([l + pri[s] for s, l in succ[i]] + [ops[i][8]]) + extra.get(i, 0.0)
-        best = None
-        for _ in range(PASSES):
+        best, z = None, 1
+        for k in range(PASSES):
             order, end = run(succ, pred, pri, [0.0] * n)
             span = max(end[i] + ops[i][8] for i in range(n))
             if best is None or span < best[0]:
-                best = (span, order)
+                best = (span, order, end)
+            end = list(best[2])
+            for i in range(n if k else 0):
+                z = (z * 1103515245 + 12345) % 2147483648
+                end[i] += SHAKE * (z / 2147483648.0 - 0.5)
             pri = run(pred, succ, end, [o[8] for o in ops])[1]
             pri = [pri[i] + extra.get(i, 0.0) for i in range(n)]
         return best[1]
@@ -322,7 +336,7 @@ def rank_program(g, core, T, topo):
 
     def tt(o, x, y, op):
         emit("v", lambda: g.vector.tensor_tensor(ap(o), ap(x), ap(y), op), [o], [x, y],
-             cost=us(o, [x, y], 1 if "p" in (x[0][0], y[0][0]) else 2))
+             cost=us(o, [x, y], 1 if "p" in (x[0][0], y[0][0]) else 2, gather=TTG))
 
     def ts(o, x, s1, op0, s2=None, op1=None):
         r = [x] + [s for s in (s1, s2) if isinstance(s, tuple)]
@@ -370,7 +384,7 @@ def rank_program(g, core, T, topo):
         s = "d%d" % nd[0]
         nd[0] += 1
         emit(eng, lambda: Q[eng].dma_start(out, in_), writes, reads, tok=(s, 16), inc=16, cost=0.05,
-             tail=2.0 + sum(width(w) for w in writes + reads) * 128 * 2 / (200e3 if writes else 100e3))
+             tail=2.0 + sum(width(w) for w in writes + reads) * 128 * 2 / (200e3 if writes else 150e3))
         after("dma" + eng)
         return s
 
@@ -378,7 +392,7 @@ def rank_program(g, core, T, topo):
 
     def S(nm, lo=0, hi=8, step=1, p0=0, p1=128):
         if nm not in scol:
-            scol[nm] = 16 * len(scol)
+            scol[nm] = 24 * len(scol)
         return v("SM", scol[nm] + lo, scol[nm] + hi, step, p0, p1)
 
     def J(nm, lo=0, hi=8, p0=0, p1=128):
@@ -388,6 +402,12 @@ def rank_program(g, core, T, topo):
 
     def S2(nm):
         return S(nm, 0, 16)
+
+    def S3(nm):
+        return S(nm, 0, 24)
+
+    def SL(nm):
+        return S(nm, 16, 24)
 
     def col(w, b):
         return (w[0], w[1] + b, w[1] + b + 1, 1, w[4], w[5])
@@ -403,9 +423,9 @@ def rank_program(g, core, T, topo):
         m = topo.mask(core, to)
         o, i = v(dst, 0, width), v(src, 0, width)
         emit("p", lambda: g.remote_dma(ap(o), ap(i), T.sem[sem], T.sem.ls, pid, rid, m), [], [i], note=False, cost=0.6)
-        ops.append(("x", None, [], [], None, 0, False, 0.0, 0.0, {len(ops) - 1: FLY + width / 80.0}))
-        dacc[dst].append((len(ops) - 1, v(dst, 0, width), True))
         cnt["ls"] += len(topo.engines(core, to))
+        ops.append(("x", None, [], [], None, 0, False, 0.0, 0.0, {len(ops) - 1: FLY + width / 100.0}))
+        dacc[dst].append((len(ops) - 1, o, True))
 
     ID, IDN, DG = v("ID"), v("IDN"), v("DG")
 
@@ -431,8 +451,8 @@ def rank_program(g, core, T, topo):
     iota(v("SEGI"), [[1, 8], [0, SG]], 0, 0)
     iota(v("POS"), [[1, 288]], 0, 0)
     iota(v("P32"), [[0, 8], [-32, SG]], 32 * (SG - 1), 0)
-    iota(S("cj", 0, 8), [[16, 8]], 63 * 128, 0)
-    iota(S("cj", 8, 16), [[1, 8]], 63 * 8, 0)
+    iota(v("CJ", 0, 8), [[16, 8]], 63 * 128, 0)
+    iota(v("CJ", 8, 24), [[1, 16]], 63 * 8, 0)
     iota(J("lo", 0, 16), [[32, 8], [8, 2]], 0, 0)
     iota(v("PP"), [[1, 36], [0, 8]], 0, 0)
     B8 = v("ROWI", 0, 8)
@@ -471,18 +491,21 @@ def rank_program(g, core, T, topo):
             act(v(nm), ID, AF.Copy, scale=w)
         for i, w in enumerate((8192.0, -4096.0, 4096.0)):
             ts(v("BW", 8 * i, 8 * i + 8), B8, pgf, A.is_equal, w, A.mult)
-        for i, w in enumerate((-128.0, -8.0, 1.0)):
+        for i, w in enumerate((-128.0, -8.0, -8.0, -8.0)):
             ts(v("CV", 8 * i, 8 * i + 8), B8, pgf, A.is_equal, w, A.mult)
-        ts(v("CVH"), B8, pgf, A.is_equal)
+        for i in range(2):
+            ts(v("CVH", 8 * i, 8 * i + 8), B8, pgf, A.is_equal)
         ms(v("ONES"), 1.0)
         ms(v("ONF"), 1.0)
         ms(v("RS", 0, NL, SG), -2.0 ** 25)
         ms(v("RZ"), 1.0)
         ms(v("RZ", 0, 256, 16), 0.0)
         ms(v("P32", 0, NL, SG), 2048.0)
+        for q in range(2):
+            act(v("DG2", 128 * q, 128 * q + 128), DG, AF.Copy)
         for nm in ("Q", "A1", "B1", "TDR", "DM"):
             ms(v(nm, 0, NL, SG), 0.0)
-        ts(S("cj", 0, 8), S("cj", 0, 8), paf, A.add)
+        ts(v("CJ", 0, 8), v("CJ", 0, 8), paf, A.add)
         ts(v("XF"), B8, float(SG), A.mult, float(SG - 1), A.add)
         ts(v("BR"), v("SEGI"), pgf, A.is_equal, -2048.0, A.mult)
         ts(v("TRI"), v("CIO"), paf, A.is_ge, 8192.0, A.mult)
@@ -498,8 +521,10 @@ def rank_program(g, core, T, topo):
         ts(v("BLF"), v("BO"), pgf, A.is_equal)
         for p in range(2, SH):
             ms(row("BR", p), 0.0)
-        ts(S("V00"), v("VI", 0, 8), dump, A.subtract)
-        ts(S("b8"), B8, -8.0, A.add)
+        ts(S("V00", 8, 16), v("VI", 0, 8), dump, A.subtract)
+        ts(dk4, pa, 4096.0, A.mult)
+        ms(v("CJ", 24, 32), 64.0 * 8)
+        act(v("P8"), v("PP"), AF.Copy, bias=8.0, scale=8.0)
         bits(k[6], pi, 0, 31)
         tc(q31, k[6])
         ts(is8, pi, 8.0, A.is_equal)
@@ -528,6 +553,8 @@ def rank_program(g, core, T, topo):
         ts(f[9], k[1], 8.0, A.mult)
         tt(f[10], f[9], k[13], A.add)
         ts(v("LU"), v("ROWI", 0, 18), 16.0, A.mult, f[10], A.add)
+        for nm, w in (("I128", 160.0), ("N128", -160.0), ("N2", -2.0)):
+            act(v(nm), ID, AF.Copy, scale=w)
         act(v("C2", 0, 128), ID, AF.Copy)
         act(v("C2", 128, 256), ID, AF.Copy)
 
@@ -552,12 +579,19 @@ def rank_program(g, core, T, topo):
     def masks(t):
         R = "R%d" % t
         lin(v("pR", 0, NL), (ID, v(R, 0, NL)), (IDN, v(R, 1, NL + 1)))
-        act(S("b25"), S("n%d" % t, 8, 16), AF.Copy, bias=-2.5 * 2 ** 25, scale=2.0 ** 25)
+        act(S("b25"), SL("n%d" % t), AF.Copy, bias=-2.5 * 2 ** 25, scale=2.0 ** 25)
         boost[0] = EARLY
         act(v("NF"), v("pR", 0, NL), AF.Relu, bias=1.0, scale=-1.0)
         for b in range(8):
             act(seg("RS", b), seg(R, b, -1), AF.Identity, bias=col(S("b25"), b), scale=-2.0 ** 25)
         boost[0] = 0.0
+
+    def to_lists(out, src, bank):
+        act(v("SK"), ind(src, v("LS")), AF.Copy)
+        for e in range(8):
+            mm(v(bank, e, 288, 8), v("C2", 128 - 16 * e, 256 - 16 * e), v("SK", e, 288, 8), True, True)
+        act(v("SO"), v(bank, 0, 288), AF.Copy)
+        act(out, ind(v("SO"), v("LU")), AF.Copy)
 
     xwin = v("X")
 
@@ -586,12 +620,12 @@ def rank_program(g, core, T, topo):
         G = P - 2
         n8, m8 = P * 8, P * 8 + 8
         W, R, Wn, Rn = "W%d" % t, "R%d" % t, "W%d" % (t + 1), "R%d" % (t + 1)
-        YR, M, MV, LW, LY, LM, LV = ["%s%d" % (q, t) for q in ("YR", "M", "MV", "LW", "LY", "LM", "LV")]
-        n, nn, V0, V0n = S2("n%d" % t), S2("n%d" % (t + 1)), S("V0%d" % t), S("V0%d" % (t + 1))
+        YR, M, LW, LY, LM = ["%s%d" % (q, t) for q in ("YR", "M", "LW", "LY", "LM")]
+        n, nn, V0, V0n = S3("n%d" % t), S3("n%d" % (t + 1)), "V0%d" % t, "V0%d" % (t + 1)
         d = 1 + t % 5
         to, fr = T.cores[(rank + d) % N], T.cores[(rank - d) % N]
         ne = len(topo.engines(fr, core))
-        for buf, sem, wd in ((LW, "aw", m8 + 8), (LY, "ay", 128 + NL), (LV, "av", 8), (LM, "am", 16)):
+        for buf, sem, wd in ((LW, "aw", m8 + 8), (LY, "ay", 128 + NL), (LM, "am", 40)):
             record((sem + str(t), ne), [v(buf, 0, wd)], [], {})
 
         def rows(nm, r0, r1):
@@ -605,12 +639,12 @@ def rank_program(g, core, T, topo):
         tcut = [0] + [cut[c] for c in TCUT] + [G]
         banks = ("pA", "pB", "pC", "pY")
         boost[0] = EARLY
-        ts(S2("L64"), n, 4.0, A.is_ge, 64.0, A.mult)
-        act(S2("L"), S2("L64"), AF.Copy, scale=1.0 / 64)
+        ts(S3("L64"), n, 4.0, A.is_ge, 64.0, A.mult)
+        act(S3("L"), S3("L64"), AF.Copy, scale=1.0 / 64)
         tc(v(W, m8, m8 + 8), S("L"))
         send(W, LW, m8 + 8, "aw%d" % t, to)
         boost[0] = 0.0
-        tt(S2("thr"), n, S2("L64"), A.max)
+        tt(S3("thr"), n, S3("L64"), A.max)
         mm(v("pK", 0, NL), ID, v("QT"), True, False)
         mm(v("pD", 0, NL), v("ONES", 0, 128, 1, 0, 64), v("THX"), True, False)
         gv = gt = 0
@@ -655,34 +689,37 @@ def rank_program(g, core, T, topo):
             gv += 1
         for r in range(SH, P):
             mm(row("pD", r), rows("XV", r, r + 1), v("BW", 8, 16))
-        for r in range(2, SH, 4):
-            mm(v(banks[(r - 2) // 4]), ID, rows("XV", r, r + 4), True, False)
-        tt(S("nL"), S("n%d" % t, 8, 16), S("L", 8, 16), A.mult)
+        shared = [(r, min(r + SW, SH)) for r in range(2, SH, SW)]
+        for q, (r0, r1) in enumerate(shared):
+            mm(v(banks[q], 0, (r1 - r0) * 128), ID, rows("XV", r0, r1), True, False)
+        tt(S("nL"), SL("n%d" % t), SL("L64"), A.min)
         act(S("bn"), S("nL"), AF.Copy, bias=0.5, scale=-1.0)
         for b in range(8):
             act(seg("DM", b), seg(R, b), AF.Sign, bias=col(S("bn"), b))
         mm(v("pD", 0, NL), v("I22"), v("NF"))
         mm(v("pD", 0, NL), v("I21"), v("DM"))
 
-        mm(v("pT", 0, 16), v("IDF"), S2("cj"), True, False)
+        act(v("NB", 0, 8), S("L"), AF.Copy, bias=1024.0, scale=-1024.0)
+        mm(v("pT", 0, 32), v("IDF"), v("CJ"), True, False)
+        mm(v("pT", 24, 32), ID, v("NB", 0, 8))
         scan(v("KS"), v("RS"), v("pK", 0, NL), A.min, A.max)
         bits(J("q"), row("KS", 0), 5, 63)
         tt(v("EXB"), ind(J("q"), v("XL")), DG, A.mult)
-        mm(v("pT", 0, 16), v("EXB"), v("CV", 0, 16), False, True)
-        tc(v("JL"), v("pT", 0, 16))
-        jk, jw = v("JL", 0, 8), v("JL", 8, 16)
+        mm(v("pT", 0, 32), v("EXB"), v("CV"), False, True)
+        tc(v("JL"), v("pT", 0, 24))
+        jk = v("JL", 0, 8)
         act(v("GA"), ind(v("XV", 128, G * 128 + 128), jk), AF.Copy, scale=2.0)
         tt(v("GB"), ind(v("T1", 0, G * 128), jk), v("GA"), A.subtract)
         tt(v("GC"), ind(v("XV", 0, G * 128), jk), v("GB"), A.subtract)
         Y = v(YR, 0, 128)
         ts(Y, v("GC"), 0.0, A.max, 63.0, A.min)
         boost[0] = YB
-        for q in range(2):
+        for q in range(YC):
             mm(v("pY", q * 128, q * 128 + 128), v("IDH"), Y, True, True)
         boost[0] = 0.0
         ts(J("kk"), row("KS", 0), 31, A.bitwise_and)
         ts(S("nk"), J("kk"), -1.0, A.mult)
-        act(S("jw"), v("pT", 8, 16), AF.Copy)
+        act(S("jw"), v("pT", 24, 32), AF.Copy)
         act(S("jb"), v("pT", 8, 16), AF.Copy, bias=-0.5, scale=-1.0)
         for b in range(8):
             act(seg("Q", b), seg(R, b), AF.Relu, bias=col(S("nk"), b))
@@ -692,7 +729,6 @@ def rank_program(g, core, T, topo):
         send(YR, LY, 128 + NL, "ay%d" % t, to)
         lin(v("pR", 0, NL), (ID, v("P32")), (ID, RK))
         act(v("PL"), v("pR", 0, NL), AF.Copy)
-        act(v("S1"), v("Q"), AF.Sign)
 
         boost[0] = UB
         mm(v("pK", 0, 8), Y, v("BW", 24, 32), True, True)
@@ -703,101 +739,122 @@ def rank_program(g, core, T, topo):
         boost[0] = 0.0
         mm(v("pD", 0, NL), Y, v("BR"))
         mm(v("pD", 0, NL), v("I22"), v("CM"))
-        shared = list(range(2, SH, 4))
         for c, r in enumerate(range(SH, P, 2)):
-            e = min(r + 2, P)
-            tt(rows("AB", r, e), rows("XV", r, e), v("pY", 0, (e - r) * 128), A.max)
-            if c % 3 == 0 and shared:
-                r0 = shared.pop(0)
-                bank = banks[(r0 - 2) // 4]
-                for q in range(4):
-                    mm(v(bank, 128 * q, 128 * q + 128), v("IDM"), Y, False, q == 3)
-                act(rows("AB", r0, r0 + 4), v(bank), AF.Abs)
-            if c % 3 == 2 and c // 3 < (SH - 2) // 4:
-                for q in range(2 + c // 3 * 4, 6 + c // 3 * 4):
+            for r1 in range(r, min(r + 2, P), YC):
+                e = min(r1 + YC, P)
+                tt(rows("AB", r1, e), rows("XV", r1, e), v("pY", 0, (e - r1) * 128), A.max)
+            if c % 3 == 0 and c // 3 < len(shared):
+                r0, r1 = shared[c // 3]
+                for q in range(r1 - r0):
+                    mm(v(banks[c // 3], 128 * q, 128 * q + 128), v("IDM"), Y, False, q == r1 - r0 - 1)
+                act(rows("AB", r0, r1), v(banks[c // 3], 0, (r1 - r0) * 128), AF.Abs)
+            if c % 3 == 2 and c // 3 < len(shared):
+                for q in range(*shared[c // 3]):
                     mm(row("pD", q), rows("AB", q, q + 1), v("BW", 16, 24))
-            for q in range(r, e):
+            for q in range(r, min(r + 2, P)):
                 mm(row("pD", q), rows("AB", q, q + 1), v("BW", 0, 8), False, q == P - 1)
-        for q in range(2):
-            tt(v("GV", 128 * q, 128 * q + 128), ind(v(W, 8 * q, n8), jw), DG, A.mult)
+        tt(v("GV"), ind(v(W, 0, n8), v("JL", 8, 24)), v("DG2"), A.mult)
         scan(v("SC"), v("RZ"), v("GV"), A.mult, A.add)
         bits(J("vk", 0, 16), v("SC", 15, 256, 16), 12, 4095)
         vk, vk1, wk = J("vk"), J("vk", 8, 16), v("SC", 15, 128, 16)
-        ts(v(MV), vk1, dump, A.subtract)
-        send(MV, LV, 8, "av%d" % t, to)
-        for b in range(8):
+        ts(v(M, 24, 32), vk1, -2048.0, A.add)
+        ts(v(M, 32, 40), vk1, dump, A.subtract)
+        tc(S("vk"), vk)
+        for b in range(0 if t in GD else 8):
             act(v("SP", b, m8, 8), v("POS", b, m8, 8), AF.Sign, bias=col(S("jb"), b))
         scan(v("FS"), v("pD", 0, NL), v("PL"), A.min, A.max)
         tt(v("EXH"), ind(v("FS"), v("XF")), DG, A.mult)
-        mm(v("pT", 0, 8), v("EXH"), v("CVH"), True, True)
-        tc(J("vm"), v("pT", 0, 8))
-        ts(v(M, 0, 8), J("vm"), 31, A.bitwise_and)
-        ts(v(M, 8, 16), row("FS", 0), 31, A.bitwise_and)
-        send(M, LM, 16, "am%d" % t, to)
-        sz = v(M)
-        ts(S2("cl"), sz, 1.0, A.min)
-        tt(S2("gr"), S2("L"), S2("cl"), A.subtract)
+        mm(v("pT", 0, 16), v("EXH"), v("CVH"), True, True)
+        tc(J("vm", 0, 16), v("pT", 0, 16))
+        ts(v(M, 0, 16), J("vm", 0, 16), 31, A.bitwise_and)
+        ts(v(M, 16, 24), row("FS", 0), 31, A.bitwise_and)
+        send(M, LM, 40, "am%d" % t, to)
+        tc(S3("sz"), v(M, 0, 24))
+        if CLV:
+            ts(S3("cl"), v(M, 0, 24), 1.0, A.min)
+        else:
+            act(S3("cl"), S3("sz"), AF.Sign)
+        tt(S3("gr"), S3("L"), S3("cl"), A.subtract)
 
         boost[0] = HB
         tc(J("u"), v("pK", 8, 16))
         ts(J("u2"), J("u"), 4095, A.bitwise_and)
         tt(J("uu"), J("u2"), J("u2"), A.mult)
-        ts(J("v37"), vk, 37.0, A.mult)
+        act(S("v37"), S("vk"), AF.Copy, scale=37.0)
         ts(J("us"), J("uu"), 5, A.arith_shift_right)
-        tt(J("h0"), J("us"), J("v37"), A.add)
+        tt(J("h0"), J("us"), S("v37"), A.add)
         ts(J("h"), J("h0"), 4095, A.bitwise_and)
         ts(S("hd"), J("h"), dump, A.subtract)
         boost[0] = 0.0
         tt(S("hg"), S("hd"), S("gr"), A.mult)
-        act(S("kg"), S("hg"), AF.Identity, bias=dumpk)
+        if KV:
+            ts(S("kg"), S("hg"), dumpk, A.add)
+        else:
+            act(S("kg"), S("hg"), AF.Identity, bias=dumpk)
         winners(S("kg"), GS)
         put(YR)
 
-        ts(S("z0"), vk, 4096.0, A.mult, float(-BIG), A.add)
+        act(S("z0"), S("vk"), AF.Copy, bias=float(-BIG), scale=4096.0)
         tt(S("z"), S("z0"), vk1, A.add)
-        ts(S("wn0"), J("h"), 4096.0, A.mult, float(-BIG), A.add)
+        act(S("wn0"), S("hd"), AF.Identity, bias=dk4, scale=4096.0)
         tt(S("wn1"), vk, wk, A.subtract)
         tt(S("wn"), S("wn0"), S("wn1"), A.add)
-        tt(S("c1"), S("b8"), S("jw"), A.subtract)
-        act(S("rs"), S("L"), AF.Copy, bias=-1000.0, scale=1000.0)
-        tt(S("c2"), S("jw"), S("rs"), A.add)
         bits(J("pm"), J("vm"), 2, 504)
-        tt(S("c3"), J("pm"), S("c1"), A.add)
-        tt(S("c4"), S("c3"), S("cl"), A.mult)
-        tt(S("pz"), S("c4"), S("c2"), A.add)
+        tt(S("pz"), J("pm"), S("jw"), A.max)
+        zv = t in ZV
+        if zv:
+            for b in range(8):
+                ts(v("ZM", b, m8, 8), v("P8", b, m8, 8), col(S("pz"), b), A.is_equal, col(S("z"), b), A.mult)
+            act(v("ZS", 0, m8), v("ZM", 0, m8), AF.Sign)
+        else:
+            for b in range(8):
+                act(v("OA", b, m8, 8), v("P8", b, m8, 8), AF.Abs, bias=col(S("pz"), b), scale=-1.0)
+            act(v("ZS", 0, m8), v("OA", 0, m8), AF.Relu, bias=1.0, scale=-1.0)
+            for b in range(8):
+                act(v("ZM", b, m8, 8), v("ZS", b, m8, 8), AF.Copy, scale=col(S("z"), b))
         for b in range(8):
-            act(v("OA", b, m8, 8), v("POS", b, m8, 8), AF.Abs, bias=col(S("pz"), b), scale=-1.0)
-        act(v("ZS", 0, m8), v("OA", 0, m8), AF.Relu, bias=1.0, scale=-1.0)
-        for b in range(8):
-            act(v("ZM", b, m8, 8), v("ZS", b, m8, 8), AF.Copy, scale=col(S("z"), b))
-        for b in range(8):
-            act(v("G1", b, m8, 8), v("SP", b, m8, 8), AF.Relu, scale=col(S("gr"), b))
+            if t in GD:
+                ts(v("G1", b, m8, 8), v("P8", b, m8, 8), col(S("jw"), b), A.is_gt, col(S("gr"), b), A.mult)
+            else:
+                act(v("G1", b, m8, 8), v("SP", b, m8, 8), AF.Relu, scale=col(S("gr"), b))
         lin(v("pB", 0, m8), (ID, v("G1", 0, m8)))
         lin(v("pC", 8, m8), (ID, v("G1", 8, m8)), (IDN, v("G1", 0, n8)))
-        lin(v("pA", 0, m8), (ID, v("ONES", 0, m8)), (IDN, v("G1", 0, m8)), (IDN, v("ZS", 0, m8)))
-        for b in range(8):
-            act(v("pC", 8 + b, m8, 8), v("pC", 8 + b, m8, 8), AF.Copy, scale=col(S("wn"), b))
-        tt(v("pB", 8, m8), v(W, 0, n8), v("pB", 8, m8), A.mult)
-        tt(v("ZM", 8, m8), v("ZM", 8, m8), v("pC", 8, m8), A.add)
-        tt(v("ZM", 8, m8), v("ZM", 8, m8), v("pB", 8, m8), A.add)
-        tt(v("pA", 0, m8), v(W, 0, m8), v("pA", 0, m8), A.mult)
-        tt(v("WA", 0, m8), v("ZM", 0, m8), v("pA", 0, m8), A.add)
+        lin(v("pA", 0, m8), (ID, v("ONES", 0, m8)), (IDN, v("G1", 0, m8)), (ID if zv else IDN, v("ZS", 0, m8)))
+        if PEADD:
+            for b in range(8):
+                act(v("OA", 8 + b, m8, 8), v("pC", 8 + b, m8, 8), AF.Copy, scale=col(S("wn"), b))
+            mm(v("pC", 0, m8), v("IDF"), v("ZM", 0, m8), True, False)
+            mm(v("pC", 8, m8), v("IDF"), v("OA", 8, m8), False, PEADD == 1)
+            tt(v("U", 8, m8), v(W, 0, n8), v("pB", 8, m8), A.mult)
+            tt(v("WA", 0, m8), v(W, 0, m8), v("pA", 0, m8), A.mult)
+            if PEADD == 2:
+                mm(v("pC", 8, m8), v("IDF"), v("U", 8, m8), False, True)
+            else:
+                tt(v("pC", 8, m8), v("U", 8, m8), v("pC", 8, m8), A.add)
+            tt(v("pA", 0, m8), v("WA", 0, m8), v("pC", 0, m8), A.add)
+        else:
+            for b in range(8):
+                act(v("pC", 8 + b, m8, 8), v("pC", 8 + b, m8, 8), AF.Copy, scale=col(S("wn"), b))
+            tt(v("pB", 8, m8), v(W, 0, n8), v("pB", 8, m8), A.mult)
+            tt(v("ZM", 8, m8), v("ZM", 8, m8), v("pC", 8, m8), A.add)
+            tt(v("ZM", 8, m8), v("ZM", 8, m8), v("pB", 8, m8), A.add)
+            tt(v("pA", 0, m8), v(W, 0, m8), v("pA", 0, m8), A.mult)
+            tt(v("WA", 0, m8), v("ZM", 0, m8), v("pA", 0, m8), A.add)
         tt(v("DW", 0, m8), v(LW, 0, m8), v("pA", 0, m8), A.subtract)
-        ts(S("nsz"), v(M, 8, 16), -1.0, A.mult)
-        act(S("g2"), S("gr", 8, 16), AF.Copy, bias=-2.0)
-        lin(v("pY", 0, NL), (ID, v("S1")), (ID, v("NF")))
-        lin(v("pD", 0, NL), (ID, v(LY, 128, 128 + NL)), (IDN, v(R, 0, NL)))
+        act(S("nsz"), SL("sz"), AF.Copy, scale=-1.0)
+        act(S("g2"), SL("gr"), AF.Copy, bias=-2.0)
+        lin(v("pY", 0, NL), (ID, v("Q")), (IDN, RK), (ID, v("NF")))
         for b in range(8):
             act(seg("A1", b), seg("Q", b), AF.Relu, bias=col(S("nsz"), b))
         for b in range(8):
             act(seg("B1", b), seg("pY", b), AF.Relu, bias=col(S("g2"), b))
         for l, r in ((ID, v(R, 0, NL)), (IDN, v("Q")), (ID, v("A1")), (ID, v("B1"))):
-            mm(v("pR", 0, NL), l, r, r[0] == R, False)
-        tt(S2("ng"), n, S2("gr"), A.add)
-        ts(S2("ng"), S2("ng"), 32.0, A.min)
-        tt(S2("n2"), S2("ng"), sz, A.subtract)
+            mm(v("pR", 0, NL), l, r, r[0] == R, r[0] == "B1" and t == ST - 1)
+        tt(S3("ng"), n, S3("gr"), A.add)
+        ts(S3("ng"), S3("ng"), 32.0, A.min)
+        tt(S3("n2"), S3("ng"), S3("sz"), A.subtract)
         if t < ST - 1:
-            act(S("clc"), S("cl", 8, 16), AF.Copy, acc_out=S("cs", 0, 1))
+            act(S("clc"), SL("cl"), AF.Copy, acc_out=S("cs", 0, 1))
             mm(v("pK", 16, 17, 1, 0, 64), v("ONF", 0, 64), S("cs", 0, 1), True, True)
             cj = J("c", 0, 1, 0, 64)
             tc(cj, v("pK", 16, 17, 1, 0, 64))
@@ -807,90 +864,94 @@ def rank_program(g, core, T, topo):
             act(v("THX"), v("SEG"), AF.Copy, scale=S("th", 2, 3, 1, 0, 64))
             boost[0] = 0.0
 
+        if t < ST - 1:
+            lin(v("pD", 0, NL), (ID, v(LY, 128, 128 + NL)), (IDN, v(R, 0, NL)))
+        else:
+            to_lists(v("RTI"), v(LY, 128, 128 + NL), "pK")
+            act(v(Rn, 0, NL), v("pR", 0, NL), AF.Copy)
+            to_lists(v("RT4"), v(Rn, 0, NL), "pD")
         act(v("pK", 320, 448), v(LY, 0, 128), AF.Copy, bias=-0.25, scale=0.5)
         tt(S("has"), S("n%d" % t), v(LW, m8, m8 + 8), A.min)
-        tt(S("hv"), S("has"), V0, A.mult)
-        tt(S("dl"), v(LV), S("hv"), A.subtract)
-        act(S("base"), S("hv"), AF.Identity, bias=dumpk)
-        tt(S("dv"), v(LV), V0, A.subtract)
-        tt(S2("tk"), v(LM), S2("thr"), A.is_gt)
-        tt(S("kd"), S("tk"), S("dl"), A.mult)
-        tt(S("kb"), S("kd"), S("base"), A.add)
-        ts(v("OG"), S("kb"), 2048.0, A.add)
-        winners(S("kb"), False)
+        tt(S("hv"), S("has"), S(V0, 8, 16), A.mult)
+        act(S(V0), S("hv"), AF.Identity, bias=dumpk)
+        tt(S3("tk"), v(LM, 0, 24), S3("thr"), A.is_gt)
+        tt(S2("dl"), v(LM, 24, 40), S2(V0), A.subtract)
+        tt(S2("kd"), S2("tk"), S2("dl"), A.mult)
+        tt(S2(V0n), S2("kd"), S2(V0), A.add)
+        ts(v("OG"), S(V0n), 2048.0, A.add)
+        winners(S(V0n), False)
         act(v("GX"), ind(xwin, v("OG")), AF.Copy, scale=0.5)
         for b in range(8):
-            act(v("pK", b, m8, 8), v("DW", b, m8, 8), AF.Copy, scale=col(S("tk"), b))
+            act(v("WA" if PEADD else "pK", b, m8, 8), v("DW", b, m8, 8), AF.Copy, scale=col(S("tk"), b))
         tt(v("BO"), v("GX"), v("pK", 320, 448), A.add)
-        tt(v(Wn, 0, m8), v("WA", 0, m8), v("pK", 0, m8), A.add)
+        tt(v(Wn, 0, m8), v("WA", 0, m8), v("pA" if PEADD else "pK", 0, m8), A.add)
         put("BO")
-        tt(S2("rc"), v(LM), S2("tk"), A.mult)
-        tt(nn, S2("rc"), S2("n2"), A.max)
-        tt(S("dvt"), S("dv"), S("tk"), A.mult)
-        tt(V0n, V0, S("dvt"), A.add)
-        for b in range(8):
-            act(seg("TDR", b), seg("pD", b), AF.Copy, scale=col(S("tk", 8, 16), b))
-        mm(v("pR", 0, NL), ID, v("TDR"), False, True)
-        act(v(Rn, 0, NL), v("pR", 0, NL), AF.Copy)
+        tt(S3("rc"), v(LM, 0, 24), S3("tk"), A.mult)
+        tt(nn, S3("rc"), S3("n2"), A.max)
         if t < ST - 1:
+            for b in range(8):
+                act(seg("TDR", b), seg("pD", b), AF.Copy, scale=col(SL("tk"), b))
+            mm(v("pR", 0, NL), ID, v("TDR"), False, True)
+            act(v(Rn, 0, NL), v("pR", 0, NL), AF.Copy)
             masks(t + 1)
             lists(t + 1)
 
     lists(0)
     late_constants()
     tc(v("NB", 0, 128, 1, 0, 8), v("NR"))
-    mm(v("pT", 8, 16), v("NB", 0, 128, 1, 0, 8), v("ID", 0, 8, 1, 0, 8), True, True)
-    tc(S("n0", 8, 16), v("pT", 8, 16))
-    tc(S("nl"), v("pT", 8, 16))
-    tt(v("EXB"), ind(S("nl"), v("XL")), DG, A.mult)
-    mm(v("pT", 0, 8), v("EXB"), v("CV", 16, 24), True, True)
-    tc(S("n0"), v("pT", 0, 8))
+    mm(v("pT", 16, 24), v("NB", 0, 128, 1, 0, 8), v("ID", 0, 8, 1, 0, 8), True, True)
+    tc(SL("n0"), v("pT", 16, 24))
+    tt(v("EXH"), ind(SL("n0"), v("XL")), DG, A.mult)
+    mm(v("pT", 0, 16), v("EXH"), v("CVH"), True, True)
+    tc(S2("n0"), v("pT", 0, 16))
     masks(0)
     for t in range(ST):
         if t == ST - 1:
             last_constants()
         step(t)
 
-    act(v("NB", 0, 8), S("n4", 8, 16), AF.Copy)
-    mm(v("pC", 0, 128, 1, 0, 8), v("NB", 0, 8), ID, True, True)
-    act(v("NO"), v("pC", 0, 128, 1, 0, 8), AF.Copy)
-    so = [dma("s", T.yx[:, 0:2048], ap(v("X", 0, 2048)), [], [v("X", 0, 2048)]),
-          dma("a", T.yx[:, 2048:4096], ap(v("X", 2048, 4096)), [], [v("X", 2048, 4096)]),
-          dma("s", T.yn[:], ap(v("NO")), [], [v("NO")])]
-    act(v("SK"), ind(v("R4", 0, NL), v("LS")), AF.Copy)
-    for e in range(8):
-        mm(v("pD", e, 288, 8), v("C2", 128 - 16 * e, 256 - 16 * e), v("SK", e, 288, 8), True, True)
-    act(v("SO"), v("pD", 0, 288), AF.Copy)
-    act(v("RT4"), ind(v("SO"), v("LU")), AF.Copy)
-    lin(v("pK", 0, 280), (ID, v("RT4", 8, 288)), (IDN, v("RT4", 0, 280)))
-    lin(v("pK", 280, 288), (ID, v("ONES", 0, 8)))
-    lin(v("pY", 0, 288), (ID, v("PP")), (IDN, v("RT4")))
-    act(S("n5"), S("n4"), AF.Copy, bias=-0.5)
+    lin(v("pD", 0, 288), (ID, v("RTI")), (IDN, v("RT4")))
     for b in range(8):
-        act(v("NM", b, 256, 8), v("PP", b, 256, 8), AF.Sign, bias=col(S("n5"), b), scale=-1.0)
-    act(v("NM"), v("NM"), AF.Relu)
-    ts(v("U"), v("W4", 0, 288), float(BIG), A.add)
-    tc(v("DLT"), v("pY", 0, 288))
-    tt(v("pA", 0, 288), v("U"), v("pK", 0, 288), A.mult)
+        act(v("SK", b, 288, 8), v("pD", b, 288, 8), AF.Copy, scale=col(S("tk"), b))
+    lin(v("pY", 0, 288), (ID, v("PP")), (IDN, v("RT4")), (IDN, v("SK")))
+    lin(v("pB", 0, 280), (ID, v("RT4", 8, 288)), (IDN, v("RT4", 0, 280)), (ID, v("SK", 8, 288)), (IDN, v("SK", 0, 280)))
+    lin(v("pB", 280, 288), (ID, v("ONES", 0, 8)))
+    tt(v("UF", 0, 288), v("W4", 0, 288), v("pB", 0, 288), A.mult)
+    for i in range(6):
+        act(v("F%d" % i, 8 << max(i - 1, 0), 288), v("pY", 8 << max(i - 1, 0), 288), AF.Copy, bias=159.5 + 1.0 / 64, scale=0.5 ** i)
     for i in range(6):
         lo = 8 << i
         w = 288 - lo
-        bit = v("BIT" if i % 2 else "CI", lo, 288)
-        bits(bit, v("DLT", lo, 288), i, 1)
-        tt(v("U", lo, 288), bit, v("pA", lo, 288), A.mult)
-        tt(v("pA", lo, 288), v("pA", lo, 288), v("U", lo, 288), A.subtract)
-        tt(v("pA", 0, w), v("pA", 0, w), v("U", lo, 288), A.add)
-    tt(v("UF", 0, 256), v("NM"), v("pA", 0, 256), A.mult)
-    tt(v("UF", 256, 384), v("NM", 0, 128), v("pA", 0, 128), A.mult)
+        bit = v("pC" if i % 2 else "pR", lo, 288)
+        if i < 5:
+            lin(bit, (v("I128"), v("ONES", lo, 288)), (ID, v("F%d" % i, lo, 288)), (v("N2"), v("F%d" % (i + 1), lo, 288)))
+        else:
+            lin(bit, (v("N128"), v("ONES", lo, 288)), (ID, v("F%d" % i, lo, 288)))
+        tt(v("pA", lo, 288), v("UF", lo, 288), bit, A.mult)
+        tt(v("UF", lo, 288), v("UF", lo, 288), v("pA", lo, 288), A.subtract)
+        tt(v("UF", 0, w), v("UF", 0, w), v("pA", lo, 288), A.add)
+    act(v("UF", 256, 384), v("UF", 0, 128), AF.Copy)
+    act(v("NB", 0, 8), SL("n4"), AF.Copy)
+    mm(v("pD", 0, 128, 1, 0, 8), v("NB", 0, 8), ID, True, True)
+    act(v("NO"), v("pD", 0, 128, 1, 0, 8), AF.Copy)
+    act(v("EXB"), ind(SL("n4"), v("XL")), AF.Copy)
+    mm(v("pD", 128, 256), v("EXB"), ID, True, True)
+    for s in range(2):
+        act(S("n5", s, s + 1), paf, AF.Copy, bias=-0.5 - 16 * s, scale=-1.0)
+        act(v("NM", s, 256, 2), v("pD", 128, 256), AF.Sign, bias=S("n5", s, s + 1))
+    act(v("pK", 0, 256), v("NM"), AF.Relu)
+    so = [dma("s", T.yx[:, 0:2048], ap(v("X", 0, 2048)), [], [v("X", 0, 2048)]),
+          dma("a", T.yx[:, 2048:4096], ap(v("X", 2048, 4096)), [], [v("X", 2048, 4096)]),
+          dma("s", T.yn[:], ap(v("NO")), [], [v("NO")])]
     for w in range(2):
         for b in range(8):
             tp(v("TAB", w * 256 + b * 32, w * 256 + b * 32 + 32), v("UF", 128 * w + b, 128 * w + 256, 8))
     tc(v("OI"), ind(v("TAB"), v("LO")))
-    ts(v("VI", 0, 256), v("OI"), 12, A.arith_shift_right)
-    tc(v("OV"), v("VI", 0, 256))
+    bits(v("VI", 0, 256), v("OI"), 12, 4095)
+    tt(v("OV"), v("VI", 0, 256), v("pK", 0, 256), A.mult)
     so.append(dma("s", T.yv[:], ap(v("OV")), [], [v("OV")]))
     ts(v("CI", 0, 256), v("OI"), 4095, A.bitwise_and)
-    tc(v("OC"), v("CI", 0, 256))
+    tt(v("OC"), v("CI", 0, 256), v("pK", 0, 256), A.mult)
     so.append(dma("a", T.yc[:], ap(v("OC")), [], [v("OC")]))
     flush()
     for s in so:

@@ -7,7 +7,8 @@ AF = ActivationFunctionType
 N = 6
 ST = 4
 BIG = 16777216
-NX = 4112
+NX = 4256
+NB = 8
 SG = 37
 NL = 8 * SG
 SLACK = 0.05
@@ -26,18 +27,20 @@ ORDER = []
 SH = 8
 SW = 2
 YC = 1
+CS = 4
+TB = 1.0
 PEADD = 0
 GS = False
-UB = 3.0
-HB = 1.0
+UB = 0.0
+HB = 0.0
 YB = 1.0
 VOWN = (0,)
-WAYS = "XYYZYZYYZ"
+WAYS = "YXYZYZYXZ"
 SIZES = (2, 4, 4, 4, 4, 4, 4, 4, 2)
 GROW = 0
-MASKAT = 0
-VCUT = (1, 3, 5, 7)
-TCUT = (1, 3, 5, 7, 8)
+MASKAT = 5
+VCUT = (1, 2, 3, 5, 7, 8)
+TCUT = (1, 2, 3, 5, 7, 8)
 LCUT = 12
 
 SCRATCH = {}
@@ -81,11 +84,12 @@ _add("sbuf", "float32", "SM", 1920)
 _add("sbuf", "int32", "SI", 480)
 _add("sbuf", "float32", "ROWI", 256)
 _add("sbuf", "bfloat16", "C2 RZ DG2", 256)
-_add("sbuf", "bfloat16", "ID IDN I128 N128 N2 I22 N22 I21 IDH IDM DG TRI EXB GA GB GC EQ GX NB", 128)
+_add("sbuf", "bfloat16", "ID IDN I128 N128 N2 I22 N22 I21 IDH IDM DG TRI EXB GA GB GC GX NB IDQ", 128)
 _add("sbuf", "float16", "BLK EXH", 128)
 _add("sbuf", "float16", "CVH", 16)
 _add("sbuf", "bfloat16", "BW CV", 32)
-_add("sbuf", "float32", "IDF EXR ONF EXF BLF EC RD", 128)
+_add("sbuf", "float32", "IDF EXR ONF EXF EC", 128)
+_add("sbuf", "bfloat16", "EQ", 1024)
 _add("sbuf", "float32", "GV", 256)
 _add("sbuf", "int32", "SC VR CR OI", 256)
 _add("sbuf", "int32", "BO CIO", 128)
@@ -111,6 +115,8 @@ def rank_program(g, core, T, topo):
     acc = {n: [] for n in TILES}
     nd = [0]
     boost = [0.0]
+    opened = {}
+    behind = {}
 
     def v(name, lo=0, hi=None, step=1, p0=0, p1=None):
         sh = TILES[name][1]
@@ -147,7 +153,7 @@ def rank_program(g, core, T, topo):
             ops[-1][9].setdefault(chains[name], -ops[chains[name]][8])
         chains[name] = len(ops) - 1
 
-    def emit(eng, call, writes, reads, tok=None, inc=1, note=True, cost=0.1, tail=0.0):
+    def emit(eng, call, writes, reads, tok=None, inc=1, note=True, cost=0.1, tail=0.0, adds=None):
         extra[len(ops)] = boost[0]
         ws = [w[1] if w[0] == "ind" else w for w in writes]
         rs = [w[2] for w in writes if w[0] == "ind"]
@@ -168,14 +174,17 @@ def rank_program(g, core, T, topo):
                     ph = phase[w[0]]
                     if ph and ph[-1][0] == eng:
                         prev = ph[-2][1] if len(ph) > 1 else []
-                        if eng == "t" and ph[-1][1][-1] != me:
-                            deps[ph[-1][1][-1]] = 0.0
+                        if eng == "t":
+                            for i in (ph[-1][1] if adds is None else [adds]):
+                                deps[i] = 0.0
                         ph[-1][1].append(me)
                     else:
                         prev = ph[-1][1] if ph else []
                         ph.append([eng, [me]])
                     for i in prev:
                         deps[i] = LAT
+        if eng in behind:
+            deps.setdefault(behind[eng], 0.0)
         deps.pop(me, None)
         for w in rs:
             dacc[w[0]].append((me, w, False))
@@ -367,7 +376,10 @@ def rank_program(g, core, T, topo):
 
     def mm(o, l, r, start=False, stop=False):
         c = max(min(64, width(l)), width(r)) * 0.00083 * (4 if TILES[r[0]][2] == "float32" else 1)
-        emit("t", lambda: g.tensor.matmul(ap(o), ap(l), ap(r), start, stop), [o], [l, r], cost=c)
+        emit("t", lambda: g.tensor.matmul(ap(o), ap(l), ap(r), start, stop), [o], [l, r], cost=c,
+             adds=None if start or stop else opened[o[0]])
+        if start:
+            opened[o[0]] = len(ops) - 1
 
     def lin(o, *terms):
         for k, (l, r) in enumerate(terms):
@@ -511,18 +523,17 @@ def rank_program(g, core, T, topo):
         ts(v("TRI"), v("CIO"), paf, A.is_ge, 8192.0, A.mult)
         ts(v("BO"), v("ROWI", 0, 128), 1.0 / 16, A.mult, -0.46875, A.add)
         ts(v("BLK"), v("BO"), pgf, A.is_equal)
-        ts(dump, pa, 4096.0, A.add)
-        ts(dumpk, pa, 2048.0, A.add)
-        tc(v("RD"), v("RZ", 0, 128))
-        ts(v("RD", 15, 128, 16), v("RZ", 15, 128, 16), dump, A.mult)
+        ts(dump, pa, 2.0, A.mult, 4096.0, A.add)
+        ts(dumpk, pa, 2.0, A.mult, 2048.0, A.add)
+        ts(f[11], pa, 4128.0, A.add)
+        ts(S("spare"), B8, 16.0, A.mult, f[11], A.add)
         ts(S("wt", 0, 1), v("WT"), 1.0, A.mult)
         ts(v("BW", 24, 32), B8, pgf, A.is_equal, S("wt", 0, 1), A.mult)
         ts(S("cvf"), B8, pgf, A.is_equal)
-        ts(v("BLF"), v("BO"), pgf, A.is_equal)
         for p in range(2, SH):
             ms(row("BR", p), 0.0)
         ts(S("V00", 8, 16), v("VI", 0, 8), dump, A.subtract)
-        ts(dk4, pa, 4096.0, A.mult)
+        ts(dk4, pa, 8192.0, A.mult)
         ms(v("CJ", 24, 32), 64.0 * 8)
         act(v("P8"), v("PP"), AF.Copy, bias=8.0, scale=8.0)
         bits(k[6], pi, 0, 31)
@@ -586,34 +597,37 @@ def rank_program(g, core, T, topo):
             act(seg("RS", b), seg(R, b, -1), AF.Identity, bias=col(S("b25"), b), scale=-2.0 ** 25)
         boost[0] = 0.0
 
-    def to_lists(out, src, bank):
-        act(v("SK"), ind(src, v("LS")), AF.Copy)
+    def to_lists(out, src, bank, one, two):
+        boost[0] = TB
+        act(v(one), ind(src, v("LS")), AF.Copy)
         for e in range(8):
-            mm(v(bank, e, 288, 8), v("C2", 128 - 16 * e, 256 - 16 * e), v("SK", e, 288, 8), True, True)
-        act(v("SO"), v(bank, 0, 288), AF.Copy)
-        act(out, ind(v("SO"), v("LU")), AF.Copy)
+            mm(v(bank, e, 288, 8), v("C2", 128 - 16 * e, 256 - 16 * e), v(one, e, 288, 8), True, True)
+        act(v(two), v(bank, 0, 288), AF.Copy)
+        act(out, ind(v(two), v("LU")), AF.Copy)
+        boost[0] = 0.0
 
     xwin = v("X")
 
-    def winners(key, on_scalar):
+    def winners(key, bank):
         mm(v("pT", 128, 256), ID, v("TRI"), True, False)
-        if on_scalar:
-            for b in range(8):
-                act(v("EXF", 16 * b, 16 * b + 16), v("DG", 0, 16), AF.Copy, scale=col(key, b))
-            mm(v("pT", 128, 256), v("BLF"), v("EXF"), False, True)
-        else:
-            tt(v("EXH"), ind(key, v("XL")), DG, A.mult)
-            mm(v("pT", 128, 256), v("BLK"), v("EXH"), False, True)
+        tt(v("EXH"), ind(key, v("XL")), DG, A.mult)
+        mm(v("pT", 128, 256), v("BLK"), v("EXH"), False, True)
+        mm(v("pT", 256, 384), v("BLK"), v("EXH"), True, True)
         act(v("EXR"), ind(key, v("XL")), AF.Copy)
-        tt(v("EQ"), v("EXR"), v("pT", 128, 256), A.is_equal)
+        tt(v("EQ", 0, 128), v("EXR"), v("pT", 128, 256), A.is_equal)
+        for s in range(1, NB):
+            tt(v("EQ", 144 * s, 128 * s + 128), v("EXR", 16 * s, 128), v("pT", 256, 384 - 16 * s), A.is_equal)
+        for s in range(NB):
+            mm(v(bank, 384 + 16 * s, 512), v("I22"), v("EQ", 144 * s, 128 * s + 128), s == 0, s == NB - 1)
         act(S("bd"), key, AF.Copy, bias=2048.0)
-        scan(v("EC"), v("RD"), v("EQ"), A.mult, A.max)
-        tt(S("of"), v("EC", 15, 128, 16), S("bd"), A.max)
-        tc(v("OF", 0, 16, 2), S("of"))
+        scan(v("EC"), v("RZ", 0, 128), v(bank, 384, 512), A.mult, A.max)
+        tt(S("ec"), v("EC", 15, 128, 16), S("spare"), A.min)
+        tt(S("of"), S("ec"), S("bd"), A.max)
+        tc(v("OF", 0, 8), S("of"))
 
     def put(src):
-        for b in range(7, -1, -1):
-            tc(ind(xwin, v("OF", 2 * b, 2 * b + 1)), v(src, 16 * b, 16 * b + 16))
+        for b in range(8 - NB, -1, -NB):
+            tc(ind(xwin, v("OF", b, b + NB)), v(src, 16 * b, 16 * (b + NB)))
 
     def step(t):
         P = 32 + t
@@ -708,15 +722,15 @@ def rank_program(g, core, T, topo):
         mm(v("pT", 0, 32), v("EXB"), v("CV"), False, True)
         tc(v("JL"), v("pT", 0, 24))
         jk = v("JL", 0, 8)
-        act(v("GA"), ind(v("XV", 128, G * 128 + 128), jk), AF.Copy, scale=2.0)
-        tt(v("GB"), ind(v("T1", 0, G * 128), jk), v("GA"), A.subtract)
-        tt(v("GC"), ind(v("XV", 0, G * 128), jk), v("GB"), A.subtract)
+        act(v("GA"), ind(v("XV", 128, G * 128 + 128), jk), AF.Copy)
+        tc(v("GB"), ind(v("T1", 0, G * 128), jk))
+        tc(v("GC"), ind(v("XV", 0, G * 128), jk))
         Y = v(YR, 0, 128)
-        ts(Y, v("GC"), 0.0, A.max, 63.0, A.min)
         boost[0] = YB
-        for q in range(YC):
-            mm(v("pY", q * 128, q * 128 + 128), v("IDH"), Y, True, True)
+        lin(v("pT", 128, 256), (v("IDM"), v("GB")), (ID, v("GA")), (v("IDH"), v("GC")))
+        ts(v("pY", 0, 128), v("pT", 128, 256), 0.0, A.max, 31.5, A.min)
         boost[0] = 0.0
+        ts(Y, v("pY", 0, 128), 2.0, A.mult)
         ts(J("kk"), row("KS", 0), 31, A.bitwise_and)
         ts(S("nk"), J("kk"), -1.0, A.mult)
         act(S("jw"), v("pT", 24, 32), AF.Copy)
@@ -726,7 +740,9 @@ def rank_program(g, core, T, topo):
         act(v("CM"), v("Q"), AF.Relu, bias=2.0, scale=-1.0)
         RK = v(YR, 128, 128 + NL)
         act(RK, v("Q"), AF.Relu, bias=-1.0)
+        boost[0] = EARLY
         send(YR, LY, 128 + NL, "ay%d" % t, to)
+        boost[0] = 0.0
         lin(v("pR", 0, NL), (ID, v("P32")), (ID, RK))
         act(v("PL"), v("pR", 0, NL), AF.Copy)
 
@@ -765,11 +781,13 @@ def rank_program(g, core, T, topo):
         scan(v("FS"), v("pD", 0, NL), v("PL"), A.min, A.max)
         tt(v("EXH"), ind(v("FS"), v("XF")), DG, A.mult)
         mm(v("pT", 0, 16), v("EXH"), v("CVH"), True, True)
+        behind["t"] = len(ops) - 1
         tc(J("vm", 0, 16), v("pT", 0, 16))
         ts(v(M, 0, 16), J("vm", 0, 16), 31, A.bitwise_and)
         ts(v(M, 16, 24), row("FS", 0), 31, A.bitwise_and)
         send(M, LM, 40, "am%d" % t, to)
         tc(S3("sz"), v(M, 0, 24))
+        ts(S("no"), v("pT", 0, 8), 2048.0, A.is_ge)
         if CLV:
             ts(S3("cl"), v(M, 0, 24), 1.0, A.min)
         else:
@@ -785,13 +803,14 @@ def rank_program(g, core, T, topo):
         tt(J("h0"), J("us"), S("v37"), A.add)
         ts(J("h"), J("h0"), 4095, A.bitwise_and)
         ts(S("hd"), J("h"), dump, A.subtract)
+        tt(S("hl"), S("hd"), S("L"), A.mult)
         boost[0] = 0.0
-        tt(S("hg"), S("hd"), S("gr"), A.mult)
+        tt(S("hg"), S("hl"), S("no"), A.mult)
         if KV:
             ts(S("kg"), S("hg"), dumpk, A.add)
         else:
             act(S("kg"), S("hg"), AF.Identity, bias=dumpk)
-        winners(S("kg"), GS)
+        winners(S("kg"), "pD")
         put(YR)
 
         act(S("z0"), S("vk"), AF.Copy, bias=float(-BIG), scale=4096.0)
@@ -867,9 +886,9 @@ def rank_program(g, core, T, topo):
         if t < ST - 1:
             lin(v("pD", 0, NL), (ID, v(LY, 128, 128 + NL)), (IDN, v(R, 0, NL)))
         else:
-            to_lists(v("RTI"), v(LY, 128, 128 + NL), "pK")
+            to_lists(v("RTI"), v(LY, 128, 128 + NL), "pK", "F0", "F1")
             act(v(Rn, 0, NL), v("pR", 0, NL), AF.Copy)
-            to_lists(v("RT4"), v(Rn, 0, NL), "pD")
+            to_lists(v("RT4"), v(Rn, 0, NL), "pR", "SK", "SO")
         act(v("pK", 320, 448), v(LY, 0, 128), AF.Copy, bias=-0.25, scale=0.5)
         tt(S("has"), S("n%d" % t), v(LW, m8, m8 + 8), A.min)
         tt(S("hv"), S("has"), S(V0, 8, 16), A.mult)
@@ -879,7 +898,7 @@ def rank_program(g, core, T, topo):
         tt(S2("kd"), S2("tk"), S2("dl"), A.mult)
         tt(S2(V0n), S2("kd"), S2(V0), A.add)
         ts(v("OG"), S(V0n), 2048.0, A.add)
-        winners(S(V0n), False)
+        winners(S(V0n), "pC")
         act(v("GX"), ind(xwin, v("OG")), AF.Copy, scale=0.5)
         for b in range(8):
             act(v("WA" if PEADD else "pK", b, m8, 8), v("DW", b, m8, 8), AF.Copy, scale=col(S("tk"), b))
@@ -927,9 +946,12 @@ def rank_program(g, core, T, topo):
             lin(bit, (v("I128"), v("ONES", lo, 288)), (ID, v("F%d" % i, lo, 288)), (v("N2"), v("F%d" % (i + 1), lo, 288)))
         else:
             lin(bit, (v("N128"), v("ONES", lo, 288)), (ID, v("F%d" % i, lo, 288)))
-        tt(v("pA", lo, 288), v("UF", lo, 288), bit, A.mult)
-        tt(v("UF", lo, 288), v("UF", lo, 288), v("pA", lo, 288), A.subtract)
-        tt(v("UF", 0, w), v("UF", 0, w), v("pA", lo, 288), A.add)
+        for h in range(CS if i < 5 else 1):
+            st = CS if i < 5 else 1
+            up = v("pA", lo + h, 288, st)
+            tt(up, v("UF", lo + h, 288, st), v(bit[0], lo + h, 288, st), A.mult)
+            tt(v("UF", lo + h, 288, st), v("UF", lo + h, 288, st), up, A.subtract)
+            tt(v("UF", h, w, st), v("UF", h, w, st), up, A.add)
     act(v("UF", 256, 384), v("UF", 0, 128), AF.Copy)
     act(v("NB", 0, 8), SL("n4"), AF.Copy)
     mm(v("pD", 0, 128, 1, 0, 8), v("NB", 0, 8), ID, True, True)

@@ -1,6 +1,4 @@
-import numpy as np
-import comms_topo
-from concourse.mybir import dt, AluOpType, AxisListType, ActivationFunctionType
+from concourse.mybir import AluOpType, ActivationFunctionType
 
 A = AluOpType
 AF = ActivationFunctionType
@@ -8,40 +6,27 @@ N = 6
 ST = 4
 BIG = 16777216
 NX = 4256
-NB = 8
+NB = 4
 SG = 37
 NL = 8 * SG
-SLACK = 0.05
-WAIT = 10.0
-TTG = 1.56
-LAT = 0.18
-FLY = 3.0
-KV = False
-GD = (3,)
-ZV = (0, 1, 2, 3)
-CLV = True
-EARLY = 4.0
-PASSES = 40
-SHAKE = 0.3
-ORDER = []
-SH = 8
-SW = 2
-YC = 1
-CS = 4
-TB = 1.0
-PEADD = 0
-GS = False
-UB = 0.0
-HB = 0.0
-YB = 1.0
-VOWN = (0,)
-WAYS = "YXYZYZYXZ"
-SIZES = (2, 4, 4, 4, 4, 4, 4, 4, 2)
-GROW = 0
-MASKAT = 5
+SIZES = (3, 4, 4, 4, 4, 4, 4, 4, 1)
+WAYS = "YXYYXYYXY"
 VCUT = (1, 2, 3, 5, 7, 8)
-TCUT = (1, 2, 3, 5, 7, 8)
 LCUT = 12
+SH = 10
+SW = 3
+CS = 4
+LAT = 0.2
+FLY = 1.0
+PEF = 0.8
+SLACK = 0.05
+EARLY = 8.0
+UB = 5.0
+VB = 2.0
+RB = 1.0
+PASSES = 300
+SHAKE = 1.5
+ORDER = []
 
 SCRATCH = {}
 TILES = {}
@@ -62,14 +47,14 @@ def _add(where, dtype, names, cols, rows=128):
 _add("sbuf", "bfloat16", "X", NX)
 _add("sbuf", "bfloat16", "XV T1 D AB", 4480)
 _add("sbuf", "int32", "W0 W1 W2 W3 W4 LW0 LW1 LW2 LW3 KS FS", 296)
-_add("sbuf", "int32", "VI CI DLT BIT", 288)
+_add("sbuf", "int32", "VI CI", 288)
 _add("sbuf", "uint16", "VL CL", 288)
 _add("sbuf", "bfloat16", "R0 R1 R2 R3 R4", 298)
-_add("sbuf", "bfloat16", "Q NF QT DM CM S1 A1 B1 TDR RS P32 BR ONES", 296)
+_add("sbuf", "bfloat16", "Q NF QT DM CM A1 B1 TDR RS P32 BR ONES", 296)
 _add("sbuf", "bfloat16", "SEG THX", 296, 64)
 _add("sbuf", "float32", "PL SEGI", 296)
-_add("sbuf", "bfloat16", "PP SP G1 ZS SK SO RT4 RTI F0 F1 F2 F3 F4 F5", 288)
-_add("sbuf", "float32", "POS P8 OA ZM WA DW U RT", 288)
+_add("sbuf", "bfloat16", "PP SP G1 ZS SK SO RT4 F0 F1 F2 F3 F4 F5", 288)
+_add("sbuf", "float32", "P8 ZM WA DW RT", 288)
 _add("sbuf", "float32", "UF", 384)
 _add("sbuf", "float32", "TAB", 512)
 _add("sbuf", "uint16", "JL", 24)
@@ -84,7 +69,7 @@ _add("sbuf", "float32", "SM", 1920)
 _add("sbuf", "int32", "SI", 480)
 _add("sbuf", "float32", "ROWI", 256)
 _add("sbuf", "bfloat16", "C2 RZ DG2", 256)
-_add("sbuf", "bfloat16", "ID IDN I128 N128 N2 I22 N22 I21 IDH IDM DG TRI EXB GA GB GC GX NB IDQ", 128)
+_add("sbuf", "bfloat16", "ID IDN I128 N128 N2 I22 N22 I21 IDH IDM DG TRI EXB GA GB GC GX NB", 128)
 _add("sbuf", "float16", "BLK EXH", 128)
 _add("sbuf", "float16", "CVH", 16)
 _add("sbuf", "bfloat16", "BW CV", 32)
@@ -226,13 +211,7 @@ def rank_program(g, core, T, topo):
                         if best is None or t0 < best[0]:
                             best = (t0, e)
                 t0, e = best
-                now = [i for i in ready[e] if avail[i] <= t0 + SLACK]
-                i = max(now, key=lambda i: (pri[i], -i))
-                j = max((j for j in ready[e] if avail[j] <= t0 + ops[i][7]), key=lambda j: (pri[j] - avail[j], -j), default=i)
-                gap = avail[j] - t0
-                if gap > SLACK and max(gap + pri[j], gap + ops[j][7] + pri[i]) + WAIT < max(pri[i], ops[i][7] + pri[j]):
-                    fits = [k for k in now if ops[k][7] <= gap + SLACK]
-                    i = max(fits, key=lambda k: (pri[k], -k)) if fits else j
+                i = max((i for i in ready[e] if avail[i] <= t0 + SLACK), key=lambda i: (pri[i], -i))
                 ready[e].remove(i)
                 end[i] = max(t0, avail[i]) + ops[i][7]
                 if e != "x":
@@ -252,14 +231,19 @@ def rank_program(g, core, T, topo):
         for k in range(PASSES):
             order, end = run(succ, pred, pri, [0.0] * n)
             span = max(end[i] + ops[i][8] for i in range(n))
-            if best is None or span < best[0]:
-                best = (span, order, end)
-            end = list(best[2])
-            for i in range(n if k else 0):
-                z = (z * 1103515245 + 12345) % 2147483648
-                end[i] += SHAKE * (z / 2147483648.0 - 0.5)
-            pri = run(pred, succ, end, [o[8] for o in ops])[1]
-            pri = [pri[i] + extra.get(i, 0.0) for i in range(n)]
+            if best is None or span <= best[0]:
+                best = (span, order, end, pri)
+            if k == 0:
+                pri = run(pred, succ, end, [o[8] for o in ops])[1]
+                pri = [pri[i] + extra.get(i, 0.0) for i in range(n)]
+                continue
+            z = (z * 1103515245 + 12345) % 2147483648
+            t0 = z / 2147483648.0 * best[0]
+            pri = list(best[3])
+            for i in range(n):
+                if t0 <= best[2][i] < t0 + 3.0:
+                    z = (z * 1103515245 + 12345) % 2147483648
+                    pri[i] += SHAKE * (z / 2147483648.0 - 0.5)
         return best[1]
 
     def issue(eng, call, writes, reads, tok=None, inc=1, note=True):
@@ -345,7 +329,7 @@ def rank_program(g, core, T, topo):
 
     def tt(o, x, y, op):
         emit("v", lambda: g.vector.tensor_tensor(ap(o), ap(x), ap(y), op), [o], [x, y],
-             cost=us(o, [x, y], 1 if "p" in (x[0][0], y[0][0]) else 2, gather=TTG))
+             cost=us(o, [x, y], 1 if "p" in (x[0][0], y[0][0]) else 2))
 
     def ts(o, x, s1, op0, s2=None, op1=None):
         r = [x] + [s for s in (s1, s2) if isinstance(s, tuple)]
@@ -375,7 +359,7 @@ def rank_program(g, core, T, topo):
             emit("a", lambda: g.scalar.activation(ap(o), ap(x), f, bias=sc(bias), scale=sc(scale)), [o], r, cost=c)
 
     def mm(o, l, r, start=False, stop=False):
-        c = max(min(64, width(l)), width(r)) * 0.00083 * (4 if TILES[r[0]][2] == "float32" else 1)
+        c = max(min(64, width(l)), width(r)) * 0.00083 * (4 if TILES[r[0]][2] == "float32" else 1) * PEF
         emit("t", lambda: g.tensor.matmul(ap(o), ap(l), ap(r), start, stop), [o], [l, r], cost=c,
              adds=None if start or stop else opened[o[0]])
         if start:
@@ -436,7 +420,7 @@ def rank_program(g, core, T, topo):
         o, i = v(dst, 0, width), v(src, 0, width)
         emit("p", lambda: g.remote_dma(ap(o), ap(i), T.sem[sem], T.sem.ls, pid, rid, m), [], [i], note=False, cost=0.6)
         cnt["ls"] += len(topo.engines(core, to))
-        ops.append(("x", None, [], [], None, 0, False, 0.0, 0.0, {len(ops) - 1: FLY + width / 100.0}))
+        ops.append(("x", None, [], [], None, 0, False, 0.0, 0.0, {len(ops) - 1: FLY + width * (2 if TILES[src][2] == "bfloat16" else 4) / 400.0}))
         dacc[dst].append((len(ops) - 1, o, True))
 
     ID, IDN, DG = v("ID"), v("IDN"), v("DG")
@@ -461,7 +445,6 @@ def rank_program(g, core, T, topo):
     iota(v("R0", 0, NL), [[0, 8], [-1, SG]], SG - 1, 0)
     iota(v("QT"), [[0, 8], [32, SG]], 27 * 32, 0)
     iota(v("SEGI"), [[1, 8], [0, SG]], 0, 0)
-    iota(v("POS"), [[1, 288]], 0, 0)
     iota(v("P32"), [[0, 8], [-32, SG]], 32 * (SG - 1), 0)
     iota(v("CJ", 0, 8), [[16, 8]], 63 * 128, 0)
     iota(v("CJ", 8, 24), [[1, 16]], 63 * 8, 0)
@@ -519,7 +502,7 @@ def rank_program(g, core, T, topo):
             ms(v(nm, 0, NL, SG), 0.0)
         ts(v("CJ", 0, 8), v("CJ", 0, 8), paf, A.add)
         ts(v("XF"), B8, float(SG), A.mult, float(SG - 1), A.add)
-        ts(v("BR"), v("SEGI"), pgf, A.is_equal, -2048.0, A.mult)
+        ts(v("BR"), v("SEGI"), pgf, A.is_equal, -4096.0, A.mult)
         ts(v("TRI"), v("CIO"), paf, A.is_ge, 8192.0, A.mult)
         ts(v("BO"), v("ROWI", 0, 128), 1.0 / 16, A.mult, -0.46875, A.add)
         ts(v("BLK"), v("BO"), pgf, A.is_equal)
@@ -577,9 +560,8 @@ def rank_program(g, core, T, topo):
             tp(v("TAB", s * 256 + w * 128, s * 256 + w * 128 + 128), v("RT", 32 * w + s, 32 * w + 256, 2))
     tc(v("W0", 0, 256), ind(v("TAB"), v("LI")))
 
-    def lists(t):
+    def lists(t, W):
         P = 32 + t
-        W = "W%d" % t
         for r0, r1 in ((0, LCUT), (LCUT, P)):
             bits(v("VI", r0 * 8, r1 * 8), v(W, r0 * 8, r1 * 8), 12, 4095)
             tc(v("VL", r0 * 8, r1 * 8), v("VI", r0 * 8, r1 * 8))
@@ -598,13 +580,11 @@ def rank_program(g, core, T, topo):
         boost[0] = 0.0
 
     def to_lists(out, src, bank, one, two):
-        boost[0] = TB
         act(v(one), ind(src, v("LS")), AF.Copy)
         for e in range(8):
             mm(v(bank, e, 288, 8), v("C2", 128 - 16 * e, 256 - 16 * e), v(one, e, 288, 8), True, True)
         act(v(two), v(bank, 0, 288), AF.Copy)
         act(out, ind(v(two), v("LU")), AF.Copy)
-        boost[0] = 0.0
 
     xwin = v("X")
 
@@ -639,7 +619,8 @@ def rank_program(g, core, T, topo):
         d = 1 + t % 5
         to, fr = T.cores[(rank + d) % N], T.cores[(rank - d) % N]
         ne = len(topo.engines(fr, core))
-        for buf, sem, wd in ((LW, "aw", m8 + 8), (LY, "ay", 128 + NL), (LM, "am", 40)):
+        wy = 128 + (NL if t < ST - 1 else 288)
+        for buf, sem, wd in ((LW, "aw", m8 + 8), (LY, "ay", wy), (LM, "am", 40)):
             record((sem + str(t), ne), [v(buf, 0, wd)], [], {})
 
         def rows(nm, r0, r1):
@@ -647,11 +628,10 @@ def rank_program(g, core, T, topo):
 
         size = list(SIZES)
         size[-2] -= max(0, 32 - G)
-        size[GROW] += max(0, G - 32)
+        size[0] += max(0, G - 32)
         cut = [sum(size[:c]) for c in range(len(size) + 1)]
         vcut = [0] + [cut[c] + 1 for c in VCUT] + [P]
-        tcut = [0] + [cut[c] for c in TCUT] + [G]
-        banks = ("pA", "pB", "pC", "pY")
+        banks = ("pA", "pB", "pC", "pY", "pT")
         boost[0] = EARLY
         ts(S3("L64"), n, 4.0, A.is_ge, 64.0, A.mult)
         act(S3("L"), S3("L64"), AF.Copy, scale=1.0 / 64)
@@ -661,23 +641,20 @@ def rank_program(g, core, T, topo):
         tt(S3("thr"), n, S3("L64"), A.max)
         mm(v("pK", 0, NL), ID, v("QT"), True, False)
         mm(v("pD", 0, NL), v("ONES", 0, 128, 1, 0, 64), v("THX"), True, False)
-        gv = gt = 0
+        gv = 0
         for c, (r0, r1) in enumerate(zip(cut, cut[1:])):
             while vcut[gv] < r1 + 1:
                 a0, a1 = vcut[gv], vcut[gv + 1]
-                if gv in VOWN:
+                if gv == 0:
                     ts(rows("XV", a0, a1), ind(v("X", 0, 4096), v("VL", a0 * 8, a1 * 8)), 0.5, A.mult)
                     after("gt")
                 else:
                     act(rows("XV", a0, a1), ind(v("X", 0, 4096), v("VL", a0 * 8, a1 * 8)), AF.Copy, scale=0.5)
                     after("gv")
                 gv += 1
-            while tcut[gt] < r1:
-                a0, a1 = tcut[gt], tcut[gt + 1]
-                tt(rows("T1", a0, a1), ind(v("X", 0, 4096), v("CL", a0 * 8, a1 * 8)), rows("XV", a0, a1), A.subtract)
-                after("gt")
-                gt += 1
-            way, bank = WAYS[c], v(banks[c % 4], 0, (r1 - r0) * 128)
+            tt(rows("T1", r0, r1), ind(v("X", 0, 4096), v("CL", r0 * 8, r1 * 8)), rows("XV", r0, r1), A.subtract)
+            after("gt")
+            way, bank = WAYS[c], v(banks[c % 5], 0, (r1 - r0) * 128)
             nxt, own, ab = rows("XV", r0 + 1, r1 + 1), rows("T1", r0, r1), rows("AB", r0, r1)
             if way == "Y":
                 lin(bank, (IDN, nxt), (ID, own))
@@ -695,12 +672,9 @@ def rank_program(g, core, T, topo):
                     mm(row("pK", r), rows("T1", r, r + 1), v("BW", 8, 16))
             for r in range(r0, r1):
                 mm(row("pK", r), rows("AB", r, r + 1), v("BW", 0, 8) if way == "X" else v("BW", 16, 24), False, r == G - 1)
-            if c == MASKAT:
+            if c == 5:
                 mm(v("pK", 0, NL), ID, v(R, 0, NL))
                 mm(v("pK", 1, NL), v("N22"), v("NF", 0, NL - 1))
-        while gv < len(vcut) - 1:
-            act(rows("XV", vcut[gv], vcut[gv + 1]), ind(v("X", 0, 4096), v("VL", vcut[gv] * 8, vcut[gv + 1] * 8)), AF.Copy, scale=0.5)
-            gv += 1
         for r in range(SH, P):
             mm(row("pD", r), rows("XV", r, r + 1), v("BW", 8, 16))
         shared = [(r, min(r + SW, SH)) for r in range(2, SH, SW)]
@@ -726,22 +700,23 @@ def rank_program(g, core, T, topo):
         tc(v("GB"), ind(v("T1", 0, G * 128), jk))
         tc(v("GC"), ind(v("XV", 0, G * 128), jk))
         Y = v(YR, 0, 128)
-        boost[0] = YB
         lin(v("pT", 128, 256), (v("IDM"), v("GB")), (ID, v("GA")), (v("IDH"), v("GC")))
         ts(v("pY", 0, 128), v("pT", 128, 256), 0.0, A.max, 31.5, A.min)
-        boost[0] = 0.0
-        ts(Y, v("pY", 0, 128), 2.0, A.mult)
+        ts(v("GA"), v("pT", 128, 256), 0.0, A.max, 31.5, A.min)
+        act(Y, v("GA"), AF.Copy, scale=2.0)
         ts(J("kk"), row("KS", 0), 31, A.bitwise_and)
         ts(S("nk"), J("kk"), -1.0, A.mult)
         act(S("jw"), v("pT", 24, 32), AF.Copy)
-        act(S("jb"), v("pT", 8, 16), AF.Copy, bias=-0.5, scale=-1.0)
+        act(S("jb"), v("pT", 24, 32), AF.Copy, bias=-0.5, scale=-1.0)
         for b in range(8):
             act(seg("Q", b), seg(R, b), AF.Relu, bias=col(S("nk"), b))
         act(v("CM"), v("Q"), AF.Relu, bias=2.0, scale=-1.0)
-        RK = v(YR, 128, 128 + NL)
+        RK = v(YR, 128, 128 + NL) if t < ST - 1 else v("TDR")
         act(RK, v("Q"), AF.Relu, bias=-1.0)
-        boost[0] = EARLY
-        send(YR, LY, 128 + NL, "ay%d" % t, to)
+        if t == ST - 1:
+            to_lists(v(YR, 128, 416), RK, "pK", "F0", "F1")
+        boost[0] = EARLY if t < ST - 1 else 0.0
+        send(YR, LY, wy, "ay%d" % t, to)
         boost[0] = 0.0
         lin(v("pR", 0, NL), (ID, v("P32")), (ID, RK))
         act(v("PL"), v("pR", 0, NL), AF.Copy)
@@ -753,31 +728,23 @@ def rank_program(g, core, T, topo):
             act(v("EXF", 16 * b, 16 * b + 16), v("DG", 0, 16), AF.Copy, scale=col(S("ul"), b))
         mm(v("pK", 8, 16), v("EXF"), S("cvf"), True, True)
         boost[0] = 0.0
-        mm(v("pD", 0, NL), Y, v("BR"))
+        mm(v("pD", 0, NL), v("GA"), v("BR"))
         mm(v("pD", 0, NL), v("I22"), v("CM"))
         for c, r in enumerate(range(SH, P, 2)):
-            for r1 in range(r, min(r + 2, P), YC):
-                e = min(r1 + YC, P)
-                tt(rows("AB", r1, e), rows("XV", r1, e), v("pY", 0, (e - r1) * 128), A.max)
+            for q in range(r, min(r + 2, P)):
+                tt(rows("AB", q, q + 1), rows("XV", q, q + 1), v("pY", 0, 128), A.max)
             if c % 3 == 0 and c // 3 < len(shared):
                 r0, r1 = shared[c // 3]
                 for q in range(r1 - r0):
-                    mm(v(banks[c // 3], 128 * q, 128 * q + 128), v("IDM"), Y, False, q == r1 - r0 - 1)
+                    mm(v(banks[c // 3], 128 * q, 128 * q + 128), IDN, v("GA"), False, q == r1 - r0 - 1)
                 act(rows("AB", r0, r1), v(banks[c // 3], 0, (r1 - r0) * 128), AF.Abs)
             if c % 3 == 2 and c // 3 < len(shared):
                 for q in range(*shared[c // 3]):
                     mm(row("pD", q), rows("AB", q, q + 1), v("BW", 16, 24))
             for q in range(r, min(r + 2, P)):
                 mm(row("pD", q), rows("AB", q, q + 1), v("BW", 0, 8), False, q == P - 1)
-        tt(v("GV"), ind(v(W, 0, n8), v("JL", 8, 24)), v("DG2"), A.mult)
-        scan(v("SC"), v("RZ"), v("GV"), A.mult, A.add)
-        bits(J("vk", 0, 16), v("SC", 15, 256, 16), 12, 4095)
-        vk, vk1, wk = J("vk"), J("vk", 8, 16), v("SC", 15, 128, 16)
-        ts(v(M, 24, 32), vk1, -2048.0, A.add)
-        ts(v(M, 32, 40), vk1, dump, A.subtract)
-        tc(S("vk"), vk)
-        for b in range(0 if t in GD else 8):
-            act(v("SP", b, m8, 8), v("POS", b, m8, 8), AF.Sign, bias=col(S("jb"), b))
+        for b in range(8):
+            act(v("SP", b, m8, 8), v("P8", b, m8, 8), AF.Sign, bias=col(S("jb"), b))
         scan(v("FS"), v("pD", 0, NL), v("PL"), A.min, A.max)
         tt(v("EXH"), ind(v("FS"), v("XF")), DG, A.mult)
         mm(v("pT", 0, 16), v("EXH"), v("CVH"), True, True)
@@ -785,16 +752,21 @@ def rank_program(g, core, T, topo):
         tc(J("vm", 0, 16), v("pT", 0, 16))
         ts(v(M, 0, 16), J("vm", 0, 16), 31, A.bitwise_and)
         ts(v(M, 16, 24), row("FS", 0), 31, A.bitwise_and)
+        tt(v("GV"), ind(v(W, 0, n8), v("JL", 8, 24)), v("DG2"), A.mult)
+        boost[0] = VB
+        scan(v("SC"), v("RZ"), v("GV"), A.mult, A.add)
+        boost[0] = 0.0
+        bits(J("vk", 0, 16), v("SC", 15, 256, 16), 12, 4095)
+        vk, vk1, wk = J("vk"), J("vk", 8, 16), v("SC", 15, 128, 16)
+        ts(v(M, 24, 32), vk1, -2048.0, A.add)
+        ts(v(M, 32, 40), vk1, dump, A.subtract)
+        tc(S("vk"), vk)
         send(M, LM, 40, "am%d" % t, to)
         tc(S3("sz"), v(M, 0, 24))
         ts(S("no"), v("pT", 0, 8), 2048.0, A.is_ge)
-        if CLV:
-            ts(S3("cl"), v(M, 0, 24), 1.0, A.min)
-        else:
-            act(S3("cl"), S3("sz"), AF.Sign)
+        ts(S3("cl"), v(M, 0, 24), 1.0, A.min)
         tt(S3("gr"), S3("L"), S3("cl"), A.subtract)
 
-        boost[0] = HB
         tc(J("u"), v("pK", 8, 16))
         ts(J("u2"), J("u"), 4095, A.bitwise_and)
         tt(J("uu"), J("u2"), J("u2"), A.mult)
@@ -804,12 +776,8 @@ def rank_program(g, core, T, topo):
         ts(J("h"), J("h0"), 4095, A.bitwise_and)
         ts(S("hd"), J("h"), dump, A.subtract)
         tt(S("hl"), S("hd"), S("L"), A.mult)
-        boost[0] = 0.0
         tt(S("hg"), S("hl"), S("no"), A.mult)
-        if KV:
-            ts(S("kg"), S("hg"), dumpk, A.add)
-        else:
-            act(S("kg"), S("hg"), AF.Identity, bias=dumpk)
+        ts(S("kg"), S("hg"), dumpk, A.add)
         winners(S("kg"), "pD")
         put(YR)
 
@@ -820,46 +788,23 @@ def rank_program(g, core, T, topo):
         tt(S("wn"), S("wn0"), S("wn1"), A.add)
         bits(J("pm"), J("vm"), 2, 504)
         tt(S("pz"), J("pm"), S("jw"), A.max)
-        zv = t in ZV
-        if zv:
-            for b in range(8):
-                ts(v("ZM", b, m8, 8), v("P8", b, m8, 8), col(S("pz"), b), A.is_equal, col(S("z"), b), A.mult)
-            act(v("ZS", 0, m8), v("ZM", 0, m8), AF.Sign)
-        else:
-            for b in range(8):
-                act(v("OA", b, m8, 8), v("P8", b, m8, 8), AF.Abs, bias=col(S("pz"), b), scale=-1.0)
-            act(v("ZS", 0, m8), v("OA", 0, m8), AF.Relu, bias=1.0, scale=-1.0)
-            for b in range(8):
-                act(v("ZM", b, m8, 8), v("ZS", b, m8, 8), AF.Copy, scale=col(S("z"), b))
         for b in range(8):
-            if t in GD:
-                ts(v("G1", b, m8, 8), v("P8", b, m8, 8), col(S("jw"), b), A.is_gt, col(S("gr"), b), A.mult)
-            else:
-                act(v("G1", b, m8, 8), v("SP", b, m8, 8), AF.Relu, scale=col(S("gr"), b))
+            ts(v("ZM", b, m8, 8), v("P8", b, m8, 8), col(S("pz"), b), A.is_equal, col(S("z"), b), A.mult)
+        act(v("ZS", 0, m8), v("ZM", 0, m8), AF.Sign)
+        for b in range(8):
+            act(v("G1", b, m8, 8), v("SP", b, m8, 8), AF.Relu, scale=col(S("no"), b))
         lin(v("pB", 0, m8), (ID, v("G1", 0, m8)))
         lin(v("pC", 8, m8), (ID, v("G1", 8, m8)), (IDN, v("G1", 0, n8)))
-        lin(v("pA", 0, m8), (ID, v("ONES", 0, m8)), (IDN, v("G1", 0, m8)), (ID if zv else IDN, v("ZS", 0, m8)))
-        if PEADD:
-            for b in range(8):
-                act(v("OA", 8 + b, m8, 8), v("pC", 8 + b, m8, 8), AF.Copy, scale=col(S("wn"), b))
-            mm(v("pC", 0, m8), v("IDF"), v("ZM", 0, m8), True, False)
-            mm(v("pC", 8, m8), v("IDF"), v("OA", 8, m8), False, PEADD == 1)
-            tt(v("U", 8, m8), v(W, 0, n8), v("pB", 8, m8), A.mult)
-            tt(v("WA", 0, m8), v(W, 0, m8), v("pA", 0, m8), A.mult)
-            if PEADD == 2:
-                mm(v("pC", 8, m8), v("IDF"), v("U", 8, m8), False, True)
-            else:
-                tt(v("pC", 8, m8), v("U", 8, m8), v("pC", 8, m8), A.add)
-            tt(v("pA", 0, m8), v("WA", 0, m8), v("pC", 0, m8), A.add)
-        else:
-            for b in range(8):
-                act(v("pC", 8 + b, m8, 8), v("pC", 8 + b, m8, 8), AF.Copy, scale=col(S("wn"), b))
-            tt(v("pB", 8, m8), v(W, 0, n8), v("pB", 8, m8), A.mult)
-            tt(v("ZM", 8, m8), v("ZM", 8, m8), v("pC", 8, m8), A.add)
-            tt(v("ZM", 8, m8), v("ZM", 8, m8), v("pB", 8, m8), A.add)
-            tt(v("pA", 0, m8), v(W, 0, m8), v("pA", 0, m8), A.mult)
-            tt(v("WA", 0, m8), v("ZM", 0, m8), v("pA", 0, m8), A.add)
+        lin(v("pA", 0, m8), (ID, v("ONES", 0, m8)), (IDN, v("G1", 0, m8)), (ID, v("ZS", 0, m8)))
+        for b in range(8):
+            act(v("pC", 8 + b, m8, 8), v("pC", 8 + b, m8, 8), AF.Copy, scale=col(S("wn"), b))
+        tt(v("pB", 8, m8), v(W, 0, n8), v("pB", 8, m8), A.mult)
+        tt(v("ZM", 8, m8), v("ZM", 8, m8), v("pC", 8, m8), A.add)
+        tt(v("ZM", 8, m8), v("ZM", 8, m8), v("pB", 8, m8), A.add)
+        tt(v("pA", 0, m8), v(W, 0, m8), v("pA", 0, m8), A.mult)
+        tt(v("WA", 0, m8), v("ZM", 0, m8), v("pA", 0, m8), A.add)
         tt(v("DW", 0, m8), v(LW, 0, m8), v("pA", 0, m8), A.subtract)
+        boost[0] = RB if t == ST - 1 else 0.0
         act(S("nsz"), SL("sz"), AF.Copy, scale=-1.0)
         act(S("g2"), SL("gr"), AF.Copy, bias=-2.0)
         lin(v("pY", 0, NL), (ID, v("Q")), (IDN, RK), (ID, v("NF")))
@@ -869,6 +814,7 @@ def rank_program(g, core, T, topo):
             act(seg("B1", b), seg("pY", b), AF.Relu, bias=col(S("g2"), b))
         for l, r in ((ID, v(R, 0, NL)), (IDN, v("Q")), (ID, v("A1")), (ID, v("B1"))):
             mm(v("pR", 0, NL), l, r, r[0] == R, r[0] == "B1" and t == ST - 1)
+        boost[0] = 0.0
         tt(S3("ng"), n, S3("gr"), A.add)
         ts(S3("ng"), S3("ng"), 32.0, A.min)
         tt(S3("n2"), S3("ng"), S3("sz"), A.subtract)
@@ -886,7 +832,6 @@ def rank_program(g, core, T, topo):
         if t < ST - 1:
             lin(v("pD", 0, NL), (ID, v(LY, 128, 128 + NL)), (IDN, v(R, 0, NL)))
         else:
-            to_lists(v("RTI"), v(LY, 128, 128 + NL), "pK", "F0", "F1")
             act(v(Rn, 0, NL), v("pR", 0, NL), AF.Copy)
             to_lists(v("RT4"), v(Rn, 0, NL), "pR", "SK", "SO")
         act(v("pK", 320, 448), v(LY, 0, 128), AF.Copy, bias=-0.25, scale=0.5)
@@ -901,9 +846,9 @@ def rank_program(g, core, T, topo):
         winners(S(V0n), "pC")
         act(v("GX"), ind(xwin, v("OG")), AF.Copy, scale=0.5)
         for b in range(8):
-            act(v("WA" if PEADD else "pK", b, m8, 8), v("DW", b, m8, 8), AF.Copy, scale=col(S("tk"), b))
+            act(v("pK", b, m8, 8), v("DW", b, m8, 8), AF.Copy, scale=col(S("tk"), b))
         tt(v("BO"), v("GX"), v("pK", 320, 448), A.add)
-        tt(v(Wn, 0, m8), v("WA", 0, m8), v("pA" if PEADD else "pK", 0, m8), A.add)
+        tt(v(Wn, 0, m8), v("WA", 0, m8), v("pK", 0, m8), A.add)
         put("BO")
         tt(S3("rc"), v(LM, 0, 24), S3("tk"), A.mult)
         tt(nn, S3("rc"), S3("n2"), A.max)
@@ -913,9 +858,9 @@ def rank_program(g, core, T, topo):
             mm(v("pR", 0, NL), ID, v("TDR"), False, True)
             act(v(Rn, 0, NL), v("pR", 0, NL), AF.Copy)
             masks(t + 1)
-            lists(t + 1)
+            lists(t + 1, Wn)
 
-    lists(0)
+    lists(0, "W0")
     late_constants()
     tc(v("NB", 0, 128, 1, 0, 8), v("NR"))
     mm(v("pT", 16, 24), v("NB", 0, 128, 1, 0, 8), v("ID", 0, 8, 1, 0, 8), True, True)
@@ -929,7 +874,7 @@ def rank_program(g, core, T, topo):
             last_constants()
         step(t)
 
-    lin(v("pD", 0, 288), (ID, v("RTI")), (IDN, v("RT4")))
+    lin(v("pD", 0, 288), (ID, v("LY3", 128, 416)), (IDN, v("RT4")))
     for b in range(8):
         act(v("SK", b, 288, 8), v("pD", b, 288, 8), AF.Copy, scale=col(S("tk"), b))
     lin(v("pY", 0, 288), (ID, v("PP")), (IDN, v("RT4")), (IDN, v("SK")))

from concourse.mybir import AluOpType, ActivationFunctionType

A = AluOpType
AF = ActivationFunctionType
N = 6
ST = 4
BIG = 16777216
NX = 4256
NB = 4
SG = 37
NL = 8 * SG
SIZES = (3, 4, 4, 4, 4, 4, 4, 4, 1)
WAYS = "YXYYXYYXY"
VCUT = (1, 2, 3, 5, 7, 8)
LCUT = 12
SH = 10
SW = 3
CS = 4
LAT = 0.2
FLY = 1.0
PEF = 0.8
SLACK = 0.05
EARLY = 8.0
UB = 5.0
VB = 2.0
RB = 1.0
PASSES = 300
SHAKE = 1.5
ORDER = []

SCRATCH = {}
TILES = {}


def _add(where, dtype, names, cols, rows=128):
    for nm in names.split():
        if where == "psum" or cols > 1024:
            SCRATCH[nm] = (where, [rows, cols], dtype)
            TILES[nm] = (where, [rows, cols], dtype, nm, 0)
        else:
            buf = "all_" + dtype
            at = SCRATCH[buf][1][1] if buf in SCRATCH else 0
            SCRATCH[buf] = (where, [128, at + (cols + 15) // 16 * 16], dtype)
            TILES[nm] = (where, [rows, cols], dtype, buf, at)


_add("sbuf", "bfloat16", "X", NX)
_add("sbuf", "bfloat16", "XV T1 D AB", 4480)
_add("sbuf", "int32", "W0 W1 W2 W3 W4 LW0 LW1 LW2 LW3 KS FS", 296)
_add("sbuf", "int32", "VI CI", 288)
_add("sbuf", "uint16", "VL CL", 288)
_add("sbuf", "bfloat16", "R0 R1 R2 R3 R4", 298)
_add("sbuf", "bfloat16", "Q NF QT DM CM A1 B1 TDR RS P32 BR ONES", 296)
_add("sbuf", "bfloat16", "SEG THX", 296, 64)
_add("sbuf", "float32", "PL SEGI", 296)
_add("sbuf", "bfloat16", "PP SP G1 ZS SK SO RT4 F0 F1 F2 F3 F4 F5", 288)
_add("sbuf", "float32", "P8 ZM WA DW RT", 288)
_add("sbuf", "float32", "UF", 384)
_add("sbuf", "float32", "TAB", 512)
_add("sbuf", "uint16", "JL", 24)
_add("sbuf", "uint16", "OF", 16)
_add("sbuf", "float32", "CJ", 32)
_add("sbuf", "uint16", "XL XF OG", 8)
_add("sbuf", "uint16", "LI LO", 16)
_add("sbuf", "uint16", "LS LU", 18)
_add("sbuf", "bfloat16", "YR0 YR1 YR2 YR3 LY0 LY1 LY2 LY3", 424)
_add("sbuf", "int32", "M0 M1 M2 M3 LM0 LM1 LM2 LM3", 40)
_add("sbuf", "float32", "SM", 1920)
_add("sbuf", "int32", "SI", 480)
_add("sbuf", "float32", "ROWI", 256)
_add("sbuf", "bfloat16", "C2 RZ DG2", 256)
_add("sbuf", "bfloat16", "ID IDN I128 N128 N2 I22 N22 I21 IDH IDM DG TRI EXB GA GB GC GX NB", 128)
_add("sbuf", "float16", "BLK EXH", 128)
_add("sbuf", "float16", "CVH", 16)
_add("sbuf", "bfloat16", "BW CV", 32)
_add("sbuf", "float32", "IDF EXR ONF EXF EC", 128)
_add("sbuf", "bfloat16", "EQ", 1024)
_add("sbuf", "float32", "GV", 256)
_add("sbuf", "int32", "SC VR CR OI", 256)
_add("sbuf", "int32", "BO CIO", 128)
_add("sbuf", "float32", "OV OC NM", 256)
_add("sbuf", "int32", "NR", 128, 8)
_add("sbuf", "float32", "NO", 128, 8)
_add("sbuf", "int32", "TH8", 4, 64)
_add("sbuf", "int32", "WT", 1)
_add("psum", "float32", "pA pB pC pK pD pY pT pR", 512)

SEMAPHORES = ["qv", "qa", "qt", "qp", "ls"] + ["d%d" % i for i in range(14)] + [
    m + str(t) for m in ("aw", "ay", "am") for t in range(ST)]


def rank_program(g, core, T, topo):
    rank = T.rank_of(core)
    if rank is None:
        return
    Q = {"v": g.vector, "a": g.scalar, "t": g.tensor, "p": g, "s": g.sync}
    SEM = {"v": "qv", "a": "qa", "t": "qt", "p": "qp", "s": None}
    cnt = {"qv": 0, "qa": 0, "qt": 0, "qp": 0, "ls": 0}
    clk = {e: {} for e in Q}
    acc = {n: [] for n in TILES}
    nd = [0]
    boost = [0.0]
    opened = {}
    behind = {}

    def v(name, lo=0, hi=None, step=1, p0=0, p1=None):
        sh = TILES[name][1]
        return (name, lo, sh[1] if hi is None else hi, step, p0, sh[0] if p1 is None else p1)

    def ap(w):
        if w[0] == "ind":
            return ap(w[1]).indirect(ap(w[2]))
        n, lo, hi, st, p0, p1 = w
        buf, at = TILES[n][3:]
        if st == 1:
            return T[buf][p0:p1, at + lo:at + hi]
        return T[buf][p0:p1, at + lo:at + hi:st]

    def ind(win, off):
        return ("ind", win, off)

    def meets(x, y):
        if x[1] >= y[2] or y[1] >= x[2] or x[4] >= y[5] or y[4] >= x[5]:
            return False
        if x[3] == y[3] and x[3] > 1 and (x[1] - y[1]) % x[3]:
            return False
        return True

    def covers(x, y):
        if x[3] > 1 and (x[3] != y[3] or (x[1] - y[1]) % x[3]):
            return False
        return x[1] <= y[1] and x[2] >= y[2] and x[4] <= y[4] and x[5] >= y[5]

    ops, dacc, phase, extra, chains = [], {n: [] for n in TILES}, {n: [] for n in TILES}, {}, {}

    def after(name):
        if name in chains:
            ops[-1][9].setdefault(chains[name], -ops[chains[name]][8])
        chains[name] = len(ops) - 1

    def emit(eng, call, writes, reads, tok=None, inc=1, note=True, cost=0.1, tail=0.0, adds=None):
        extra[len(ops)] = boost[0]
        ws = [w[1] if w[0] == "ind" else w for w in writes]
        rs = [w[2] for w in writes if w[0] == "ind"]
        for w in reads:
            if w[0] == "ind":
                rs.append(w[1]); rs.append(w[2])
            elif isinstance(w, tuple):
                rs.append(w)
        me, deps = len(ops), {}
        for lst, wr in ((rs, False), (ws, True)):
            for w in lst:
                psum = w[0][0] == "p"
                if not (psum and eng == "t"):
                    for (i, w2, wr2) in dacc[w[0]]:
                        if (wr or wr2) and meets(w, w2):
                            deps[i] = LAT
                if psum:
                    ph = phase[w[0]]
                    if ph and ph[-1][0] == eng:
                        prev = ph[-2][1] if len(ph) > 1 else []
                        if eng == "t":
                            for i in (ph[-1][1] if adds is None else [adds]):
                                deps[i] = 0.0
                        ph[-1][1].append(me)
                    else:
                        prev = ph[-1][1] if ph else []
                        ph.append([eng, [me]])
                    for i in prev:
                        deps[i] = LAT
        if eng in behind:
            deps.setdefault(behind[eng], 0.0)
        deps.pop(me, None)
        for w in rs:
            dacc[w[0]].append((me, w, False))
        for w in ws:
            if w[0][0] == "p" and eng == "t":
                dacc[w[0]] = []
            else:
                dacc[w[0]] = [x for x in dacc[w[0]] if not covers(w, x[1])] + [(me, w, True)]
        ops.append((eng, call, writes, reads, tok, inc, note, cost, tail, deps))

    def flush():
        if not ORDER:
            ORDER.extend(arrange())
        for i in ORDER:
            if ops[i][0] != "x":
                issue(*ops[i][:7])

    def arrange():
        n = len(ops)
        succ, pred = [[] for _ in range(n)], [[] for _ in range(n)]
        for i, o in enumerate(ops):
            for d in o[9]:
                succ[d].append((i, o[9][d] + ops[d][8]))
                pred[i].append((d, o[9][d] + ops[d][8]))

        def run(nxt, prv, pri, avail):
            left = [len(x) for x in prv]
            ready = {e: [] for e in list(Q) + ["x"]}
            for i in range(n):
                if not left[i]:
                    ready[ops[i][0]].append(i)
            free = {e: 0.0 for e in ready}
            order, end = [], [0.0] * n
            while len(order) < n:
                best = None
                for e in ready:
                    if ready[e]:
                        t0 = max(free[e], min(avail[i] for i in ready[e]))
                        if best is None or t0 < best[0]:
                            best = (t0, e)
                t0, e = best
                i = max((i for i in ready[e] if avail[i] <= t0 + SLACK), key=lambda i: (pri[i], -i))
                ready[e].remove(i)
                end[i] = max(t0, avail[i]) + ops[i][7]
                if e != "x":
                    free[e] = end[i]
                order.append(i)
                for s, l in nxt[i]:
                    avail[s] = max(avail[s], end[i] + l)
                    left[s] -= 1
                    if not left[s]:
                        ready[ops[s][0]].append(s)
            return order, end

        pri = [0.0] * n
        for i in range(n - 1, -1, -1):
            pri[i] = ops[i][7] + max([l + pri[s] for s, l in succ[i]] + [ops[i][8]]) + extra.get(i, 0.0)
        best, z = None, 1
        for k in range(PASSES):
            order, end = run(succ, pred, pri, [0.0] * n)
            span = max(end[i] + ops[i][8] for i in range(n))
            if best is None or span <= best[0]:
                best = (span, order, end, pri)
            if k == 0:
                pri = run(pred, succ, end, [o[8] for o in ops])[1]
                pri = [pri[i] + extra.get(i, 0.0) for i in range(n)]
                continue
            z = (z * 1103515245 + 12345) % 2147483648
            t0 = z / 2147483648.0 * best[0]
            pri = list(best[3])
            for i in range(n):
                if t0 <= best[2][i] < t0 + 3.0:
                    z = (z * 1103515245 + 12345) % 2147483648
                    pri[i] += SHAKE * (z / 2147483648.0 - 0.5)
        return best[1]

    def issue(eng, call, writes, reads, tok=None, inc=1, note=True):
        ws, rs = [], []
        for w in writes:
            if w[0] == "ind":
                ws.append(w[1]); rs.append(w[2])
            else:
                ws.append(w)
        for w in reads:
            if w[0] == "ind":
                rs.append(w[1]); rs.append(w[2])
            elif isinstance(w, tuple):
                rs.append(w)
        mysem = tok[0] if tok else SEM[eng]
        need = {}
        for lst, wr in ((rs, False), (ws, True)):
            for w in lst:
                psum = w[0][0] == "p"
                for (tk, w2, wr2, ck2) in acc[w[0]]:
                    same = tk[0] == mysem
                    if psum and not same:
                        hit = True
                    elif same:
                        hit = (wr or wr2) and meets(w, w2) and not (psum and eng == "t")
                    else:
                        hit = (wr or wr2) and meets(w, w2)
                    if hit and clk[eng].get(tk[0], 0) < tk[1] and need.get(tk[0], (0,))[0] < tk[1]:
                        need[tk[0]] = (tk[1], ck2)
        ck = clk[eng]
        for s in list(need):
            val, c2 = need[s]
            if any(s2 != s and need[s2][1].get(s, 0) >= val for s2 in need):
                continue
            Q[eng].wait_ge(T.sem[s], val)
            for k2 in c2:
                ck[k2] = max(ck.get(k2, 0), c2[k2])
            ck[s] = max(ck.get(s, 0), val)
        ins = call()
        if not note:
            return None
        if tok is None:
            cnt[mysem] += 1
            tok = (mysem, cnt[mysem])
        ins.then_inc(T.sem[tok[0]], inc)
        snap = dict(ck)
        snap[tok[0]] = tok[1]
        record(tok, ws, rs, snap)
        return tok

    def record(tok, ws, rs, snap):
        for w in rs:
            old = acc[w[0]]
            if w[0][0] == "p":
                old = [x for x in old if x[0][0] == tok[0]]
            acc[w[0]] = [x for x in old if not (x[0][0] == tok[0] and not x[2] and covers(w, x[1]))] + [(tok, w, False, snap)]
        for w in ws:
            old = acc[w[0]]
            if w[0][0] == "p":
                old = [x for x in old if x[0][0] == tok[0] and tok[0] != "qt"]
            acc[w[0]] = [x for x in old if not covers(w, x[1])] + [(tok, w, True, snap)]

    def sc(x):
        return ap(x) if isinstance(x, tuple) else x

    def width(w):
        if w[0] == "ind":
            return 16 * (w[2][2] - w[2][1])
        return (w[2] - w[1] + w[3] - 1) // w[3]

    def us(o, ins, rate, fix=0.0, gather=1.56):
        if o[0] == "ind":
            return 0.05 + 3.5 * width(o) * 0.00083
        if any(x[0] == "ind" for x in ins):
            return 0.05 + gather * width(o) * 0.00083
        return max(64, max(width(x) for x in ins) * rate) * 0.00083 + fix

    def small(*vs):
        return 0.5 if all(x[0] != "ind" and x[0][0] != "p" and TILES[x[0]][2] in ("bfloat16", "uint16") for x in vs) else 1

    def tc(o, i):
        emit("v", lambda: g.vector.tensor_copy(ap(o), ap(i)), [o], [i], cost=us(o, [i], small(o, i)))

    def tt(o, x, y, op):
        emit("v", lambda: g.vector.tensor_tensor(ap(o), ap(x), ap(y), op), [o], [x, y],
             cost=us(o, [x, y], 1 if "p" in (x[0][0], y[0][0]) else 2))

    def ts(o, x, s1, op0, s2=None, op1=None):
        r = [x] + [s for s in (s1, s2) if isinstance(s, tuple)]
        c = us(o, [x], small(o, x))
        if op1 is None:
            emit("v", lambda: g.vector.tensor_scalar(ap(o), ap(x), sc(s1), None, op0), [o], r, cost=c)
        else:
            emit("v", lambda: g.vector.tensor_scalar(ap(o), ap(x), sc(s1), sc(s2), op0, op1), [o], r, cost=c)

    def scan(o, x, y, op0, op1):
        emit("v", lambda: g.vector.tensor_tensor_scan(ap(o), ap(x), ap(y), 0.0, op0, op1), [o], [x, y], cost=us(o, [x, y], 1))

    def ms(o, c):
        emit("v", lambda: g.vector.memset(ap(o), c), [o], [], cost=us(o, [o], small(o)))

    def tp(o, x):
        emit("v", lambda: g.vector.transpose(ap(o), ap(x)), [o], [x], cost=us(o, [x], 1))

    def act(o, x, f, bias=None, scale=1.0, acc_out=None):
        r = [x] + [s for s in (bias, scale) if isinstance(s, tuple)]
        c = us(o, [x], 1)
        if acc_out is not None:
            emit("a", lambda: g.scalar.activation(ap(o), ap(x), f, accum_out=ap(acc_out)), [o, acc_out], r, cost=c + 0.02)
        elif bias is None:
            emit("a", lambda: g.scalar.activation(ap(o), ap(x), f, scale=sc(scale)), [o], r, cost=c)
        else:
            emit("a", lambda: g.scalar.activation(ap(o), ap(x), f, bias=sc(bias), scale=sc(scale)), [o], r, cost=c)

    def mm(o, l, r, start=False, stop=False):
        c = max(min(64, width(l)), width(r)) * 0.00083 * (4 if TILES[r[0]][2] == "float32" else 1) * PEF
        emit("t", lambda: g.tensor.matmul(ap(o), ap(l), ap(r), start, stop), [o], [l, r], cost=c,
             adds=None if start or stop else opened[o[0]])
        if start:
            opened[o[0]] = len(ops) - 1

    def lin(o, *terms):
        for k, (l, r) in enumerate(terms):
            mm(o, l, r, k == 0, k == len(terms) - 1)

    def iota(o, pat, base, cm):
        c = 0.13 + 2 * width(o) * 0.00083
        if TILES[o[0]][2] == "int32":
            emit("p", lambda: g.iota(ap(o), pat, base, cm), [o], [], cost=c)
        else:
            emit("p", lambda: g.iota(ap(o), pat, base, cm, allow_small_or_imprecise_dtypes=True), [o], [], cost=c)

    def dma(eng, out, in_, writes, reads):
        s = "d%d" % nd[0]
        nd[0] += 1
        emit(eng, lambda: Q[eng].dma_start(out, in_), writes, reads, tok=(s, 16), inc=16, cost=0.05,
             tail=2.0 + sum(width(w) for w in writes + reads) * 128 * 2 / (200e3 if writes else 150e3))
        after("dma" + eng)
        return s

    scol, jcol = {}, {}

    def S(nm, lo=0, hi=8, step=1, p0=0, p1=128):
        if nm not in scol:
            scol[nm] = 24 * len(scol)
        return v("SM", scol[nm] + lo, scol[nm] + hi, step, p0, p1)

    def J(nm, lo=0, hi=8, p0=0, p1=128):
        if nm not in jcol:
            jcol[nm] = 16 * len(jcol)
        return v("SI", jcol[nm] + lo, jcol[nm] + hi, 1, p0, p1)

    def S2(nm):
        return S(nm, 0, 16)

    def S3(nm):
        return S(nm, 0, 24)

    def SL(nm):
        return S(nm, 16, 24)

    def col(w, b):
        return (w[0], w[1] + b, w[1] + b + 1, 1, w[4], w[5])

    def seg(nm, k, off=0):
        return v(nm, off + k * SG + 1, off + k * SG + SG)

    def row(nm, p):
        return v(nm, SG - 1 - p, NL, SG)

    def send(src, dst, width, sem, to):
        rid, pid, _e = topo.addr(to)
        m = topo.mask(core, to)
        o, i = v(dst, 0, width), v(src, 0, width)
        emit("p", lambda: g.remote_dma(ap(o), ap(i), T.sem[sem], T.sem.ls, pid, rid, m), [], [i], note=False, cost=0.6)
        cnt["ls"] += len(topo.engines(core, to))
        ops.append(("x", None, [], [], None, 0, False, 0.0, 0.0, {len(ops) - 1: FLY + width * (2 if TILES[src][2] == "bfloat16" else 4) / 400.0}))
        dacc[dst].append((len(ops) - 1, o, True))

    ID, IDN, DG = v("ID"), v("IDN"), v("DG")

    boost[0] = 100.0
    ms(v("TH8"), 0)
    dma("s", ap(v("VR")), T.vl[:], [v("VR")], [])
    dma("a", ap(v("CR")), T.cl[:], [v("CR")], [])
    dma("a", ap(v("X", 2048, 4096)), T.xc[:, 2048:4096], [v("X", 2048, 4096)], [])
    dma("s", ap(v("X", 0, 2048)), T.xc[:, 0:2048], [v("X", 0, 2048)], [])
    dma("s", ap(v("NR")), T.ln[:], [v("NR")], [])
    dma("a", ap(v("WT")), T.wt[:], [v("WT")], [])
    for p0, e in ((0, "s"), (32, "a")):
        dma(e, ap(v("TH8", 0, 1, 1, p0, p0 + 8)), T.th[:], [v("TH8", 0, 4, 1, p0, p0 + 8)], [])
    boost[0] = 0.0

    pi, pg, pa = J("pi", 0, 1), J("pi", 1, 2), J("pi", 2, 3)
    iota(pi, [[1, 1]], 0, 1)
    iota(v("ROWI"), [[1, 256]], 0, 0)
    iota(J("li", 0, 16), [[256, 2], [2, 8]], 0, 0)
    iota(v("CIO"), [[0, 8], [1, 16]], 0, 0)
    iota(v("R0", 0, NL), [[0, 8], [-1, SG]], SG - 1, 0)
    iota(v("QT"), [[0, 8], [32, SG]], 27 * 32, 0)
    iota(v("SEGI"), [[1, 8], [0, SG]], 0, 0)
    iota(v("P32"), [[0, 8], [-32, SG]], 32 * (SG - 1), 0)
    iota(v("CJ", 0, 8), [[16, 8]], 63 * 128, 0)
    iota(v("CJ", 8, 24), [[1, 16]], 63 * 8, 0)
    iota(J("lo", 0, 16), [[32, 8], [8, 2]], 0, 0)
    iota(v("PP"), [[1, 36], [0, 8]], 0, 0)
    B8 = v("ROWI", 0, 8)
    ts(pg, pi, 4, A.arith_shift_right)
    ts(pa, pi, 15, A.bitwise_and)
    pf, pgf, paf, dump, dumpk, dk4, q31, is8 = [S("cols", b, b + 1) for b in range(8)]
    tc(S("cols", 0, 3), J("pi", 0, 3))

    def bits(o, x, sh, mask):
        ts(o, x, sh, A.arith_shift_right, mask, A.bitwise_and)

    k = [J("k", b, b + 1) for b in range(16)]
    f = [S("kf", b, b + 1) for b in range(16)]
    bits(k[0], pi, 4, 1)
    bits(k[1], pi, 3, 1)
    bits(k[2], pi, 0, 7)
    tt(k[3], k[2], k[0], A.subtract)
    bits(k[4], k[3], 0, 1)
    bits(k[5], k[3], 1, 3)
    ts(f[0], k[0], 16.0, A.mult)
    ts(f[1], k[4], 128.0, A.mult, f[0], A.add)
    ts(f[2], k[5], 32.0, A.mult, f[1], A.add)
    tt(f[3], f[2], k[1], A.add)
    ts(v("LI"), J("li", 0, 16), f[3], A.add)
    ts(ID, v("ROWI", 0, 128), pf, A.is_equal)
    ts(DG, v("CIO"), paf, A.is_equal)
    ts(v("XL"), B8, 1.0, A.mult)
    for t in range(ST + 1):
        ms(v("W%d" % t, 256, 296), -BIG)
        ms(v("R%d" % t, 0 if t == 0 else NL, 298, SG), -1.0)
    ms(v("X", 4096, NX), 0.0)

    def late_constants():
        for nm, w in (("IDN", -1.0), ("I22", 2.0 ** 22), ("N22", -2.0 ** 22), ("I21", 2.0 ** 21), ("IDH", 0.5),
                      ("IDM", -0.5), ("IDF", 1.0)):
            act(v(nm), ID, AF.Copy, scale=w)
        for i, w in enumerate((8192.0, -4096.0, 4096.0)):
            ts(v("BW", 8 * i, 8 * i + 8), B8, pgf, A.is_equal, w, A.mult)
        for i, w in enumerate((-128.0, -8.0, -8.0, -8.0)):
            ts(v("CV", 8 * i, 8 * i + 8), B8, pgf, A.is_equal, w, A.mult)
        for i in range(2):
            ts(v("CVH", 8 * i, 8 * i + 8), B8, pgf, A.is_equal)
        ms(v("ONES"), 1.0)
        ms(v("ONF"), 1.0)
        ms(v("RS", 0, NL, SG), -2.0 ** 25)
        ms(v("RZ"), 1.0)
        ms(v("RZ", 0, 256, 16), 0.0)
        ms(v("P32", 0, NL, SG), 2048.0)
        for q in range(2):
            act(v("DG2", 128 * q, 128 * q + 128), DG, AF.Copy)
        for nm in ("Q", "A1", "B1", "TDR", "DM"):
            ms(v(nm, 0, NL, SG), 0.0)
        ts(v("CJ", 0, 8), v("CJ", 0, 8), paf, A.add)
        ts(v("XF"), B8, float(SG), A.mult, float(SG - 1), A.add)
        ts(v("BR"), v("SEGI"), pgf, A.is_equal, -4096.0, A.mult)
        ts(v("TRI"), v("CIO"), paf, A.is_ge, 8192.0, A.mult)
        ts(v("BO"), v("ROWI", 0, 128), 1.0 / 16, A.mult, -0.46875, A.add)
        ts(v("BLK"), v("BO"), pgf, A.is_equal)
        ts(dump, pa, 2.0, A.mult, 4096.0, A.add)
        ts(dumpk, pa, 2.0, A.mult, 2048.0, A.add)
        ts(f[11], pa, 4128.0, A.add)
        ts(S("spare"), B8, 16.0, A.mult, f[11], A.add)
        ts(S("wt", 0, 1), v("WT"), 1.0, A.mult)
        ts(v("BW", 24, 32), B8, pgf, A.is_equal, S("wt", 0, 1), A.mult)
        ts(S("cvf"), B8, pgf, A.is_equal)
        for p in range(2, SH):
            ms(row("BR", p), 0.0)
        ts(S("V00", 8, 16), v("VI", 0, 8), dump, A.subtract)
        ts(dk4, pa, 8192.0, A.mult)
        ms(v("CJ", 24, 32), 64.0 * 8)
        act(v("P8"), v("PP"), AF.Copy, bias=8.0, scale=8.0)
        bits(k[6], pi, 0, 31)
        tc(q31, k[6])
        ts(is8, pi, 8.0, A.is_equal)
        ts(v("SEG"), v("SEGI", 0, NL, 1, 0, 64), S("cols", 6, 7, 1, 0, 64), A.is_equal, S("cols", 7, 8, 1, 0, 64), A.max)
        ts(v("TH8", 1, 2, 1, 0, 32), v("TH8", 0, 1, 1, 0, 32), 992, A.bitwise_and)
        ts(v("TH8", 1, 2, 1, 32, 64), v("TH8", 0, 1, 1, 32, 64), 31, A.bitwise_and)
        ts(f[4], is8, 2.0 ** 21, A.mult)
        ts(S("th", 0, 1, 1, 0, 64), v("TH8", 1, 2), -2048.0, A.mult, S("kf", 4, 5, 1, 0, 64), A.add)
        ts(S("th", 1, 2), pi, 32.0, A.is_ge, -2048.0, A.mult)
        ts(v("THX"), v("SEG"), S("th", 0, 1, 1, 0, 64), A.mult)

    def last_constants():
        bits(k[7], pi, 0, 1)
        tt(k[8], k[7], k[0], A.not_equal)
        bits(k[9], pi, 1, 7)
        ts(f[5], k[8], 256.0, A.mult, f[0], A.add)
        tt(f[6], f[5], k[9], A.add)
        ts(v("LO"), J("lo", 0, 16), f[6], A.add)
        tt(k[10], pg, k[2], A.add)
        bits(k[11], k[10], 0, 7)
        ts(f[7], k[11], float(SG), A.mult, float(SG - 1), A.add)
        tt(f[8], f[7], k[1], A.subtract)
        ts(v("LS"), v("ROWI", 0, 18), -2.0, A.mult, f[8], A.add)
        tt(k[12], pg, k[2], A.subtract)
        bits(k[13], k[12], 0, 7)
        ts(f[9], k[1], 8.0, A.mult)
        tt(f[10], f[9], k[13], A.add)
        ts(v("LU"), v("ROWI", 0, 18), 16.0, A.mult, f[10], A.add)
        for nm, w in (("I128", 160.0), ("N128", -160.0), ("N2", -2.0)):
            act(v(nm), ID, AF.Copy, scale=w)
        act(v("C2", 0, 128), ID, AF.Copy)
        act(v("C2", 128, 256), ID, AF.Copy)

    ts(v("pA", 0, 256), v("VR"), 4096.0, A.mult, float(-BIG), A.add)
    tt(v("RT", 0, 256), v("CR"), v("pA", 0, 256), A.add)
    tc(v("RT", 256, 288), v("RT", 0, 32))
    for s in range(2):
        for w in range(2):
            tp(v("TAB", s * 256 + w * 128, s * 256 + w * 128 + 128), v("RT", 32 * w + s, 32 * w + 256, 2))
    tc(v("W0", 0, 256), ind(v("TAB"), v("LI")))

    def lists(t, W):
        P = 32 + t
        for r0, r1 in ((0, LCUT), (LCUT, P)):
            bits(v("VI", r0 * 8, r1 * 8), v(W, r0 * 8, r1 * 8), 12, 4095)
            tc(v("VL", r0 * 8, r1 * 8), v("VI", r0 * 8, r1 * 8))
        for r0, r1 in ((0, LCUT), (LCUT, P - 2)):
            ts(v("CI", r0 * 8, r1 * 8), v(W, r0 * 8, r1 * 8), 4095, A.bitwise_and)
            tc(v("CL", r0 * 8, r1 * 8), v("CI", r0 * 8, r1 * 8))

    def masks(t):
        R = "R%d" % t
        lin(v("pR", 0, NL), (ID, v(R, 0, NL)), (IDN, v(R, 1, NL + 1)))
        act(S("b25"), SL("n%d" % t), AF.Copy, bias=-2.5 * 2 ** 25, scale=2.0 ** 25)
        boost[0] = EARLY
        act(v("NF"), v("pR", 0, NL), AF.Relu, bias=1.0, scale=-1.0)
        for b in range(8):
            act(seg("RS", b), seg(R, b, -1), AF.Identity, bias=col(S("b25"), b), scale=-2.0 ** 25)
        boost[0] = 0.0

    def to_lists(out, src, bank, one, two):
        act(v(one), ind(src, v("LS")), AF.Copy)
        for e in range(8):
            mm(v(bank, e, 288, 8), v("C2", 128 - 16 * e, 256 - 16 * e), v(one, e, 288, 8), True, True)
        act(v(two), v(bank, 0, 288), AF.Copy)
        act(out, ind(v(two), v("LU")), AF.Copy)

    xwin = v("X")

    def winners(key, bank):
        mm(v("pT", 128, 256), ID, v("TRI"), True, False)
        tt(v("EXH"), ind(key, v("XL")), DG, A.mult)
        mm(v("pT", 128, 256), v("BLK"), v("EXH"), False, True)
        mm(v("pT", 256, 384), v("BLK"), v("EXH"), True, True)
        act(v("EXR"), ind(key, v("XL")), AF.Copy)
        tt(v("EQ", 0, 128), v("EXR"), v("pT", 128, 256), A.is_equal)
        for s in range(1, NB):
            tt(v("EQ", 144 * s, 128 * s + 128), v("EXR", 16 * s, 128), v("pT", 256, 384 - 16 * s), A.is_equal)
        for s in range(NB):
            mm(v(bank, 384 + 16 * s, 512), v("I22"), v("EQ", 144 * s, 128 * s + 128), s == 0, s == NB - 1)
        act(S("bd"), key, AF.Copy, bias=2048.0)
        scan(v("EC"), v("RZ", 0, 128), v(bank, 384, 512), A.mult, A.max)
        tt(S("ec"), v("EC", 15, 128, 16), S("spare"), A.min)
        tt(S("of"), S("ec"), S("bd"), A.max)
        tc(v("OF", 0, 8), S("of"))

    def put(src):
        for b in range(8 - NB, -1, -NB):
            tc(ind(xwin, v("OF", b, b + NB)), v(src, 16 * b, 16 * (b + NB)))

    def step(t):
        P = 32 + t
        G = P - 2
        n8, m8 = P * 8, P * 8 + 8
        W, R, Wn, Rn = "W%d" % t, "R%d" % t, "W%d" % (t + 1), "R%d" % (t + 1)
        YR, M, LW, LY, LM = ["%s%d" % (q, t) for q in ("YR", "M", "LW", "LY", "LM")]
        n, nn, V0, V0n = S3("n%d" % t), S3("n%d" % (t + 1)), "V0%d" % t, "V0%d" % (t + 1)
        d = 1 + t % 5
        to, fr = T.cores[(rank + d) % N], T.cores[(rank - d) % N]
        ne = len(topo.engines(fr, core))
        wy = 128 + (NL if t < ST - 1 else 288)
        for buf, sem, wd in ((LW, "aw", m8 + 8), (LY, "ay", wy), (LM, "am", 40)):
            record((sem + str(t), ne), [v(buf, 0, wd)], [], {})

        def rows(nm, r0, r1):
            return v(nm, r0 * 128, r1 * 128)

        size = list(SIZES)
        size[-2] -= max(0, 32 - G)
        size[0] += max(0, G - 32)
        cut = [sum(size[:c]) for c in range(len(size) + 1)]
        vcut = [0] + [cut[c] + 1 for c in VCUT] + [P]
        banks = ("pA", "pB", "pC", "pY", "pT")
        boost[0] = EARLY
        ts(S3("L64"), n, 4.0, A.is_ge, 64.0, A.mult)
        act(S3("L"), S3("L64"), AF.Copy, scale=1.0 / 64)
        tc(v(W, m8, m8 + 8), S("L"))
        send(W, LW, m8 + 8, "aw%d" % t, to)
        boost[0] = 0.0
        tt(S3("thr"), n, S3("L64"), A.max)
        mm(v("pK", 0, NL), ID, v("QT"), True, False)
        mm(v("pD", 0, NL), v("ONES", 0, 128, 1, 0, 64), v("THX"), True, False)
        gv = 0
        for c, (r0, r1) in enumerate(zip(cut, cut[1:])):
            while vcut[gv] < r1 + 1:
                a0, a1 = vcut[gv], vcut[gv + 1]
                if gv == 0:
                    ts(rows("XV", a0, a1), ind(v("X", 0, 4096), v("VL", a0 * 8, a1 * 8)), 0.5, A.mult)
                    after("gt")
                else:
                    act(rows("XV", a0, a1), ind(v("X", 0, 4096), v("VL", a0 * 8, a1 * 8)), AF.Copy, scale=0.5)
                    after("gv")
                gv += 1
            tt(rows("T1", r0, r1), ind(v("X", 0, 4096), v("CL", r0 * 8, r1 * 8)), rows("XV", r0, r1), A.subtract)
            after("gt")
            way, bank = WAYS[c], v(banks[c % 5], 0, (r1 - r0) * 128)
            nxt, own, ab = rows("XV", r0 + 1, r1 + 1), rows("T1", r0, r1), rows("AB", r0, r1)
            if way == "Y":
                lin(bank, (IDN, nxt), (ID, own))
                act(ab, bank, AF.Abs)
            elif way == "Z":
                lin(bank, (ID, nxt))
                tt(rows("D", r0, r1), own, bank, A.subtract)
                act(ab, rows("D", r0, r1), AF.Abs)
            else:
                lin(bank, (ID, nxt))
                tt(ab, own, bank, A.max)
            for r in range(r0, r1):
                if way == "X":
                    mm(row("pK", r), rows("XV", r + 1, r + 2), v("BW", 8, 16))
                    mm(row("pK", r), rows("T1", r, r + 1), v("BW", 8, 16))
            for r in range(r0, r1):
                mm(row("pK", r), rows("AB", r, r + 1), v("BW", 0, 8) if way == "X" else v("BW", 16, 24), False, r == G - 1)
            if c == 5:
                mm(v("pK", 0, NL), ID, v(R, 0, NL))
                mm(v("pK", 1, NL), v("N22"), v("NF", 0, NL - 1))
        for r in range(SH, P):
            mm(row("pD", r), rows("XV", r, r + 1), v("BW", 8, 16))
        shared = [(r, min(r + SW, SH)) for r in range(2, SH, SW)]
        for q, (r0, r1) in enumerate(shared):
            mm(v(banks[q], 0, (r1 - r0) * 128), ID, rows("XV", r0, r1), True, False)
        tt(S("nL"), SL("n%d" % t), SL("L64"), A.min)
        act(S("bn"), S("nL"), AF.Copy, bias=0.5, scale=-1.0)
        for b in range(8):
            act(seg("DM", b), seg(R, b), AF.Sign, bias=col(S("bn"), b))
        mm(v("pD", 0, NL), v("I22"), v("NF"))
        mm(v("pD", 0, NL), v("I21"), v("DM"))

        act(v("NB", 0, 8), S("L"), AF.Copy, bias=1024.0, scale=-1024.0)
        mm(v("pT", 0, 32), v("IDF"), v("CJ"), True, False)
        mm(v("pT", 24, 32), ID, v("NB", 0, 8))
        scan(v("KS"), v("RS"), v("pK", 0, NL), A.min, A.max)
        bits(J("q"), row("KS", 0), 5, 63)
        tt(v("EXB"), ind(J("q"), v("XL")), DG, A.mult)
        mm(v("pT", 0, 32), v("EXB"), v("CV"), False, True)
        tc(v("JL"), v("pT", 0, 24))
        jk = v("JL", 0, 8)
        act(v("GA"), ind(v("XV", 128, G * 128 + 128), jk), AF.Copy)
        tc(v("GB"), ind(v("T1", 0, G * 128), jk))
        tc(v("GC"), ind(v("XV", 0, G * 128), jk))
        Y = v(YR, 0, 128)
        lin(v("pT", 128, 256), (v("IDM"), v("GB")), (ID, v("GA")), (v("IDH"), v("GC")))
        ts(v("pY", 0, 128), v("pT", 128, 256), 0.0, A.max, 31.5, A.min)
        ts(v("GA"), v("pT", 128, 256), 0.0, A.max, 31.5, A.min)
        act(Y, v("GA"), AF.Copy, scale=2.0)
        ts(J("kk"), row("KS", 0), 31, A.bitwise_and)
        ts(S("nk"), J("kk"), -1.0, A.mult)
        act(S("jw"), v("pT", 24, 32), AF.Copy)
        act(S("jb"), v("pT", 24, 32), AF.Copy, bias=-0.5, scale=-1.0)
        for b in range(8):
            act(seg("Q", b), seg(R, b), AF.Relu, bias=col(S("nk"), b))
        act(v("CM"), v("Q"), AF.Relu, bias=2.0, scale=-1.0)
        RK = v(YR, 128, 128 + NL) if t < ST - 1 else v("TDR")
        act(RK, v("Q"), AF.Relu, bias=-1.0)
        if t == ST - 1:
            to_lists(v(YR, 128, 416), RK, "pK", "F0", "F1")
        boost[0] = EARLY if t < ST - 1 else 0.0
        send(YR, LY, wy, "ay%d" % t, to)
        boost[0] = 0.0
        lin(v("pR", 0, NL), (ID, v("P32")), (ID, RK))
        act(v("PL"), v("pR", 0, NL), AF.Copy)

        boost[0] = UB
        mm(v("pK", 0, 8), Y, v("BW", 24, 32), True, True)
        act(S("ul"), v("pK", 0, 8), AF.Copy)
        for b in range(8):
            act(v("EXF", 16 * b, 16 * b + 16), v("DG", 0, 16), AF.Copy, scale=col(S("ul"), b))
        mm(v("pK", 8, 16), v("EXF"), S("cvf"), True, True)
        boost[0] = 0.0
        mm(v("pD", 0, NL), v("GA"), v("BR"))
        mm(v("pD", 0, NL), v("I22"), v("CM"))
        for c, r in enumerate(range(SH, P, 2)):
            for q in range(r, min(r + 2, P)):
                tt(rows("AB", q, q + 1), rows("XV", q, q + 1), v("pY", 0, 128), A.max)
            if c % 3 == 0 and c // 3 < len(shared):
                r0, r1 = shared[c // 3]
                for q in range(r1 - r0):
                    mm(v(banks[c // 3], 128 * q, 128 * q + 128), IDN, v("GA"), False, q == r1 - r0 - 1)
                act(rows("AB", r0, r1), v(banks[c // 3], 0, (r1 - r0) * 128), AF.Abs)
            if c % 3 == 2 and c // 3 < len(shared):
                for q in range(*shared[c // 3]):
                    mm(row("pD", q), rows("AB", q, q + 1), v("BW", 16, 24))
            for q in range(r, min(r + 2, P)):
                mm(row("pD", q), rows("AB", q, q + 1), v("BW", 0, 8), False, q == P - 1)
        for b in range(8):
            act(v("SP", b, m8, 8), v("P8", b, m8, 8), AF.Sign, bias=col(S("jb"), b))
        scan(v("FS"), v("pD", 0, NL), v("PL"), A.min, A.max)
        tt(v("EXH"), ind(v("FS"), v("XF")), DG, A.mult)
        mm(v("pT", 0, 16), v("EXH"), v("CVH"), True, True)
        behind["t"] = len(ops) - 1
        tc(J("vm", 0, 16), v("pT", 0, 16))
        ts(v(M, 0, 16), J("vm", 0, 16), 31, A.bitwise_and)
        ts(v(M, 16, 24), row("FS", 0), 31, A.bitwise_and)
        tt(v("GV"), ind(v(W, 0, n8), v("JL", 8, 24)), v("DG2"), A.mult)
        boost[0] = VB
        scan(v("SC"), v("RZ"), v("GV"), A.mult, A.add)
        boost[0] = 0.0
        bits(J("vk", 0, 16), v("SC", 15, 256, 16), 12, 4095)
        vk, vk1, wk = J("vk"), J("vk", 8, 16), v("SC", 15, 128, 16)
        ts(v(M, 24, 32), vk1, -2048.0, A.add)
        ts(v(M, 32, 40), vk1, dump, A.subtract)
        tc(S("vk"), vk)
        send(M, LM, 40, "am%d" % t, to)
        tc(S3("sz"), v(M, 0, 24))
        ts(S("no"), v("pT", 0, 8), 2048.0, A.is_ge)
        ts(S3("cl"), v(M, 0, 24), 1.0, A.min)
        tt(S3("gr"), S3("L"), S3("cl"), A.subtract)

        tc(J("u"), v("pK", 8, 16))
        ts(J("u2"), J("u"), 4095, A.bitwise_and)
        tt(J("uu"), J("u2"), J("u2"), A.mult)
        act(S("v37"), S("vk"), AF.Copy, scale=37.0)
        ts(J("us"), J("uu"), 5, A.arith_shift_right)
        tt(J("h0"), J("us"), S("v37"), A.add)
        ts(J("h"), J("h0"), 4095, A.bitwise_and)
        ts(S("hd"), J("h"), dump, A.subtract)
        tt(S("hl"), S("hd"), S("L"), A.mult)
        tt(S("hg"), S("hl"), S("no"), A.mult)
        ts(S("kg"), S("hg"), dumpk, A.add)
        winners(S("kg"), "pD")
        put(YR)

        act(S("z0"), S("vk"), AF.Copy, bias=float(-BIG), scale=4096.0)
        tt(S("z"), S("z0"), vk1, A.add)
        act(S("wn0"), S("hd"), AF.Identity, bias=dk4, scale=4096.0)
        tt(S("wn1"), vk, wk, A.subtract)
        tt(S("wn"), S("wn0"), S("wn1"), A.add)
        bits(J("pm"), J("vm"), 2, 504)
        tt(S("pz"), J("pm"), S("jw"), A.max)
        for b in range(8):
            ts(v("ZM", b, m8, 8), v("P8", b, m8, 8), col(S("pz"), b), A.is_equal, col(S("z"), b), A.mult)
        act(v("ZS", 0, m8), v("ZM", 0, m8), AF.Sign)
        for b in range(8):
            act(v("G1", b, m8, 8), v("SP", b, m8, 8), AF.Relu, scale=col(S("no"), b))
        lin(v("pB", 0, m8), (ID, v("G1", 0, m8)))
        lin(v("pC", 8, m8), (ID, v("G1", 8, m8)), (IDN, v("G1", 0, n8)))
        lin(v("pA", 0, m8), (ID, v("ONES", 0, m8)), (IDN, v("G1", 0, m8)), (ID, v("ZS", 0, m8)))
        for b in range(8):
            act(v("pC", 8 + b, m8, 8), v("pC", 8 + b, m8, 8), AF.Copy, scale=col(S("wn"), b))
        tt(v("pB", 8, m8), v(W, 0, n8), v("pB", 8, m8), A.mult)
        tt(v("ZM", 8, m8), v("ZM", 8, m8), v("pC", 8, m8), A.add)
        tt(v("ZM", 8, m8), v("ZM", 8, m8), v("pB", 8, m8), A.add)
        tt(v("pA", 0, m8), v(W, 0, m8), v("pA", 0, m8), A.mult)
        tt(v("WA", 0, m8), v("ZM", 0, m8), v("pA", 0, m8), A.add)
        tt(v("DW", 0, m8), v(LW, 0, m8), v("pA", 0, m8), A.subtract)
        boost[0] = RB if t == ST - 1 else 0.0
        act(S("nsz"), SL("sz"), AF.Copy, scale=-1.0)
        act(S("g2"), SL("gr"), AF.Copy, bias=-2.0)
        lin(v("pY", 0, NL), (ID, v("Q")), (IDN, RK), (ID, v("NF")))
        for b in range(8):
            act(seg("A1", b), seg("Q", b), AF.Relu, bias=col(S("nsz"), b))
        for b in range(8):
            act(seg("B1", b), seg("pY", b), AF.Relu, bias=col(S("g2"), b))
        for l, r in ((ID, v(R, 0, NL)), (IDN, v("Q")), (ID, v("A1")), (ID, v("B1"))):
            mm(v("pR", 0, NL), l, r, r[0] == R, r[0] == "B1" and t == ST - 1)
        boost[0] = 0.0
        tt(S3("ng"), n, S3("gr"), A.add)
        ts(S3("ng"), S3("ng"), 32.0, A.min)
        tt(S3("n2"), S3("ng"), S3("sz"), A.subtract)
        if t < ST - 1:
            act(S("clc"), SL("cl"), AF.Copy, acc_out=S("cs", 0, 1))
            mm(v("pK", 16, 17, 1, 0, 64), v("ONF", 0, 64), S("cs", 0, 1), True, True)
            cj = J("c", 0, 1, 0, 64)
            tc(cj, v("pK", 16, 17, 1, 0, 64))
            ts(cj, cj, 31, A.bitwise_and)
            ts(S("th", 2, 3, 1, 0, 64), cj, S("th", 1, 2, 1, 0, 64), A.mult, S("th", 0, 1, 1, 0, 64), A.add)
            boost[0] = EARLY
            act(v("THX"), v("SEG"), AF.Copy, scale=S("th", 2, 3, 1, 0, 64))
            boost[0] = 0.0

        if t < ST - 1:
            lin(v("pD", 0, NL), (ID, v(LY, 128, 128 + NL)), (IDN, v(R, 0, NL)))
        else:
            act(v(Rn, 0, NL), v("pR", 0, NL), AF.Copy)
            to_lists(v("RT4"), v(Rn, 0, NL), "pR", "SK", "SO")
        act(v("pK", 320, 448), v(LY, 0, 128), AF.Copy, bias=-0.25, scale=0.5)
        tt(S("has"), S("n%d" % t), v(LW, m8, m8 + 8), A.min)
        tt(S("hv"), S("has"), S(V0, 8, 16), A.mult)
        act(S(V0), S("hv"), AF.Identity, bias=dumpk)
        tt(S3("tk"), v(LM, 0, 24), S3("thr"), A.is_gt)
        tt(S2("dl"), v(LM, 24, 40), S2(V0), A.subtract)
        tt(S2("kd"), S2("tk"), S2("dl"), A.mult)
        tt(S2(V0n), S2("kd"), S2(V0), A.add)
        ts(v("OG"), S(V0n), 2048.0, A.add)
        winners(S(V0n), "pC")
        act(v("GX"), ind(xwin, v("OG")), AF.Copy, scale=0.5)
        for b in range(8):
            act(v("pK", b, m8, 8), v("DW", b, m8, 8), AF.Copy, scale=col(S("tk"), b))
        tt(v("BO"), v("GX"), v("pK", 320, 448), A.add)
        tt(v(Wn, 0, m8), v("WA", 0, m8), v("pK", 0, m8), A.add)
        put("BO")
        tt(S3("rc"), v(LM, 0, 24), S3("tk"), A.mult)
        tt(nn, S3("rc"), S3("n2"), A.max)
        if t < ST - 1:
            for b in range(8):
                act(seg("TDR", b), seg("pD", b), AF.Copy, scale=col(SL("tk"), b))
            mm(v("pR", 0, NL), ID, v("TDR"), False, True)
            act(v(Rn, 0, NL), v("pR", 0, NL), AF.Copy)
            masks(t + 1)
            lists(t + 1, Wn)

    lists(0, "W0")
    late_constants()
    tc(v("NB", 0, 128, 1, 0, 8), v("NR"))
    mm(v("pT", 16, 24), v("NB", 0, 128, 1, 0, 8), v("ID", 0, 8, 1, 0, 8), True, True)
    tc(SL("n0"), v("pT", 16, 24))
    tt(v("EXH"), ind(SL("n0"), v("XL")), DG, A.mult)
    mm(v("pT", 0, 16), v("EXH"), v("CVH"), True, True)
    tc(S2("n0"), v("pT", 0, 16))
    masks(0)
    for t in range(ST):
        if t == ST - 1:
            last_constants()
        step(t)

    lin(v("pD", 0, 288), (ID, v("LY3", 128, 416)), (IDN, v("RT4")))
    for b in range(8):
        act(v("SK", b, 288, 8), v("pD", b, 288, 8), AF.Copy, scale=col(S("tk"), b))
    lin(v("pY", 0, 288), (ID, v("PP")), (IDN, v("RT4")), (IDN, v("SK")))
    lin(v("pB", 0, 280), (ID, v("RT4", 8, 288)), (IDN, v("RT4", 0, 280)), (ID, v("SK", 8, 288)), (IDN, v("SK", 0, 280)))
    lin(v("pB", 280, 288), (ID, v("ONES", 0, 8)))
    tt(v("UF", 0, 288), v("W4", 0, 288), v("pB", 0, 288), A.mult)
    for i in range(6):
        act(v("F%d" % i, 8 << max(i - 1, 0), 288), v("pY", 8 << max(i - 1, 0), 288), AF.Copy, bias=159.5 + 1.0 / 64, scale=0.5 ** i)
    for i in range(6):
        lo = 8 << i
        w = 288 - lo
        bit = v("pC" if i % 2 else "pR", lo, 288)
        if i < 5:
            lin(bit, (v("I128"), v("ONES", lo, 288)), (ID, v("F%d" % i, lo, 288)), (v("N2"), v("F%d" % (i + 1), lo, 288)))
        else:
            lin(bit, (v("N128"), v("ONES", lo, 288)), (ID, v("F%d" % i, lo, 288)))
        for h in range(CS if i < 5 else 1):
            st = CS if i < 5 else 1
            up = v("pA", lo + h, 288, st)
            tt(up, v("UF", lo + h, 288, st), v(bit[0], lo + h, 288, st), A.mult)
            tt(v("UF", lo + h, 288, st), v("UF", lo + h, 288, st), up, A.subtract)
            tt(v("UF", h, w, st), v("UF", h, w, st), up, A.add)
    act(v("UF", 256, 384), v("UF", 0, 128), AF.Copy)
    act(v("NB", 0, 8), SL("n4"), AF.Copy)
    mm(v("pD", 0, 128, 1, 0, 8), v("NB", 0, 8), ID, True, True)
    act(v("NO"), v("pD", 0, 128, 1, 0, 8), AF.Copy)
    act(v("EXB"), ind(SL("n4"), v("XL")), AF.Copy)
    mm(v("pD", 128, 256), v("EXB"), ID, True, True)
    for s in range(2):
        act(S("n5", s, s + 1), paf, AF.Copy, bias=-0.5 - 16 * s, scale=-1.0)
        act(v("NM", s, 256, 2), v("pD", 128, 256), AF.Sign, bias=S("n5", s, s + 1))
    act(v("pK", 0, 256), v("NM"), AF.Relu)
    so = [dma("s", T.yx[:, 0:2048], ap(v("X", 0, 2048)), [], [v("X", 0, 2048)]),
          dma("a", T.yx[:, 2048:4096], ap(v("X", 2048, 4096)), [], [v("X", 2048, 4096)]),
          dma("s", T.yn[:], ap(v("NO")), [], [v("NO")])]
    for w in range(2):
        for b in range(8):
            tp(v("TAB", w * 256 + b * 32, w * 256 + b * 32 + 32), v("UF", 128 * w + b, 128 * w + 256, 8))
    tc(v("OI"), ind(v("TAB"), v("LO")))
    bits(v("VI", 0, 256), v("OI"), 12, 4095)
    tt(v("OV"), v("VI", 0, 256), v("pK", 0, 256), A.mult)
    so.append(dma("s", T.yv[:], ap(v("OV")), [], [v("OV")]))
    ts(v("CI", 0, 256), v("OI"), 4095, A.bitwise_and)
    tt(v("OC"), v("CI", 0, 256), v("pK", 0, 256), A.mult)
    so.append(dma("a", T.yc[:], ap(v("OC")), [], [v("OC")]))
    flush()
    for s in so:
        g.sync.wait_ge(T.sem[s], 16)
    for s in ("qv", "qa", "qt", "qp"):
        g.sync.wait_ge(T.sem[s], cnt[s])
    g.wait_ge(T.sem.ls, cnt["ls"])
